import numpy as np
import ml_dtypes


def mxq(x, axis, fmt="e4m3"):
    dtype, down = {"e4m3": (ml_dtypes.float8_e4m3fn, 7), "e5m2": (ml_dtypes.float8_e5m2, 14)}[fmt]
    v = np.moveaxis(np.asarray(x, np.float32).astype(ml_dtypes.bfloat16).astype(np.float64), axis, -1)
    blocks = v.reshape(v.shape[:-1] + (-1, 32))
    amax = np.abs(blocks).max(-1, keepdims=True)
    byte = np.maximum(np.where(amax > 0, np.frexp(amax)[1] - 1 + 127, 0) - down, 1)
    scale = np.exp2(byte - 127.0)
    codes = (blocks / scale).astype(np.float32).astype(dtype).astype(np.float64)
    return np.moveaxis((codes * scale).reshape(v.shape), -1, axis)


WIDE = False


def mx_kscale(k):
    if not WIDE:
        return np.ones(k)
    levels = np.array([30, -30])
    if k % 512:
        return np.exp2(np.random.permutation(np.resize(levels, k // 32))).repeat(32)
    a = np.empty((k // 512, 16))
    for p in range(k // 512):
        a[p, :8] = np.random.permutation(np.resize(levels, 8))
        for g in range(8):
            far = levels[np.abs(levels - a[p, g]) >= 10]
            a[p, g + 8] = far[np.random.randint(len(far))]
    return np.exp2(a.ravel()).repeat(32)


def f64(x):
    return np.asarray(x).astype(np.float64)


def striped(idx):
    return np.tile(idx.reshape(-1, 16).T, (8, 1)).astype(np.uint16)


def unstriped(offs):
    return offs[:16].T.reshape(-1).astype(np.int64)


def bf(x):
    return np.asarray(x, np.float32).astype(ml_dtypes.bfloat16)


E2M1 = np.array([0.0, 0.5, 1.0, 1.5, 2.0, 3.0, 4.0, 6.0, -0.0, -0.5, -1.0, -1.5, -2.0, -3.0, -4.0, -6.0])


def pack_weight(w, fmt):
    k, n = w.shape
    w = f64(bf(w)).reshape(k // 32, 32, n)
    amax = np.abs(w).max(1)
    if fmt in ("e4m3", "e5m2"):
        byte = np.frexp(amax)[1] - 1 + 127 - (7 if fmt == "e4m3" else 14)
    else:
        mant, ex = np.frexp(amax / 6.0)
        byte = np.where(mant > 0.5, ex, ex - 1) + 127
    byte = np.clip(np.where(amax > 0, byte, 1), 1, 254)
    scaled = (w * np.exp2(127.0 - byte)[:, None, :]).reshape(k, n).astype(np.float32)
    by_word = np.ascontiguousarray(scaled.reshape(k // 512, 128, 4, n).transpose(0, 1, 3, 2))
    if fmt in ("e4m3", "e5m2"):
        words = by_word.astype(ml_dtypes.float8_e4m3fn if fmt == "e4m3" else ml_dtypes.float8_e5m2).view(np.uint8)
    else:
        c = by_word.astype(ml_dtypes.float4_e2m1fn).view(np.uint8) & 0xF
        words = c[..., 0::2] | (c[..., 1::2] << 4)
    return np.ascontiguousarray(words), np.ascontiguousarray(byte.astype(np.uint8).reshape(k // 512, 16, n))


def unpack_weight(words, scales, fmt):
    g, p, n, _ = words.shape
    if fmt in ("e4m3", "e5m2"):
        vals = np.ascontiguousarray(words).view(ml_dtypes.float8_e4m3fn if fmt == "e4m3" else ml_dtypes.float8_e5m2).astype(np.float64)
    else:
        nib = np.empty((g, p, n, 4), np.uint8)
        nib[..., 0::2] = words & 0xF
        nib[..., 1::2] = words >> 4
        vals = E2M1[nib]
    vals = vals * np.repeat(np.exp2(scales.astype(np.float64) - 127.0), 8, axis=1)[..., None]
    return vals.transpose(0, 1, 3, 2).reshape(g * 512, n)


K, T, S, H, N, T2 = 1024, 2048, 1024, 1536, 512, 2048

def setup_inputs():
    n = np.random.standard_normal
    s = mx_kscale(K)[:, None]
    u = mx_kscale(H)[:, None]
    tab_words, tab_scales = pack_weight(n((K, T)) * np.exp(1.0 * n((1, T))) * s, "e5m2")
    w1_words, w1_scales = pack_weight(n((K, H)) / np.sqrt(K) / s * u.T, "e4m3")
    return {
        "tab_words": tab_words,
        "tab_scales": tab_scales,
        "offs": striped(np.random.permutation(T)[:S]),
        "offs2": striped(np.random.permutation(T2)[:S]),
        "sT": np.random.uniform(-2.8, 2.8, (H, T)).astype(np.float32),
        "w1_words": w1_words,
        "w1_scales": w1_scales,
        "amp": np.random.uniform(0.3, 0.8, H).astype(np.float32),
        "w2": (n((H, N)) / np.sqrt(H) / u).astype(np.float32),
        "wgo": np.exp(0.3 * n((128, S))).astype(np.float32),
    }

def reference(tab_words, tab_scales, offs, offs2, sT, w1_words, w1_scales, amp, w2, wgo):
    v = unpack_weight(tab_words, tab_scales, "e5m2")[:, unstriped(offs)]
    ph = f64(sT)[:, unstriped(offs)]
    w1 = unpack_weight(w1_words, w1_scales, "e4m3")
    h = w1.T @ v
    d = h * np.cos(ph)
    z = d * (1.0 - f64(amp)[:, None] * np.sin(ph))
    zq = mxq(z, 0, "e4m3")
    w2q = mxq(f64(w2), 0, "e4m3")
    y = w2q.T @ zq
    out = np.zeros((N, T2))
    out[:, unstriped(offs2)] = np.tile(f64(wgo), (N // 128, 1)) * y
    return out

@@ -1,0 +1,286 @@
+import math
+from contextlib import ExitStack
+
+import concourse.mybir as mybir
+
+K, T, S, H, N, T2 = 1024, 2048, 1024, 1536, 512, 2048
+FLOPS = 2 * K * H * S + 2 * H * N * S
+
+F32 = mybir.dt.float32
+BF16 = mybir.dt.bfloat16
+I32 = mybir.dt.int32
+U32 = mybir.dt.uint32
+U16 = mybir.dt.uint16
+U8 = mybir.dt.uint8
+E4 = mybir.dt.float8_e4m3fn_x4
+E5 = mybir.dt.float8_e5m2_x4
+ACT = mybir.ActivationFunctionType
+ALU = mybir.AluOpType
+
+P = 128
+PACK = 4
+KP = P * PACK
+NA = K // KP
+NB = H // KP
+JW = 512
+NH = S // JW
+NT = N // P
+RING = 5
+
+
+def tile_list_lattice_flow_adjoint_kernel(
+    tc, tab_words, tab_scales, offs, offs2, sT, w1_words, w1_scales, amp, w2, wgo, out
+):
+    nc = tc.nc
+    with ExitStack() as ctx:
+        keep = ctx.enter_context(tc.tile_pool(name="keep", bufs=1))
+        ring = ctx.enter_context(tc.tile_pool(name="ring", bufs=RING))
+        two = ctx.enter_context(tc.tile_pool(name="two", bufs=2))
+        three = ctx.enter_context(tc.tile_pool(name="three", bufs=3))
+        four = ctx.enter_context(tc.tile_pool(name="four", bufs=4))
+        hps = ctx.enter_context(tc.psum_pool(name="hps", bufs=6))
+        yps = ctx.enter_context(tc.psum_pool(name="yps", bufs=2))
+
+        idx = keep.tile([P, S // 16], U16, name="idx")
+        nc.sync.dma_start(idx[:], offs)
+        idx2 = keep.tile([P, S // 16], U16, name="idx2")
+
+        sT_rows = sT.rearrange("(b p t) c -> b t p c", p=P, t=PACK)
+        w2_rows = w2.rearrange("(b p t) n -> b p (t n)", p=P, t=PACK)
+        stream = (
+            [("s", b, t) for b in range(2) for t in range(PACK)]
+            + [("tab", 0, 0), ("tab", 1, 0), ("w1", 0, 0), ("w1", 1, 0)]
+            + [("s", 2, t) for t in range(PACK)]
+            + [("w2", b, 0) for b in range(NB)]
+            + [("wgo", 0, 0)]
+        )
+        loaded = []
+
+        def load_next():
+            if len(loaded) == len(stream):
+                return
+            kind, u, v = stream[len(loaded)]
+            if kind == "s":
+                tile = ring.tile([P, T], F32, name="in", align_bytes=64)
+                nc.sync.dma_start(tile[:], sT_rows[u, v])
+            elif kind == "tab":
+                tile = ring.tile([P, T], I32, name="in", align_bytes=64)
+                nc.sync.dma_start(tile[:], tab_words[u].rearrange("p c i -> p (c i)").bitcast(I32))
+            elif kind == "w1":
+                tile = ring.tile([P, H], I32, name="in", align_bytes=64)
+                nc.sync.dma_start(tile[:], w1_words[u].rearrange("p c i -> p (c i)").bitcast(I32))
+            elif kind == "wgo":
+                tile = ring.tile([P, S], F32, name="in", align_bytes=64)
+                nc.sync.dma_start(tile[:], wgo)
+            else:
+                tile = ring.tile([P, PACK * N], F32, name="in", align_bytes=64)
+                nc.sync.dma_start(tile[:], w2_rows[u])
+            loaded.append(tile)
+
+        def take(kind, u, v):
+            return loaded[stream.index((kind, u, v))]
+
+        for unused in range(RING):
+            load_next()
+
+        amp_sb = keep.tile([P, NB, PACK], F32, name="amp_sb")
+        nc.gpsimd.dma_start(amp_sb[:], amp.rearrange("(b p t) -> p b t", p=P, t=PACK))
+        nc.sync.dma_start(idx2[:], offs2)
+        tabs = keep.tile([P, T], U8, name="tabs", align_bytes=64)
+        w1s = keep.tile([P, H], U8, name="w1s", align_bytes=64)
+        tabs1 = keep.tile([P, S], U8, name="tabs1", align_bytes=64)
+        w1s1 = keep.tile([P, H], U8, name="w1s1", align_bytes=64)
+        nc.gpsimd.memset(tabs[:].bitcast(I32), 0)
+        nc.gpsimd.memset(w1s[:].bitcast(I32), 0)
+        for q in range(4):
+            nc.gpsimd.dma_start(tabs[32 * q : 32 * q + 8, :].bitcast(I32), tab_scales[:, 4 * q : 4 * q + 4, :].bitcast(I32))
+        for q in range(4):
+            nc.gpsimd.dma_start(w1s[32 * q : 32 * q + 8, :].bitcast(I32), w1_scales[:, 4 * q : 4 * q + 4, :].bitcast(I32))
+        nc.gpsimd.memset(tabs1[:].bitcast(I32), 0)
+        nc.gpsimd.memset(w1s1[:].bitcast(I32), 0)
+
+        windows = [keep.tile([P, T2], F32, name=f"window{n}") for n in range(NT)]
+        for n in range(NT):
+            (nc.vector if n < 2 else nc.gpsimd).memset(windows[n][:], 0.0)
+
+        phases = {}
+
+        def gather_phases(b, t):
+            if t == 0:
+                phases[b] = three.tile([P, PACK, S], F32, name="phases")
+            nc.vector.tensor_copy(phases[b][:, t, :], take("s", b, t)[:].indirect(idx[:]))
+            load_next()
+
+        v_codes = [keep.tile([P, S], U32, name=f"v_codes{a}", align_bytes=64) for a in range(NA)]
+        tabs0 = keep.tile([P, S], U8, name="tabs0", align_bytes=64)
+        v_scales = [tabs0, tabs1]
+        w1_codes = [keep.tile([P, H], U32, name=f"w1_codes{a}", align_bytes=64) for a in range(NA)]
+        w1s0 = keep.tile([P, H], U8, name="w1s0", align_bytes=64)
+        w1_planes = [w1s0, w1s1]
+
+        def gather_table():
+            nc.vector.tensor_copy(tabs0[:], tabs[:].indirect(idx[:]))
+            nc.gpsimd.dma_start(tabs1[0:100, :].bitcast(I32), tabs0[4:104, :].bitcast(I32))
+            nc.vector.tensor_copy(
+                w1s0[:].rearrange("p (b t m) -> p b t m", t=PACK, m=P), w1s[:].rearrange("p (b m t) -> p b t m", t=PACK, m=P)
+            )
+            nc.gpsimd.dma_start(w1s1[0:100, :].bitcast(I32), w1s0[4:104, :].bitcast(I32))
+            for a in range(NA):
+                nc.vector.tensor_copy(v_codes[a][:], take("tab", a, 0)[:].bitcast(U32).indirect(idx[:]))
+                load_next()
+            for a in range(NA):
+                for b in range(NB):
+                    cols = slice(b * KP, (b + 1) * KP)
+                    nc.vector.tensor_copy(
+                        w1_codes[a][:, cols].rearrange("p (t m i) -> p m t i", t=PACK, i=4),
+                        take("w1", a, 0)[:, cols].bitcast(U32).rearrange("p (m i t) -> p m t i", t=PACK, i=4),
+                    )
+                load_next()
+
+        cosf, sinf, hbank, zb, z_codes, z_scales = {}, {}, {}, {}, {}, {}
+
+        def trig(b, h, groups):
+            js = slice(h * JW, (h + 1) * JW)
+            cosf[b, h] = four.tile([P, PACK, JW], F32, name="cosf")
+            sinf[b, h] = phases[b][:, :, js]
+            for ts in groups:
+                x = phases[b][:, ts, js]
+                nc.scalar.activation(cosf[b, h][:, ts, :], x, ACT.Sin, scale=0.5)
+                nc.scalar.activation(cosf[b, h][:, ts, :], cosf[b, h][:, ts, :], ACT.Square, scale=math.sqrt(2.0))
+                nc.scalar.activation(sinf[b, h][:, ts, :], x, ACT.Sin)
+                for t in range(ts.start, ts.stop):
+                    nc.scalar.activation(
+                        sinf[b, h][:, t, :], sinf[b, h][:, t, :], ACT.Identity, scale=amp_sb[:, b, t : t + 1], bias=-1.0
+                    )
+
+        def first_product(b, h):
+            js = slice(h * JW, (h + 1) * JW)
+            for t in range(PACK):
+                cols = slice(b * KP + t * P, b * KP + (t + 1) * P)
+                hbank[b, h, t] = hps.tile([P, JW], F32, name="hbank")
+                for a in range(NA):
+                    nc.tensor.matmul_mx(
+                        hbank[b, h, t][:],
+                        lhsT=w1_codes[a][:, cols].bitcast(E4),
+                        lhsT_scale=w1_planes[a][:, cols],
+                        rhs=v_codes[a][:, js].bitcast(E5),
+                        rhs_scale=v_scales[a][:, js],
+                        start=(a == 0),
+                        stop=(a == NA - 1),
+                    )
+
+        def times_cos(b, h):
+            for t in range(PACK):
+                c = cosf[b, h][:, t, :]
+                nc.vector.scalar_tensor_tensor(c, c, 1.0, hbank[b, h, t][:], ALU.subtract, ALU.mult)
+
+        def times_sin(b, h, engine):
+            zb[b, h] = two.tile([P, JW, PACK], BF16, name="zb", align_bytes=64)
+            engine.tensor_tensor(
+                zb[b, h][:].rearrange("p (c i) t -> p c t i", i=4),
+                cosf[b, h][:].rearrange("p t (c i) -> p c t i", i=4),
+                sinf[b, h].rearrange("p t (c i) -> p c t i", i=4),
+                ALU.mult,
+            )
+
+        def quantise_z(b, h):
+            z_codes[b, h] = keep.tile([P, JW], U32, name=f"z_codes{b}{h}", align_bytes=64)
+            z_scales[b, h] = keep.tile([P, JW], U8, name=f"z_scales{b}{h}", align_bytes=64)
+            nc.vector.quantize_mx(z_codes[b, h][:].bitcast(E4), z_scales[b, h][:], zb[b, h][:].rearrange("p c t -> p (c t)"))
+
+        w2b, w2_codes, w2_scales = {}, {}, {}
+
+        def round_w2(b):
+            w2b[b] = two.tile([P, N, PACK], BF16, name="w2b", align_bytes=64)
+            nc.scalar.copy(
+                w2b[b][:].rearrange("p (c i) t -> p c t i", i=4),
+                take("w2", b, 0)[:].rearrange("p (t c i) -> p c t i", t=PACK, i=4),
+            )
+            load_next()
+
+        def quantise_w2(b):
+            w2_codes[b] = keep.tile([P, N], U32, name=f"w2_codes{b}", align_bytes=64)
+            w2_scales[b] = keep.tile([P, N], U8, name=f"w2_scales{b}", align_bytes=64)
+            nc.vector.quantize_mx(w2_codes[b][:].bitcast(E4), w2_scales[b][:], w2b[b][:].rearrange("p c t -> p (c t)"))
+
+        forces = {}
+
+        def second_product(h, n):
+            cols = slice(n * P, (n + 1) * P)
+            ybank = yps.tile([P, JW], F32, name="ybank")
+            for b in range(NB):
+                nc.tensor.matmul_mx(
+                    ybank[:],
+                    lhsT=w2_codes[b][:, cols].bitcast(E4),
+                    lhsT_scale=w2_scales[b][:, cols],
+                    rhs=z_codes[b, h][:].bitcast(E4),
+                    rhs_scale=z_scales[b, h][:],
+                    start=(b == 0),
+                    stop=(b == NB - 1),
+                )
+            forces[h, n] = four.tile([P, JW], F32, name="forces")
+            nc.scalar.copy(forces[h, n][:], ybank[:])
+
+        def scatter(h, n):
+            places = idx2[:, h * (JW // 16) : (h + 1) * (JW // 16)]
+            nc.vector.tensor_tensor(windows[n][:].indirect(places), forces[h, n][:], take("wgo", 0, 0)[:, h * JW : (h + 1) * JW], ALU.mult)
+
+        whole = [slice(0, PACK)]
+        single = [slice(t, t + 1) for t in range(PACK)]
+        V = nc.vector
+        E00, E01, E10, E20, E11, E21 = V, V, V, V, V, V
+
+        for t in range(PACK):
+            gather_phases(0, t)
+        trig(0, 0, single)
+        trig(0, 1, whole)
+        for t in range(PACK):
+            gather_phases(1, t)
+        trig(1, 0, whole)
+        trig(1, 1, whole)
+        gather_table()
+        first_product(0, 0)
+        gather_phases(2, 0)
+        times_cos(0, 0)
+        first_product(0, 1)
+        gather_phases(2, 1)
+        times_sin(0, 0, E00)
+        times_cos(0, 1)
+        quantise_z(0, 0)
+        first_product(1, 0)
+        gather_phases(2, 2)
+        times_sin(0, 1, E01)
+        gather_phases(2, 3)
+        quantise_z(0, 1)
+        round_w2(0)
+        round_w2(1)
+        trig(2, 0, whole)
+        times_cos(1, 0)
+        first_product(1, 1)
+        quantise_w2(0)
+        round_w2(2)
+        times_sin(1, 0, E10)
+        quantise_w2(1)
+        times_cos(1, 1)
+        quantise_z(1, 0)
+        first_product(2, 0)
+        times_sin(1, 1, E11)
+        quantise_w2(2)
+        trig(2, 1, whole)
+        times_cos(2, 0)
+        quantise_z(1, 1)
+        first_product(2, 1)
+        times_sin(2, 0, E20)
+        times_cos(2, 1)
+        quantise_z(2, 0)
+        for n in range(NT):
+            second_product(0, n)
+        times_sin(2, 1, E21)
+        scatter(0, 0)
+        quantise_z(2, 1)
+        for n in range(1, NT):
+            scatter(0, n)
+        for n in range(NT):
+            second_product(1, n)
+            scatter(1, n)
+            nc.sync.dma_start(out[n * P : (n + 1) * P, :], windows[n][:])

@@ -25,7 +25,8 @@ NB = H // KP
 JW = 512
 NH = S // JW
 NT = N // P
-RING = 5
+RING = 7
+SMALL = 6
 
 
 def tile_list_lattice_flow_adjoint_kernel(
@@ -35,9 +36,9 @@ def tile_list_lattice_flow_adjoint_kernel(
     with ExitStack() as ctx:
         keep = ctx.enter_context(tc.tile_pool(name="keep", bufs=1))
         ring = ctx.enter_context(tc.tile_pool(name="ring", bufs=RING))
-        two = ctx.enter_context(tc.tile_pool(name="two", bufs=2))
         three = ctx.enter_context(tc.tile_pool(name="three", bufs=3))
         four = ctx.enter_context(tc.tile_pool(name="four", bufs=4))
+        six = ctx.enter_context(tc.tile_pool(name="six", bufs=SMALL))
         hps = ctx.enter_context(tc.psum_pool(name="hps", bufs=6))
         yps = ctx.enter_context(tc.psum_pool(name="yps", bufs=2))
 
@@ -48,9 +49,9 @@ def tile_list_lattice_flow_adjoint_kernel(
         sT_rows = sT.rearrange("(b p t) c -> b t p c", p=P, t=PACK)
         w2_rows = w2.rearrange("(b p t) n -> b p (t n)", p=P, t=PACK)
         stream = (
-            [("s", b, t) for b in range(2) for t in range(PACK)]
-            + [("tab", 0, 0), ("tab", 1, 0), ("w1", 0, 0), ("w1", 1, 0)]
-            + [("s", 2, t) for t in range(PACK)]
+            [("s", 0, 0), ("w1", 0, 0), ("w1", 1, 0)]
+            + [("s", b, t) for b in range(NB) for t in range(PACK)][1:]
+            + [("tab", 0, 0), ("tab", 1, 0)]
             + [("w2", b, 0) for b in range(NB)]
             + [("wgo", 0, 0)]
         )
@@ -80,28 +81,26 @@ def tile_list_lattice_flow_adjoint_kernel(
         def take(kind, u, v):
             return loaded[stream.index((kind, u, v))]
 
-        for unused in range(RING):
-            load_next()
-
-        amp_sb = keep.tile([P, NB, PACK], F32, name="amp_sb")
-        nc.gpsimd.dma_start(amp_sb[:], amp.rearrange("(b p t) -> p b t", p=P, t=PACK))
-        nc.sync.dma_start(idx2[:], offs2)
         tabs = keep.tile([P, T], U8, name="tabs", align_bytes=64)
         w1s = keep.tile([P, H], U8, name="w1s", align_bytes=64)
         tabs1 = keep.tile([P, S], U8, name="tabs1", align_bytes=64)
         w1s1 = keep.tile([P, H], U8, name="w1s1", align_bytes=64)
-        nc.gpsimd.memset(tabs[:].bitcast(I32), 0)
         nc.gpsimd.memset(w1s[:].bitcast(I32), 0)
+        nc.gpsimd.memset(tabs[:].bitcast(I32), 0)
+        load_next()
+        amp_sb = keep.tile([P, NB, PACK], F32, name="amp_sb")
+        nc.sync.dma_start(amp_sb[:], amp.rearrange("(b p t) -> p b t", p=P, t=PACK))
         for q in range(4):
-            nc.gpsimd.dma_start(tabs[32 * q : 32 * q + 8, :].bitcast(I32), tab_scales[:, 4 * q : 4 * q + 4, :].bitcast(I32))
+            nc.sync.dma_start(w1s[32 * q : 32 * q + 8, :].bitcast(I32), w1_scales[:, 4 * q : 4 * q + 4, :].bitcast(I32))
+        for unused in range(RING - 1):
+            load_next()
+        nc.sync.dma_start(idx2[:], offs2)
         for q in range(4):
-            nc.gpsimd.dma_start(w1s[32 * q : 32 * q + 8, :].bitcast(I32), w1_scales[:, 4 * q : 4 * q + 4, :].bitcast(I32))
-        nc.gpsimd.memset(tabs1[:].bitcast(I32), 0)
-        nc.gpsimd.memset(w1s1[:].bitcast(I32), 0)
+            nc.sync.dma_start(tabs[32 * q : 32 * q + 8, :].bitcast(I32), tab_scales[:, 4 * q : 4 * q + 4, :].bitcast(I32))
 
         windows = [keep.tile([P, T2], F32, name=f"window{n}") for n in range(NT)]
         for n in range(NT):
-            (nc.vector if n < 2 else nc.gpsimd).memset(windows[n][:], 0.0)
+            nc.vector.memset(windows[n][:], 0.0)
 
         phases = {}
 
@@ -118,40 +117,36 @@ def tile_list_lattice_flow_adjoint_kernel(
         w1s0 = keep.tile([P, H], U8, name="w1s0", align_bytes=64)
         w1_planes = [w1s0, w1s1]
 
-        def gather_table():
-            nc.vector.tensor_copy(tabs0[:], tabs[:].indirect(idx[:]))
-            nc.gpsimd.dma_start(tabs1[0:100, :].bitcast(I32), tabs0[4:104, :].bitcast(I32))
+        def order_w1():
+            for a in range(NA):
+                nc.vector.tensor_copy(
+                    w1_codes[a][:].rearrange("p (b t m i) -> p b m t i", t=PACK, b=NB, i=4),
+                    take("w1", a, 0)[:].bitcast(U32).rearrange("p (b m i t) -> p b m t i", t=PACK, b=NB, i=4),
+                )
+                load_next()
             nc.vector.tensor_copy(
                 w1s0[:].rearrange("p (b t m) -> p b t m", t=PACK, m=P), w1s[:].rearrange("p (b m t) -> p b t m", t=PACK, m=P)
             )
-            nc.gpsimd.dma_start(w1s1[0:100, :].bitcast(I32), w1s0[4:104, :].bitcast(I32))
+            nc.sync.dma_start(w1s1[0:100, :].bitcast(I32), w1s0[4:104, :].bitcast(I32))
+
+        def gather_table():
+            nc.vector.tensor_copy(tabs0[:], tabs[:].indirect(idx[:]))
+            nc.sync.dma_start(tabs1[0:100, :].bitcast(I32), tabs0[4:104, :].bitcast(I32))
             for a in range(NA):
                 nc.vector.tensor_copy(v_codes[a][:], take("tab", a, 0)[:].bitcast(U32).indirect(idx[:]))
-                load_next()
-            for a in range(NA):
-                for b in range(NB):
-                    cols = slice(b * KP, (b + 1) * KP)
-                    nc.vector.tensor_copy(
-                        w1_codes[a][:, cols].rearrange("p (t m i) -> p m t i", t=PACK, i=4),
-                        take("w1", a, 0)[:, cols].bitcast(U32).rearrange("p (m i t) -> p m t i", t=PACK, i=4),
-                    )
                 load_next()
 
         cosf, sinf, hbank, zb, z_codes, z_scales = {}, {}, {}, {}, {}, {}
 
-        def trig(b, h, groups):
-            js = slice(h * JW, (h + 1) * JW)
-            cosf[b, h] = four.tile([P, PACK, JW], F32, name="cosf")
-            sinf[b, h] = phases[b][:, :, js]
-            for ts in groups:
-                x = phases[b][:, ts, js]
-                nc.scalar.activation(cosf[b, h][:, ts, :], x, ACT.Sin, scale=0.5)
-                nc.scalar.activation(cosf[b, h][:, ts, :], cosf[b, h][:, ts, :], ACT.Square, scale=math.sqrt(2.0))
-                nc.scalar.activation(sinf[b, h][:, ts, :], x, ACT.Sin)
-                for t in range(ts.start, ts.stop):
-                    nc.scalar.activation(
-                        sinf[b, h][:, t, :], sinf[b, h][:, t, :], ACT.Identity, scale=amp_sb[:, b, t : t + 1], bias=-1.0
-                    )
+        def trig(b, t, js):
+            x = phases[b][:, t, js]
+            c = six.tile([P, js.stop - js.start], F32, name="small", align_bytes=64)
+            s = six.tile([P, js.stop - js.start], F32, name="small", align_bytes=64)
+            nc.scalar.activation(c[:], x, ACT.Abs)
+            nc.scalar.activation(s[:], x, ACT.Sin)
+            nc.scalar.activation(c[:], c[:], ACT.Sin, bias=-math.pi / 2)
+            nc.gpsimd.tensor_scalar(s[:], s[:], amp_sb[:, b, t : t + 1], -1.0, ALU.mult, ALU.add)
+            nc.gpsimd.tensor_tensor(x, s[:], c[:], ALU.mult)
 
         def first_product(b, h):
             js = slice(h * JW, (h + 1) * JW)
@@ -169,18 +164,16 @@ def tile_list_lattice_flow_adjoint_kernel(
                         stop=(a == NA - 1),
                     )
 
-        def times_cos(b, h):
+        def times_factor(b, h):
             for t in range(PACK):
-                c = cosf[b, h][:, t, :]
-                nc.vector.scalar_tensor_tensor(c, c, 1.0, hbank[b, h, t][:], ALU.subtract, ALU.mult)
+                f = phases[b][:, t, h * JW : (h + 1) * JW]
+                nc.vector.tensor_tensor(f, f, hbank[b, h, t][:], ALU.mult)
 
-        def times_sin(b, h, engine):
-            zb[b, h] = two.tile([P, JW, PACK], BF16, name="zb", align_bytes=64)
-            engine.tensor_tensor(
+        def round_z(b, h, copy):
+            zb[b, h] = six.tile([P, JW, PACK], BF16, name="small", align_bytes=64)
+            copy(
                 zb[b, h][:].rearrange("p (c i) t -> p c t i", i=4),
-                cosf[b, h][:].rearrange("p t (c i) -> p c t i", i=4),
-                sinf[b, h].rearrange("p t (c i) -> p c t i", i=4),
-                ALU.mult,
+                phases[b][:, :, h * JW : (h + 1) * JW].rearrange("p t (c i) -> p c t i", i=4),
             )
 
         def quantise_z(b, h):
@@ -190,9 +183,9 @@ def tile_list_lattice_flow_adjoint_kernel(
 
         w2b, w2_codes, w2_scales = {}, {}, {}
 
-        def round_w2(b):
-            w2b[b] = two.tile([P, N, PACK], BF16, name="w2b", align_bytes=64)
-            nc.scalar.copy(
+        def round_w2(b, copy):
+            w2b[b] = six.tile([P, N, PACK], BF16, name="small", align_bytes=64)
+            copy(
                 w2b[b][:].rearrange("p (c i) t -> p c t i", i=4),
                 take("w2", b, 0)[:].rearrange("p (t c i) -> p c t i", t=PACK, i=4),
             )
@@ -225,61 +218,40 @@ def tile_list_lattice_flow_adjoint_kernel(
             places = idx2[:, h * (JW // 16) : (h + 1) * (JW // 16)]
             nc.vector.tensor_tensor(windows[n][:].indirect(places), forces[h, n][:], take("wgo", 0, 0)[:, h * JW : (h + 1) * JW], ALU.mult)
 
-        whole = [slice(0, PACK)]
-        single = [slice(t, t + 1) for t in range(PACK)]
-        V = nc.vector
-        E00, E01, E10, E20, E11, E21 = V, V, V, V, V, V
-
-        for t in range(PACK):
-            gather_phases(0, t)
-        trig(0, 0, single)
-        trig(0, 1, whole)
-        for t in range(PACK):
-            gather_phases(1, t)
-        trig(1, 0, whole)
-        trig(1, 1, whole)
+        SC, VC = nc.scalar.copy, nc.vector.tensor_copy
+        for b in range(NB):
+            for t in range(PACK):
+                gather_phases(b, t)
+                if (b, t) == (0, 0):
+                    order_w1()
+                trig(b, t, slice(0, S if b < NB - 1 else JW))
         gather_table()
-        first_product(0, 0)
-        gather_phases(2, 0)
-        times_cos(0, 0)
-        first_product(0, 1)
-        gather_phases(2, 1)
-        times_sin(0, 0, E00)
-        times_cos(0, 1)
+        for t in range(PACK):
+            trig(NB - 1, t, slice(JW, S))
+        for b, h in ((0, 0), (1, 0), (2, 0), (0, 1), (1, 1)):
+            first_product(b, h)
+            times_factor(b, h)
+        round_z(0, 0, SC)
+        round_z(1, 0, SC)
+        round_z(2, 0, SC)
+        round_w2(0, VC)
         quantise_z(0, 0)
-        first_product(1, 0)
-        gather_phases(2, 2)
-        times_sin(0, 1, E01)
-        gather_phases(2, 3)
-        quantise_z(0, 1)
-        round_w2(0)
-        round_w2(1)
-        trig(2, 0, whole)
-        times_cos(1, 0)
-        first_product(1, 1)
-        quantise_w2(0)
-        round_w2(2)
-        times_sin(1, 0, E10)
-        quantise_w2(1)
-        times_cos(1, 1)
+        round_w2(1, VC)
         quantise_z(1, 0)
-        first_product(2, 0)
-        times_sin(1, 1, E11)
-        quantise_w2(2)
-        trig(2, 1, whole)
-        times_cos(2, 0)
-        quantise_z(1, 1)
-        first_product(2, 1)
-        times_sin(2, 0, E20)
-        times_cos(2, 1)
+        round_w2(2, VC)
         quantise_z(2, 0)
+        quantise_w2(0)
+        quantise_w2(1)
+        quantise_w2(2)
+        first_product(2, 1)
+        times_factor(2, 1)
         for n in range(NT):
             second_product(0, n)
-        times_sin(2, 1, E21)
-        scatter(0, 0)
-        quantise_z(2, 1)
-        for n in range(1, NT):
-            scatter(0, n)
+        for b in range(NB):
+            round_z(b, 1, SC)
+            scatter(0, b)
+            quantise_z(b, 1)
+        scatter(0, 3)
         for n in range(NT):
             second_product(1, n)
             scatter(1, n)

@@ -26,7 +26,7 @@ JW = 512
 NH = S // JW
 NT = N // P
 RING = 7
-SMALL = 6
+SMALL = 8
 
 
 def tile_list_lattice_flow_adjoint_kernel(
@@ -120,8 +120,8 @@ def tile_list_lattice_flow_adjoint_kernel(
         def order_w1():
             for a in range(NA):
                 nc.vector.tensor_copy(
-                    w1_codes[a][:].rearrange("p (b t m i) -> p b m t i", t=PACK, b=NB, i=4),
-                    take("w1", a, 0)[:].bitcast(U32).rearrange("p (b m i t) -> p b m t i", t=PACK, b=NB, i=4),
+                    w1_codes[a][:].rearrange("p (b t m i) -> p m b t i", t=PACK, b=NB, i=4),
+                    take("w1", a, 0)[:].bitcast(U32).rearrange("p (b m i t) -> p m b t i", t=PACK, b=NB, i=4),
                 )
                 load_next()
             nc.vector.tensor_copy(
@@ -132,9 +132,12 @@ def tile_list_lattice_flow_adjoint_kernel(
         def gather_table():
             nc.vector.tensor_copy(tabs0[:], tabs[:].indirect(idx[:]))
             nc.sync.dma_start(tabs1[0:100, :].bitcast(I32), tabs0[4:104, :].bitcast(I32))
-            for a in range(NA):
-                nc.vector.tensor_copy(v_codes[a][:], take("tab", a, 0)[:].bitcast(U32).indirect(idx[:]))
-                load_next()
+            for h in range(NH):
+                for a in range(NA):
+                    picks = idx[:, h * (JW // 16) : (h + 1) * (JW // 16)]
+                    nc.vector.tensor_copy(v_codes[a][:, h * JW : (h + 1) * JW], take("tab", a, 0)[:].bitcast(U32).indirect(picks))
+            load_next()
+            load_next()
 
         cosf, sinf, hbank, zb, z_codes, z_scales = {}, {}, {}, {}, {}, {}
 
@@ -236,21 +239,27 @@ def tile_list_lattice_flow_adjoint_kernel(
         round_z(2, 0, SC)
         round_w2(0, VC)
         quantise_z(0, 0)
-        round_w2(1, VC)
+        round_w2(1, SC)
         quantise_z(1, 0)
-        round_w2(2, VC)
+        round_w2(2, SC)
         quantise_z(2, 0)
         quantise_w2(0)
         quantise_w2(1)
         quantise_w2(2)
         first_product(2, 1)
         times_factor(2, 1)
-        for n in range(NT):
-            second_product(0, n)
+        second_product(0, 0)
+        second_product(0, 1)
         for b in range(NB):
             round_z(b, 1, SC)
-            scatter(0, b)
-            quantise_z(b, 1)
+        second_product(0, 2)
+        second_product(0, 3)
+        quantise_z(0, 1)
+        scatter(0, 0)
+        quantise_z(1, 1)
+        scatter(0, 1)
+        quantise_z(2, 1)
+        scatter(0, 2)
         scatter(0, 3)
         for n in range(NT):
             second_product(1, n)

@@ -12,21 +12,27 @@ I32 = mybir.dt.int32
 U32 = mybir.dt.uint32
 U16 = mybir.dt.uint16
 U8 = mybir.dt.uint8
-E4 = mybir.dt.float8_e4m3fn_x4
-E5 = mybir.dt.float8_e5m2_x4
+E4M3X4 = mybir.dt.float8_e4m3fn_x4
+E5M2X4 = mybir.dt.float8_e5m2_x4
 ACT = mybir.ActivationFunctionType
 ALU = mybir.AluOpType
 
 P = 128
 PACK = 4
-KP = P * PACK
-NA = K // KP
-NB = H // KP
-JW = 512
-NH = S // JW
-NT = N // P
-RING = 7
-SMALL = 8
+PASS = P * PACK
+K_PASSES = K // PASS
+ROW_BLOCKS = H // PASS
+HALF = 512
+HALVES = S // HALF
+OUT_TILES = N // P
+PER_COLUMN = 16
+QUADRANTS = 4
+SCALE_ROWS = 4
+SHIFTED = 32 * (QUADRANTS - 1) + SCALE_ROWS
+LINE = 4
+STREAM_SLOTS = 7
+SMALL_SLOTS = 6
+H_BANKS, Y_BANKS = 6, 2
 
 
 def tile_list_lattice_flow_adjoint_kernel(
@@ -35,233 +41,244 @@ def tile_list_lattice_flow_adjoint_kernel(
     nc = tc.nc
     with ExitStack() as ctx:
         keep = ctx.enter_context(tc.tile_pool(name="keep", bufs=1))
-        ring = ctx.enter_context(tc.tile_pool(name="ring", bufs=RING))
-        three = ctx.enter_context(tc.tile_pool(name="three", bufs=3))
-        four = ctx.enter_context(tc.tile_pool(name="four", bufs=4))
-        six = ctx.enter_context(tc.tile_pool(name="six", bufs=SMALL))
-        hps = ctx.enter_context(tc.psum_pool(name="hps", bufs=6))
-        yps = ctx.enter_context(tc.psum_pool(name="yps", bufs=2))
+        stream_pool = ctx.enter_context(tc.tile_pool(name="stream", bufs=STREAM_SLOTS))
+        phase_pool = ctx.enter_context(tc.tile_pool(name="phases", bufs=ROW_BLOCKS))
+        y_pool = ctx.enter_context(tc.tile_pool(name="y", bufs=OUT_TILES))
+        small_pool = ctx.enter_context(tc.tile_pool(name="small", bufs=SMALL_SLOTS))
+        h_psum = ctx.enter_context(tc.psum_pool(name="h_psum", bufs=H_BANKS))
+        y_psum = ctx.enter_context(tc.psum_pool(name="y_psum", bufs=Y_BANKS))
 
-        idx = keep.tile([P, S // 16], U16, name="idx")
+        def entries(half):
+            return slice(half * HALF, (half + 1) * HALF)
+
+        def list_columns(half):
+            return slice(half * HALF // PER_COLUMN, (half + 1) * HALF // PER_COLUMN)
+
+        idx = keep.tile([P, S // PER_COLUMN], U16, name="idx")
         nc.sync.dma_start(idx[:], offs)
-        idx2 = keep.tile([P, S // 16], U16, name="idx2")
+        idx2 = keep.tile([P, S // PER_COLUMN], U16, name="idx2")
 
-        sT_rows = sT.rearrange("(b p t) c -> b t p c", p=P, t=PACK)
-        w2_rows = w2.rearrange("(b p t) n -> b p (t n)", p=P, t=PACK)
-        stream = (
-            [("s", 0, 0), ("w1", 0, 0), ("w1", 1, 0)]
-            + [("s", b, t) for b in range(NB) for t in range(PACK)][1:]
-            + [("tab", 0, 0), ("tab", 1, 0)]
-            + [("w2", b, 0) for b in range(NB)]
-            + [("wgo", 0, 0)]
+        sT_slices = sT.rearrange("(b p t) c -> b t p c", p=P, t=PACK)
+        w2_blocks = w2.rearrange("(b p t) n -> b p (t n)", p=P, t=PACK)
+        slices = [(b, t) for b in range(ROW_BLOCKS) for t in range(PACK)]
+        sources = {("sT", b, t): (sT_slices[b, t], F32) for b, t in slices}
+        for a in range(K_PASSES):
+            sources["w1", a] = (w1_words[a].rearrange("p c i -> p (c i)").bitcast(I32), I32)
+            sources["tab", a] = (tab_words[a].rearrange("p c i -> p (c i)").bitcast(I32), I32)
+        for b in range(ROW_BLOCKS):
+            sources["w2", b] = (w2_blocks[b], F32)
+        sources["wgo",] = (wgo, F32)
+        to_load = (
+            [("sT",) + slices[0]]
+            + [("w1", a) for a in range(K_PASSES)]
+            + [("sT",) + s for s in slices[1:]]
+            + [("tab", a) for a in range(K_PASSES)]
+            + [("w2", b) for b in range(ROW_BLOCKS)]
+            + [("wgo",)]
         )
-        loaded = []
+        loaded = {}
 
-        def load_next():
-            if len(loaded) == len(stream):
-                return
-            kind, u, v = stream[len(loaded)]
-            if kind == "s":
-                tile = ring.tile([P, T], F32, name="in", align_bytes=64)
-                nc.sync.dma_start(tile[:], sT_rows[u, v])
-            elif kind == "tab":
-                tile = ring.tile([P, T], I32, name="in", align_bytes=64)
-                nc.sync.dma_start(tile[:], tab_words[u].rearrange("p c i -> p (c i)").bitcast(I32))
-            elif kind == "w1":
-                tile = ring.tile([P, H], I32, name="in", align_bytes=64)
-                nc.sync.dma_start(tile[:], w1_words[u].rearrange("p c i -> p (c i)").bitcast(I32))
-            elif kind == "wgo":
-                tile = ring.tile([P, S], F32, name="in", align_bytes=64)
-                nc.sync.dma_start(tile[:], wgo)
-            else:
-                tile = ring.tile([P, PACK * N], F32, name="in", align_bytes=64)
-                nc.sync.dma_start(tile[:], w2_rows[u])
-            loaded.append(tile)
+        def load_next(count=1):
+            for key in to_load[len(loaded) : len(loaded) + count]:
+                source, dtype = sources[key]
+                loaded[key] = stream_pool.tile([P, source.shape[1]], dtype, name="slot", align_bytes=64)
+                nc.sync.dma_start(loaded[key][:], source)
 
-        def take(kind, u, v):
-            return loaded[stream.index((kind, u, v))]
+        def load_scale_rows(tile, scales):
+            for q in range(QUADRANTS):
+                nc.sync.dma_start(
+                    tile[32 * q : 32 * q + K_PASSES * SCALE_ROWS, :].bitcast(I32),
+                    scales[:, SCALE_ROWS * q : SCALE_ROWS * (q + 1), :].bitcast(I32),
+                )
 
-        tabs = keep.tile([P, T], U8, name="tabs", align_bytes=64)
-        w1s = keep.tile([P, H], U8, name="w1s", align_bytes=64)
-        tabs1 = keep.tile([P, S], U8, name="tabs1", align_bytes=64)
-        w1s1 = keep.tile([P, H], U8, name="w1s1", align_bytes=64)
-        nc.gpsimd.memset(w1s[:].bitcast(I32), 0)
-        nc.gpsimd.memset(tabs[:].bitcast(I32), 0)
+        def shift_second_pass(plane, both):
+            nc.sync.dma_start(plane[0:SHIFTED, :].bitcast(I32), both[SCALE_ROWS : SCALE_ROWS + SHIFTED, :].bitcast(I32))
+
+        tab_rows = keep.tile([P, T], U8, name="tab_rows", align_bytes=64)
+        w1_rows = keep.tile([P, H], U8, name="w1_rows", align_bytes=64)
+        v_plane1 = keep.tile([P, S], U8, name="v_plane1", align_bytes=64)
+        w1_plane1 = keep.tile([P, H], U8, name="w1_plane1", align_bytes=64)
+        nc.gpsimd.memset(w1_rows[:].bitcast(I32), 0)
+        nc.gpsimd.memset(tab_rows[:].bitcast(I32), 0)
         load_next()
-        amp_sb = keep.tile([P, NB, PACK], F32, name="amp_sb")
+        amp_sb = keep.tile([P, ROW_BLOCKS, PACK], F32, name="amp_sb")
         nc.sync.dma_start(amp_sb[:], amp.rearrange("(b p t) -> p b t", p=P, t=PACK))
-        for q in range(4):
-            nc.sync.dma_start(w1s[32 * q : 32 * q + 8, :].bitcast(I32), w1_scales[:, 4 * q : 4 * q + 4, :].bitcast(I32))
-        for unused in range(RING - 1):
-            load_next()
+        load_scale_rows(w1_rows, w1_scales)
+        load_next(STREAM_SLOTS - 1)
         nc.sync.dma_start(idx2[:], offs2)
-        for q in range(4):
-            nc.sync.dma_start(tabs[32 * q : 32 * q + 8, :].bitcast(I32), tab_scales[:, 4 * q : 4 * q + 4, :].bitcast(I32))
+        load_scale_rows(tab_rows, tab_scales)
 
-        windows = [keep.tile([P, T2], F32, name=f"window{n}") for n in range(NT)]
-        for n in range(NT):
-            nc.vector.memset(windows[n][:], 0.0)
+        windows = [keep.tile([P, T2], F32, name=f"window{n}") for n in range(OUT_TILES)]
+        for window in windows:
+            nc.vector.memset(window[:], 0.0)
 
-        phases = {}
+        v_codes = [keep.tile([P, S], U32, name=f"v_codes{a}", align_bytes=64) for a in range(K_PASSES)]
+        v_plane0 = keep.tile([P, S], U8, name="v_plane0", align_bytes=64)
+        v_planes = [v_plane0, v_plane1]
+        w1_codes = [keep.tile([P, H], U32, name=f"w1_codes{a}", align_bytes=64) for a in range(K_PASSES)]
+        w1_plane0 = keep.tile([P, H], U8, name="w1_plane0", align_bytes=64)
+        w1_planes = [w1_plane0, w1_plane1]
+
+        work, h_banks, z_bf16, z_codes, z_scales = {}, {}, {}, {}, {}
+        w2_bf16, w2_codes, w2_scales, y_sb = {}, {}, {}, {}
 
         def gather_phases(b, t):
             if t == 0:
-                phases[b] = three.tile([P, PACK, S], F32, name="phases")
-            nc.vector.tensor_copy(phases[b][:, t, :], take("s", b, t)[:].indirect(idx[:]))
+                work[b] = phase_pool.tile([P, PACK, S], F32, name="work")
+            nc.vector.tensor_copy(work[b][:, t, :], loaded["sT", b, t][:].indirect(idx[:]))
             load_next()
 
-        v_codes = [keep.tile([P, S], U32, name=f"v_codes{a}", align_bytes=64) for a in range(NA)]
-        tabs0 = keep.tile([P, S], U8, name="tabs0", align_bytes=64)
-        v_scales = [tabs0, tabs1]
-        w1_codes = [keep.tile([P, H], U32, name=f"w1_codes{a}", align_bytes=64) for a in range(NA)]
-        w1s0 = keep.tile([P, H], U8, name="w1s0", align_bytes=64)
-        w1_planes = [w1s0, w1s1]
-
-        def order_w1():
-            for a in range(NA):
+        def reorder_w1():
+            for a in range(K_PASSES):
                 nc.vector.tensor_copy(
-                    w1_codes[a][:].rearrange("p (b t m i) -> p m b t i", t=PACK, b=NB, i=4),
-                    take("w1", a, 0)[:].bitcast(U32).rearrange("p (b m i t) -> p m b t i", t=PACK, b=NB, i=4),
+                    w1_codes[a][:].rearrange("p (b t m i) -> p m b t i", t=PACK, b=ROW_BLOCKS, i=LINE),
+                    loaded["w1", a][:].bitcast(U32).rearrange("p (b m i t) -> p m b t i", t=PACK, b=ROW_BLOCKS, i=LINE),
                 )
                 load_next()
             nc.vector.tensor_copy(
-                w1s0[:].rearrange("p (b t m) -> p b t m", t=PACK, m=P), w1s[:].rearrange("p (b m t) -> p b t m", t=PACK, m=P)
+                w1_plane0[:].rearrange("p (b t m) -> p t b m", t=PACK, m=P),
+                w1_rows[:].rearrange("p (b m t) -> p t b m", t=PACK, m=P),
             )
-            nc.sync.dma_start(w1s1[0:100, :].bitcast(I32), w1s0[4:104, :].bitcast(I32))
+            shift_second_pass(w1_plane1, w1_plane0)
 
         def gather_table():
-            nc.vector.tensor_copy(tabs0[:], tabs[:].indirect(idx[:]))
-            nc.sync.dma_start(tabs1[0:100, :].bitcast(I32), tabs0[4:104, :].bitcast(I32))
-            for h in range(NH):
-                for a in range(NA):
-                    picks = idx[:, h * (JW // 16) : (h + 1) * (JW // 16)]
-                    nc.vector.tensor_copy(v_codes[a][:, h * JW : (h + 1) * JW], take("tab", a, 0)[:].bitcast(U32).indirect(picks))
-            load_next()
-            load_next()
+            nc.vector.tensor_copy(v_plane0[:], tab_rows[:].indirect(idx[:]))
+            shift_second_pass(v_plane1, v_plane0)
+            for half in range(HALVES):
+                for a in range(K_PASSES):
+                    words = loaded["tab", a][:].bitcast(U32)
+                    nc.vector.tensor_copy(v_codes[a][:, entries(half)], words.indirect(idx[:, list_columns(half)]))
+            load_next(K_PASSES)
 
-        cosf, sinf, hbank, zb, z_codes, z_scales = {}, {}, {}, {}, {}, {}
+        def sines(minus_cos, sin, x):
+            nc.scalar.activation(minus_cos, x, ACT.Abs)
+            nc.scalar.activation(sin, x, ACT.Sin)
+            nc.scalar.activation(minus_cos, minus_cos, ACT.Sin, bias=-math.pi / 2)
 
-        def trig(b, t, js):
-            x = phases[b][:, t, js]
-            c = six.tile([P, js.stop - js.start], F32, name="small", align_bytes=64)
-            s = six.tile([P, js.stop - js.start], F32, name="small", align_bytes=64)
-            nc.scalar.activation(c[:], x, ACT.Abs)
-            nc.scalar.activation(s[:], x, ACT.Sin)
-            nc.scalar.activation(c[:], c[:], ACT.Sin, bias=-math.pi / 2)
-            nc.gpsimd.tensor_scalar(s[:], s[:], amp_sb[:, b, t : t + 1], -1.0, ALU.mult, ALU.add)
-            nc.gpsimd.tensor_tensor(x, s[:], c[:], ALU.mult)
+        def amp_sin_minus_one_on_scalar(sin, b, t):
+            nc.scalar.activation(sin, sin, ACT.Identity, scale=amp_sb[:, b, t : t + 1], bias=-1.0)
 
-        def first_product(b, h):
-            js = slice(h * JW, (h + 1) * JW)
+        def factor(b, t, columns):
+            x = work[b][:, t, columns]
+            minus_cos = small_pool.tile([P, columns.stop - columns.start], F32, name="small", align_bytes=64)
+            sin = small_pool.tile([P, columns.stop - columns.start], F32, name="small", align_bytes=64)
+            sines(minus_cos[:], sin[:], x)
+            if (b, t) == slices[0]:
+                amp_sin_minus_one_on_scalar(sin[:], b, t)
+            else:
+                nc.gpsimd.tensor_scalar(sin[:], sin[:], amp_sb[:, b, t : t + 1], -1.0, ALU.mult, ALU.add)
+            nc.gpsimd.tensor_tensor(x, sin[:], minus_cos[:], ALU.mult)
+
+        def first_product(b, half):
             for t in range(PACK):
-                cols = slice(b * KP + t * P, b * KP + (t + 1) * P)
-                hbank[b, h, t] = hps.tile([P, JW], F32, name="hbank")
-                for a in range(NA):
+                rows = slice(b * PASS + t * P, b * PASS + (t + 1) * P)
+                h_banks[b, half, t] = h_psum.tile([P, HALF], F32, name="h_bank")
+                for a in range(K_PASSES):
                     nc.tensor.matmul_mx(
-                        hbank[b, h, t][:],
-                        lhsT=w1_codes[a][:, cols].bitcast(E4),
-                        lhsT_scale=w1_planes[a][:, cols],
-                        rhs=v_codes[a][:, js].bitcast(E5),
-                        rhs_scale=v_scales[a][:, js],
+                        h_banks[b, half, t][:],
+                        lhsT=w1_codes[a][:, rows].bitcast(E4M3X4),
+                        lhsT_scale=w1_planes[a][:, rows],
+                        rhs=v_codes[a][:, entries(half)].bitcast(E5M2X4),
+                        rhs_scale=v_planes[a][:, entries(half)],
                         start=(a == 0),
-                        stop=(a == NA - 1),
+                        stop=(a == K_PASSES - 1),
                     )
 
-        def times_factor(b, h):
+        def times_h(unit_values, b, half):
             for t in range(PACK):
-                f = phases[b][:, t, h * JW : (h + 1) * JW]
-                nc.vector.tensor_tensor(f, f, hbank[b, h, t][:], ALU.mult)
+                values = unit_values[:, t, :]
+                nc.vector.tensor_tensor(values, values, h_banks[b, half, t][:], ALU.mult)
 
-        def round_z(b, h, copy):
-            zb[b, h] = six.tile([P, JW, PACK], BF16, name="small", align_bytes=64)
-            copy(
-                zb[b, h][:].rearrange("p (c i) t -> p c t i", i=4),
-                phases[b][:, :, h * JW : (h + 1) * JW].rearrange("p t (c i) -> p c t i", i=4),
-            )
+        def by_slice(values):
+            return values.rearrange("p t (c i) -> p c t i", i=LINE)
 
-        def quantise_z(b, h):
-            z_codes[b, h] = keep.tile([P, JW], U32, name=f"z_codes{b}{h}", align_bytes=64)
-            z_scales[b, h] = keep.tile([P, JW], U8, name=f"z_scales{b}{h}", align_bytes=64)
-            nc.vector.quantize_mx(z_codes[b, h][:].bitcast(E4), z_scales[b, h][:], zb[b, h][:].rearrange("p c t -> p (c t)"))
+        def side_by_side(tile):
+            return tile[:].rearrange("p (c i) t -> p c t i", i=LINE)
 
-        w2b, w2_codes, w2_scales = {}, {}, {}
+        def round_z(b, half):
+            z_bf16[b, half] = small_pool.tile([P, HALF, PACK], BF16, name="small", align_bytes=64)
+            nc.scalar.copy(side_by_side(z_bf16[b, half]), by_slice(work[b][:, :, entries(half)]))
 
         def round_w2(b, copy):
-            w2b[b] = six.tile([P, N, PACK], BF16, name="small", align_bytes=64)
-            copy(
-                w2b[b][:].rearrange("p (c i) t -> p c t i", i=4),
-                take("w2", b, 0)[:].rearrange("p (t c i) -> p c t i", t=PACK, i=4),
-            )
-            load_next()
+            w2_bf16[b] = small_pool.tile([P, N, PACK], BF16, name="small", align_bytes=64)
+            copy(side_by_side(w2_bf16[b]), by_slice(loaded["w2", b][:].rearrange("p (t n) -> p t n", t=PACK)))
 
-        def quantise_w2(b):
-            w2_codes[b] = keep.tile([P, N], U32, name=f"w2_codes{b}", align_bytes=64)
-            w2_scales[b] = keep.tile([P, N], U8, name=f"w2_scales{b}", align_bytes=64)
-            nc.vector.quantize_mx(w2_codes[b][:].bitcast(E4), w2_scales[b][:], w2b[b][:].rearrange("p c t -> p (c t)"))
+        def quantise(source, name):
+            codes = keep.tile([P, source.shape[1]], U32, name=f"{name}_codes", align_bytes=64)
+            scales = keep.tile([P, source.shape[1]], U8, name=f"{name}_scales", align_bytes=64)
+            nc.vector.quantize_mx(codes[:].bitcast(E4M3X4), scales[:], source.rearrange("p c t -> p (c t)"))
+            return codes, scales
 
-        forces = {}
+        def quantise_z(b, half):
+            z_codes[b, half], z_scales[b, half] = quantise(z_bf16[b, half][:], f"z{b}{half}")
 
-        def second_product(h, n):
-            cols = slice(n * P, (n + 1) * P)
-            ybank = yps.tile([P, JW], F32, name="ybank")
-            for b in range(NB):
+        def second_product(half, n):
+            columns = slice(n * P, (n + 1) * P)
+            y_bank = y_psum.tile([P, HALF], F32, name="y_bank")
+            for b in range(ROW_BLOCKS):
                 nc.tensor.matmul_mx(
-                    ybank[:],
-                    lhsT=w2_codes[b][:, cols].bitcast(E4),
-                    lhsT_scale=w2_scales[b][:, cols],
-                    rhs=z_codes[b, h][:].bitcast(E4),
-                    rhs_scale=z_scales[b, h][:],
+                    y_bank[:],
+                    lhsT=w2_codes[b][:, columns].bitcast(E4M3X4),
+                    lhsT_scale=w2_scales[b][:, columns],
+                    rhs=z_codes[b, half][:].bitcast(E4M3X4),
+                    rhs_scale=z_scales[b, half][:],
                     start=(b == 0),
-                    stop=(b == NB - 1),
+                    stop=(b == ROW_BLOCKS - 1),
                 )
-            forces[h, n] = four.tile([P, JW], F32, name="forces")
-            nc.scalar.copy(forces[h, n][:], ybank[:])
+            y_sb[half, n] = y_pool.tile([P, HALF], F32, name="y_sb")
+            nc.scalar.copy(y_sb[half, n][:], y_bank[:])
 
-        def scatter(h, n):
-            places = idx2[:, h * (JW // 16) : (h + 1) * (JW // 16)]
-            nc.vector.tensor_tensor(windows[n][:].indirect(places), forces[h, n][:], take("wgo", 0, 0)[:, h * JW : (h + 1) * JW], ALU.mult)
+        def scatter(half, n):
+            nc.vector.tensor_tensor(
+                windows[n][:].indirect(idx2[:, list_columns(half)]),
+                y_sb[half, n][:],
+                loaded["wgo",][:, entries(half)],
+                ALU.mult,
+            )
 
-        SC, VC = nc.scalar.copy, nc.vector.tensor_copy
-        for b in range(NB):
-            for t in range(PACK):
-                gather_phases(b, t)
-                if (b, t) == (0, 0):
-                    order_w1()
-                trig(b, t, slice(0, S if b < NB - 1 else JW))
+        last = ROW_BLOCKS - 1
+        for b, t in slices:
+            gather_phases(b, t)
+            if (b, t) == slices[0]:
+                reorder_w1()
+            factor(b, t, entries(0) if b == last else slice(0, S))
         gather_table()
-        for t in range(PACK):
-            trig(NB - 1, t, slice(JW, S))
-        for b, h in ((0, 0), (1, 0), (2, 0), (0, 1), (1, 1)):
-            first_product(b, h)
-            times_factor(b, h)
-        round_z(0, 0, SC)
-        round_z(1, 0, SC)
-        round_z(2, 0, SC)
-        round_w2(0, VC)
-        quantise_z(0, 0)
-        round_w2(1, SC)
-        quantise_z(1, 0)
-        round_w2(2, SC)
-        quantise_z(2, 0)
-        quantise_w2(0)
-        quantise_w2(1)
-        quantise_w2(2)
-        first_product(2, 1)
-        times_factor(2, 1)
+
+        for b, half in [(b, half) for half in range(HALVES) for b in range(ROW_BLOCKS)][:-1]:
+            first_product(b, half)
+            times_h(work[b][:, :, entries(half)], b, half)
+
+        for b in range(ROW_BLOCKS):
+            round_z(b, 0)
+            round_w2(b, nc.scalar.copy if b == 0 else nc.vector.tensor_copy)
+        for b in range(ROW_BLOCKS):
+            quantise_z(b, 0)
+            w2_codes[b], w2_scales[b] = quantise(w2_bf16[b][:], f"w2{b}")
+
         second_product(0, 0)
         second_product(0, 1)
-        for b in range(NB):
-            round_z(b, 1, SC)
+        round_z(0, 1)
+        last_sin = work[last][:, :, entries(1)]
+        last_cos = stream_pool.tile([P, PACK, HALF], F32, name="slot", align_bytes=64)
+        sines(last_cos[:], last_sin, last_sin)
+        for t in range(PACK):
+            amp_sin_minus_one_on_scalar(last_sin[:, t, :], last, t)
+        round_z(1, 1)
         second_product(0, 2)
         second_product(0, 3)
-        quantise_z(0, 1)
+        first_product(last, 1)
         scatter(0, 0)
-        quantise_z(1, 1)
+        quantise_z(0, 1)
         scatter(0, 1)
-        quantise_z(2, 1)
+        times_h(last_cos[:], last, 1)
+        quantise_z(1, 1)
+        z_bf16[last, 1] = small_pool.tile([P, HALF, PACK], BF16, name="small", align_bytes=64)
+        nc.vector.tensor_tensor(side_by_side(z_bf16[last, 1]), by_slice(last_cos[:]), by_slice(last_sin), ALU.mult)
         scatter(0, 2)
+        quantise_z(last, 1)
         scatter(0, 3)
-        for n in range(NT):
+
+        for n in range(OUT_TILES):
             second_product(1, n)
             scatter(1, n)
             nc.sync.dma_start(out[n * P : (n + 1) * P, :], windows[n][:])

@@ -30,8 +30,8 @@ QUADRANTS = 4
 SCALE_ROWS = 4
 SHIFTED = 32 * (QUADRANTS - 1) + SCALE_ROWS
 LINE = 4
-STREAM_SLOTS = 7
-SMALL_SLOTS = 6
+STREAM_SLOTS = 6
+SMALL_SLOTS = 8
 H_BANKS, Y_BANKS = 6, 2
 
 
@@ -69,24 +69,27 @@ def tile_list_lattice_flow_adjoint_kernel(
             sources["w2", b] = (w2_blocks[b], F32)
         sources["wgo",] = (wgo, F32)
         to_load = (
-            [("sT",) + slices[0]]
+            [("sT",) + s for s in slices]
             + [("w1", a) for a in range(K_PASSES)]
-            + [("sT",) + s for s in slices[1:]]
             + [("tab", a) for a in range(K_PASSES)]
             + [("w2", b) for b in range(ROW_BLOCKS)]
             + [("wgo",)]
         )
         loaded = {}
+        lent = {("sT", 1, 0): "w1_plane0", ("sT", 1, 1): "v_plane0"}
 
         def load_next(count=1):
             for key in to_load[len(loaded) : len(loaded) + count]:
                 source, dtype = sources[key]
-                loaded[key] = stream_pool.tile([P, source.shape[1]], dtype, name="slot", align_bytes=64)
+                if key in lent:
+                    loaded[key] = keep.tile([P, source.shape[1]], dtype, name=lent[key], align_bytes=64)
+                else:
+                    loaded[key] = stream_pool.tile([P, source.shape[1]], dtype, name="slot", align_bytes=64)
                 nc.sync.dma_start(loaded[key][:], source)
 
         def load_scale_rows(tile, scales):
             for q in range(QUADRANTS):
-                nc.sync.dma_start(
+                nc.gpsimd.dma_start(
                     tile[32 * q : 32 * q + K_PASSES * SCALE_ROWS, :].bitcast(I32),
                     scales[:, SCALE_ROWS * q : SCALE_ROWS * (q + 1), :].bitcast(I32),
                 )
@@ -98,19 +101,18 @@ def tile_list_lattice_flow_adjoint_kernel(
         w1_rows = keep.tile([P, H], U8, name="w1_rows", align_bytes=64)
         v_plane1 = keep.tile([P, S], U8, name="v_plane1", align_bytes=64)
         w1_plane1 = keep.tile([P, H], U8, name="w1_plane1", align_bytes=64)
-        nc.gpsimd.memset(w1_rows[:].bitcast(I32), 0)
-        nc.gpsimd.memset(tab_rows[:].bitcast(I32), 0)
         load_next()
         amp_sb = keep.tile([P, ROW_BLOCKS, PACK], F32, name="amp_sb")
         nc.sync.dma_start(amp_sb[:], amp.rearrange("(b p t) -> p b t", p=P, t=PACK))
-        load_scale_rows(w1_rows, w1_scales)
-        load_next(STREAM_SLOTS - 1)
+        load_next(STREAM_SLOTS + len(lent) - 1)
         nc.sync.dma_start(idx2[:], offs2)
-        load_scale_rows(tab_rows, tab_scales)
 
         windows = [keep.tile([P, T2], F32, name=f"window{n}") for n in range(OUT_TILES)]
         for window in windows:
             nc.vector.memset(window[:], 0.0)
+        for rows, scales in ((w1_rows, w1_scales), (tab_rows, tab_scales)):
+            nc.vector.memset(rows[:].bitcast(I32), 0)
+            load_scale_rows(rows, scales)
 
         v_codes = [keep.tile([P, S], U32, name=f"v_codes{a}", align_bytes=64) for a in range(K_PASSES)]
         v_plane0 = keep.tile([P, S], U8, name="v_plane0", align_bytes=64)
@@ -126,47 +128,47 @@ def tile_list_lattice_flow_adjoint_kernel(
             if t == 0:
                 work[b] = phase_pool.tile([P, PACK, S], F32, name="work")
             nc.vector.tensor_copy(work[b][:, t, :], loaded["sT", b, t][:].indirect(idx[:]))
-            load_next()
+            if ("sT", b, t) not in lent:
+                load_next()
 
         def reorder_w1():
             for a in range(K_PASSES):
                 nc.vector.tensor_copy(
-                    w1_codes[a][:].rearrange("p (b t m i) -> p m b t i", t=PACK, b=ROW_BLOCKS, i=LINE),
-                    loaded["w1", a][:].bitcast(U32).rearrange("p (b m i t) -> p m b t i", t=PACK, b=ROW_BLOCKS, i=LINE),
+                    w1_codes[a][:].rearrange("p (b t m i) -> p b m t i", t=PACK, b=ROW_BLOCKS, i=LINE),
+                    loaded["w1", a][:].bitcast(U32).rearrange("p (b m i t) -> p b m t i", t=PACK, b=ROW_BLOCKS, i=LINE),
                 )
                 load_next()
+
+        def reorder_w1_scales():
             nc.vector.tensor_copy(
-                w1_plane0[:].rearrange("p (b t m) -> p t b m", t=PACK, m=P),
-                w1_rows[:].rearrange("p (b m t) -> p t b m", t=PACK, m=P),
+                w1_plane0[:].rearrange("p (b t m) -> p b t m", t=PACK, m=P),
+                w1_rows[:].rearrange("p (b m t) -> p b t m", t=PACK, m=P),
             )
             shift_second_pass(w1_plane1, w1_plane0)
 
-        def gather_table():
+        def gather_table_scales():
             nc.vector.tensor_copy(v_plane0[:], tab_rows[:].indirect(idx[:]))
             shift_second_pass(v_plane1, v_plane0)
+
+        def gather_table():
             for half in range(HALVES):
                 for a in range(K_PASSES):
                     words = loaded["tab", a][:].bitcast(U32)
                     nc.vector.tensor_copy(v_codes[a][:, entries(half)], words.indirect(idx[:, list_columns(half)]))
             load_next(K_PASSES)
 
-        def sines(minus_cos, sin, x):
-            nc.scalar.activation(minus_cos, x, ACT.Abs)
-            nc.scalar.activation(sin, x, ACT.Sin)
-            nc.scalar.activation(minus_cos, minus_cos, ACT.Sin, bias=-math.pi / 2)
-
-        def amp_sin_minus_one_on_scalar(sin, b, t):
-            nc.scalar.activation(sin, sin, ACT.Identity, scale=amp_sb[:, b, t : t + 1], bias=-1.0)
-
         def factor(b, t, columns):
             x = work[b][:, t, columns]
             minus_cos = small_pool.tile([P, columns.stop - columns.start], F32, name="small", align_bytes=64)
             sin = small_pool.tile([P, columns.stop - columns.start], F32, name="small", align_bytes=64)
-            sines(minus_cos[:], sin[:], x)
+            amp_column = amp_sb[:, b, t : t + 1]
+            nc.scalar.activation(minus_cos[:], x, ACT.Abs)
+            nc.scalar.activation(sin[:], x, ACT.Sin)
+            nc.scalar.activation(minus_cos[:], minus_cos[:], ACT.Sin, bias=-math.pi / 2)
             if (b, t) == slices[0]:
-                amp_sin_minus_one_on_scalar(sin[:], b, t)
+                nc.scalar.activation(sin[:], sin[:], ACT.Identity, scale=amp_column, bias=-1.0)
             else:
-                nc.gpsimd.tensor_scalar(sin[:], sin[:], amp_sb[:, b, t : t + 1], -1.0, ALU.mult, ALU.add)
+                nc.gpsimd.tensor_scalar(sin[:], sin[:], amp_column, -1.0, ALU.mult, ALU.add)
             nc.gpsimd.tensor_tensor(x, sin[:], minus_cos[:], ALU.mult)
 
         def first_product(b, half):
@@ -184,9 +186,9 @@ def tile_list_lattice_flow_adjoint_kernel(
                         stop=(a == K_PASSES - 1),
                     )
 
-        def times_h(unit_values, b, half):
+        def times_h(b, half):
             for t in range(PACK):
-                values = unit_values[:, t, :]
+                values = work[b][:, t, entries(half)]
                 nc.vector.tensor_tensor(values, values, h_banks[b, half, t][:], ALU.mult)
 
         def by_slice(values):
@@ -239,14 +241,19 @@ def tile_list_lattice_flow_adjoint_kernel(
         last = ROW_BLOCKS - 1
         for b, t in slices:
             gather_phases(b, t)
-            if (b, t) == slices[0]:
-                reorder_w1()
+            if ("sT", b, t) == max(lent):
+                reorder_w1_scales()
+                gather_table_scales()
             factor(b, t, entries(0) if b == last else slice(0, S))
+        reorder_w1()
         gather_table()
+        for t in range(PACK):
+            factor(last, t, entries(1))
 
-        for b, half in [(b, half) for half in range(HALVES) for b in range(ROW_BLOCKS)][:-1]:
+        units = [(b, half) for half in range(HALVES) for b in range(last)] + [(last, half) for half in range(HALVES)]
+        for b, half in units:
             first_product(b, half)
-            times_h(work[b][:, :, entries(half)], b, half)
+            times_h(b, half)
 
         for b in range(ROW_BLOCKS):
             round_z(b, 0)
@@ -257,25 +264,16 @@ def tile_list_lattice_flow_adjoint_kernel(
 
         second_product(0, 0)
         second_product(0, 1)
-        round_z(0, 1)
-        last_sin = work[last][:, :, entries(1)]
-        last_cos = stream_pool.tile([P, PACK, HALF], F32, name="slot", align_bytes=64)
-        sines(last_cos[:], last_sin, last_sin)
-        for t in range(PACK):
-            amp_sin_minus_one_on_scalar(last_sin[:, t, :], last, t)
-        round_z(1, 1)
+        for b in range(ROW_BLOCKS):
+            round_z(b, 1)
         second_product(0, 2)
         second_product(0, 3)
-        first_product(last, 1)
-        scatter(0, 0)
         quantise_z(0, 1)
-        scatter(0, 1)
-        times_h(last_cos[:], last, 1)
+        scatter(0, 0)
         quantise_z(1, 1)
-        z_bf16[last, 1] = small_pool.tile([P, HALF, PACK], BF16, name="small", align_bytes=64)
-        nc.vector.tensor_tensor(side_by_side(z_bf16[last, 1]), by_slice(last_cos[:]), by_slice(last_sin), ALU.mult)
-        scatter(0, 2)
+        scatter(0, 1)
         quantise_z(last, 1)
+        scatter(0, 2)
         scatter(0, 3)
 
         for n in range(OUT_TILES):

@@ -30,9 +30,23 @@ QUADRANTS = 4
 SCALE_ROWS = 4
 SHIFTED = 32 * (QUADRANTS - 1) + SCALE_ROWS
 LINE = 4
-STREAM_SLOTS = 6
-SMALL_SLOTS = 8
+GROUP = HALF // PACK
 H_BANKS, Y_BANKS = 6, 2
+KIB = 1024
+STREAM_SLOTS = 5
+SINE_SLOTS = 3
+
+WINDOWS_AT = 0
+WORK_AT = WINDOWS_AT + OUT_TILES * 8 * KIB
+STREAM_AT = WORK_AT + ROW_BLOCKS * 16 * KIB
+SINES_AT = STREAM_AT + STREAM_SLOTS * 8 * KIB
+LATE_AT = SINES_AT + SINE_SLOTS * 8 * KIB
+Z_AT = LATE_AT + 12 * KIB
+V_CODES_AT = Z_AT + ROW_BLOCKS * HALVES * 4 * KIB
+W1_CODES_AT = V_CODES_AT + K_PASSES * 4 * KIB
+EXTRA_AT = W1_CODES_AT + K_PASSES * 6 * KIB
+SCALES_AT = EXTRA_AT + 9 * KIB
+ROWS_AT = SCALES_AT + 5 * KIB
 
 
 def tile_list_lattice_flow_adjoint_kernel(
@@ -41,12 +55,11 @@ def tile_list_lattice_flow_adjoint_kernel(
     nc = tc.nc
     with ExitStack() as ctx:
         keep = ctx.enter_context(tc.tile_pool(name="keep", bufs=1))
-        stream_pool = ctx.enter_context(tc.tile_pool(name="stream", bufs=STREAM_SLOTS))
-        phase_pool = ctx.enter_context(tc.tile_pool(name="phases", bufs=ROW_BLOCKS))
-        y_pool = ctx.enter_context(tc.tile_pool(name="y", bufs=OUT_TILES))
-        small_pool = ctx.enter_context(tc.tile_pool(name="small", bufs=SMALL_SLOTS))
-        h_psum = ctx.enter_context(tc.psum_pool(name="h_psum", bufs=H_BANKS))
-        y_psum = ctx.enter_context(tc.psum_pool(name="y_psum", bufs=Y_BANKS))
+        sbuf = ctx.enter_context(tc.tile_pool(name="sbuf", bufs=1))
+        psum = ctx.enter_context(tc.psum_pool(name="psum", bufs=1))
+
+        def place(name, shape, dtype, at):
+            return sbuf.tile(shape, dtype, name=name, offset=at, align_bytes=64)
 
         def entries(half):
             return slice(half * HALF, (half + 1) * HALF)
@@ -57,6 +70,7 @@ def tile_list_lattice_flow_adjoint_kernel(
         idx = keep.tile([P, S // PER_COLUMN], U16, name="idx")
         nc.sync.dma_start(idx[:], offs)
         idx2 = keep.tile([P, S // PER_COLUMN], U16, name="idx2")
+        amp_sb = keep.tile([P, ROW_BLOCKS, PACK], F32, name="amp_sb")
 
         sT_slices = sT.rearrange("(b p t) c -> b t p c", p=P, t=PACK)
         w2_blocks = w2.rearrange("(b p t) n -> b p (t n)", p=P, t=PACK)
@@ -64,27 +78,21 @@ def tile_list_lattice_flow_adjoint_kernel(
         sources = {("sT", b, t): (sT_slices[b, t], F32) for b, t in slices}
         for a in range(K_PASSES):
             sources["w1", a] = (w1_words[a].rearrange("p c i -> p (c i)").bitcast(I32), I32)
+        for a in range(K_PASSES):
             sources["tab", a] = (tab_words[a].rearrange("p c i -> p (c i)").bitcast(I32), I32)
         for b in range(ROW_BLOCKS):
             sources["w2", b] = (w2_blocks[b], F32)
         sources["wgo",] = (wgo, F32)
-        to_load = (
-            [("sT",) + s for s in slices]
-            + [("w1", a) for a in range(K_PASSES)]
-            + [("tab", a) for a in range(K_PASSES)]
-            + [("w2", b) for b in range(ROW_BLOCKS)]
-            + [("wgo",)]
-        )
+        to_load = list(sources)
+        lent = ("sT", 1, 0)
+        ring = [key for key in to_load if key != lent]
         loaded = {}
-        lent = {("sT", 1, 0): "w1_plane0", ("sT", 1, 1): "v_plane0"}
 
         def load_next(count=1):
             for key in to_load[len(loaded) : len(loaded) + count]:
                 source, dtype = sources[key]
-                if key in lent:
-                    loaded[key] = keep.tile([P, source.shape[1]], dtype, name=lent[key], align_bytes=64)
-                else:
-                    loaded[key] = stream_pool.tile([P, source.shape[1]], dtype, name="slot", align_bytes=64)
+                at = EXTRA_AT if key == lent else STREAM_AT + ring.index(key) % STREAM_SLOTS * 8 * KIB
+                loaded[key] = place("load_" + "_".join(str(part) for part in key), [P, source.shape[1]], dtype, at)
                 nc.sync.dma_start(loaded[key][:], source)
 
         def load_scale_rows(tile, scales):
@@ -97,38 +105,33 @@ def tile_list_lattice_flow_adjoint_kernel(
         def shift_second_pass(plane, both):
             nc.sync.dma_start(plane[0:SHIFTED, :].bitcast(I32), both[SCALE_ROWS : SCALE_ROWS + SHIFTED, :].bitcast(I32))
 
-        tab_rows = keep.tile([P, T], U8, name="tab_rows", align_bytes=64)
-        w1_rows = keep.tile([P, H], U8, name="w1_rows", align_bytes=64)
-        v_plane1 = keep.tile([P, S], U8, name="v_plane1", align_bytes=64)
-        w1_plane1 = keep.tile([P, H], U8, name="w1_plane1", align_bytes=64)
+        tab_rows = place("tab_rows", [P, T], U8, ROWS_AT)
+        w1_rows = place("w1_rows", [P, H], U8, ROWS_AT + T)
+        v_plane1 = place("v_plane1", [P, S], U8, ROWS_AT + T + H)
+        w1_plane1 = place("w1_plane1", [P, H], U8, ROWS_AT + T + H + S)
         load_next()
-        amp_sb = keep.tile([P, ROW_BLOCKS, PACK], F32, name="amp_sb")
         nc.sync.dma_start(amp_sb[:], amp.rearrange("(b p t) -> p b t", p=P, t=PACK))
-        load_next(STREAM_SLOTS + len(lent) - 1)
+        load_next(STREAM_SLOTS)
         nc.sync.dma_start(idx2[:], offs2)
 
-        windows = [keep.tile([P, T2], F32, name=f"window{n}") for n in range(OUT_TILES)]
+        windows = [place(f"window{n}", [P, T2], F32, WINDOWS_AT + n * 8 * KIB) for n in range(OUT_TILES)]
         for window in windows:
             nc.vector.memset(window[:], 0.0)
         for rows, scales in ((w1_rows, w1_scales), (tab_rows, tab_scales)):
             nc.vector.memset(rows[:].bitcast(I32), 0)
             load_scale_rows(rows, scales)
 
-        v_codes = [keep.tile([P, S], U32, name=f"v_codes{a}", align_bytes=64) for a in range(K_PASSES)]
-        v_plane0 = keep.tile([P, S], U8, name="v_plane0", align_bytes=64)
-        v_planes = [v_plane0, v_plane1]
-        w1_codes = [keep.tile([P, H], U32, name=f"w1_codes{a}", align_bytes=64) for a in range(K_PASSES)]
-        w1_plane0 = keep.tile([P, H], U8, name="w1_plane0", align_bytes=64)
-        w1_planes = [w1_plane0, w1_plane1]
-
-        work, h_banks, z_bf16, z_codes, z_scales = {}, {}, {}, {}, {}
-        w2_bf16, w2_codes, w2_scales, y_sb = {}, {}, {}, {}
+        v_codes = [place(f"v_codes{a}", [P, S], U32, V_CODES_AT + a * 4 * KIB) for a in range(K_PASSES)]
+        w1_codes = [place(f"w1_codes{a}", [P, H], U32, W1_CODES_AT + a * 6 * KIB) for a in range(K_PASSES)]
+        v_planes = [place("v_plane0", [P, S], U8, EXTRA_AT), v_plane1]
+        w1_planes = [place("w1_plane0", [P, H], U8, EXTRA_AT + S), w1_plane1]
+        work = [place(f"work{b}", [P, PACK, S], F32, WORK_AT + b * 16 * KIB) for b in range(ROW_BLOCKS)]
+        z_bf16, codes, scales, w2_bf16, y_sb = {}, {}, {}, {}, {}
+        h_count, y_count, factor_count = [], [], []
 
         def gather_phases(b, t):
-            if t == 0:
-                work[b] = phase_pool.tile([P, PACK, S], F32, name="work")
             nc.vector.tensor_copy(work[b][:, t, :], loaded["sT", b, t][:].indirect(idx[:]))
-            if ("sT", b, t) not in lent:
+            if ("sT", b, t) != lent:
                 load_next()
 
         def reorder_w1():
@@ -139,16 +142,14 @@ def tile_list_lattice_flow_adjoint_kernel(
                 )
                 load_next()
 
-        def reorder_w1_scales():
+        def make_planes():
             nc.vector.tensor_copy(
-                w1_plane0[:].rearrange("p (b t m) -> p b t m", t=PACK, m=P),
+                w1_planes[0][:].rearrange("p (b t m) -> p b t m", t=PACK, m=P),
                 w1_rows[:].rearrange("p (b m t) -> p b t m", t=PACK, m=P),
             )
-            shift_second_pass(w1_plane1, w1_plane0)
-
-        def gather_table_scales():
-            nc.vector.tensor_copy(v_plane0[:], tab_rows[:].indirect(idx[:]))
-            shift_second_pass(v_plane1, v_plane0)
+            shift_second_pass(w1_planes[1], w1_planes[0])
+            nc.vector.tensor_copy(v_planes[0][:], tab_rows[:].indirect(idx[:]))
+            shift_second_pass(v_planes[1], v_planes[0])
 
         def gather_table():
             for half in range(HALVES):
@@ -157,77 +158,84 @@ def tile_list_lattice_flow_adjoint_kernel(
                     nc.vector.tensor_copy(v_codes[a][:, entries(half)], words.indirect(idx[:, list_columns(half)]))
             load_next(K_PASSES)
 
-        def factor(b, t, columns):
+        def factor(b, t, columns, sines):
             x = work[b][:, t, columns]
-            minus_cos = small_pool.tile([P, columns.stop - columns.start], F32, name="small", align_bytes=64)
-            sin = small_pool.tile([P, columns.stop - columns.start], F32, name="small", align_bytes=64)
+            minus_cos, sin = sines[:, 0, :], sines[:, 1, :]
             amp_column = amp_sb[:, b, t : t + 1]
-            nc.scalar.activation(minus_cos[:], x, ACT.Abs)
-            nc.scalar.activation(sin[:], x, ACT.Sin)
-            nc.scalar.activation(minus_cos[:], minus_cos[:], ACT.Sin, bias=-math.pi / 2)
+            nc.scalar.activation(minus_cos, x, ACT.Abs)
+            nc.scalar.activation(sin, x, ACT.Sin)
+            nc.scalar.activation(minus_cos, minus_cos, ACT.Sin, bias=-math.pi / 2)
             if (b, t) == slices[0]:
-                nc.scalar.activation(sin[:], sin[:], ACT.Identity, scale=amp_column, bias=-1.0)
+                nc.scalar.activation(sin, sin, ACT.Identity, scale=amp_column, bias=-1.0)
             else:
-                nc.gpsimd.tensor_scalar(sin[:], sin[:], amp_column, -1.0, ALU.mult, ALU.add)
-            nc.gpsimd.tensor_tensor(x, sin[:], minus_cos[:], ALU.mult)
+                nc.gpsimd.tensor_scalar(sin, sin, amp_column, -1.0, ALU.mult, ALU.add)
+            nc.gpsimd.tensor_tensor(x, sin, minus_cos, ALU.mult)
 
-        def first_product(b, half):
-            for t in range(PACK):
-                rows = slice(b * PASS + t * P, b * PASS + (t + 1) * P)
-                h_banks[b, half, t] = h_psum.tile([P, HALF], F32, name="h_bank")
-                for a in range(K_PASSES):
-                    nc.tensor.matmul_mx(
-                        h_banks[b, half, t][:],
-                        lhsT=w1_codes[a][:, rows].bitcast(E4M3X4),
-                        lhsT_scale=w1_planes[a][:, rows],
-                        rhs=v_codes[a][:, entries(half)].bitcast(E5M2X4),
-                        rhs_scale=v_planes[a][:, entries(half)],
-                        start=(a == 0),
-                        stop=(a == K_PASSES - 1),
-                    )
-
-        def times_h(b, half):
-            for t in range(PACK):
-                values = work[b][:, t, entries(half)]
-                nc.vector.tensor_tensor(values, values, h_banks[b, half, t][:], ALU.mult)
+        def factor_in_ring(b, t, columns):
+            count = len(factor_count)
+            factor_count.append(count)
+            at = SINES_AT + count % SINE_SLOTS * 8 * KIB
+            factor(b, t, columns, place(f"sines{count}", [P, 2, columns.stop - columns.start], F32, at))
 
         def by_slice(values):
             return values.rearrange("p t (c i) -> p c t i", i=LINE)
 
-        def side_by_side(tile):
-            return tile[:].rearrange("p (c i) t -> p c t i", i=LINE)
+        def side_by_side(values):
+            return values.rearrange("p (c i) t -> p c t i", i=LINE)
 
-        def round_z(b, half):
-            z_bf16[b, half] = small_pool.tile([P, HALF, PACK], BF16, name="small", align_bytes=64)
-            nc.scalar.copy(side_by_side(z_bf16[b, half]), by_slice(work[b][:, :, entries(half)]))
+        def z_at(b, half):
+            return Z_AT + (half * ROW_BLOCKS + b) * 4 * KIB
 
-        def round_w2(b, copy):
-            w2_bf16[b] = small_pool.tile([P, N, PACK], BF16, name="small", align_bytes=64)
-            copy(side_by_side(w2_bf16[b]), by_slice(loaded["w2", b][:].rearrange("p (t n) -> p t n", t=PACK)))
+        def make_z(b, half):
+            z_bf16[b, half] = place(f"z{b}{half}", [P, HALF, PACK], BF16, z_at(b, half))
+            for start in range(0, HALF, GROUP):
+                group = slice(half * HALF + start, half * HALF + start + GROUP)
+                h_bank = psum.tile([P, PACK, GROUP], F32, name=f"h_bank{len(h_count) % H_BANKS}")
+                h_count.append(start)
+                for t in range(PACK):
+                    rows = slice(b * PASS + t * P, b * PASS + (t + 1) * P)
+                    for a in range(K_PASSES):
+                        nc.tensor.matmul_mx(
+                            h_bank[:, t, :],
+                            lhsT=w1_codes[a][:, rows].bitcast(E4M3X4),
+                            lhsT_scale=w1_planes[a][:, rows],
+                            rhs=v_codes[a][:, group].bitcast(E5M2X4),
+                            rhs_scale=v_planes[a][:, group],
+                            start=(a == 0),
+                            stop=(a == K_PASSES - 1),
+                        )
+                nc.vector.tensor_tensor(
+                    side_by_side(z_bf16[b, half][:, start : start + GROUP, :]),
+                    by_slice(work[b][:, :, group]),
+                    by_slice(h_bank[:]),
+                    ALU.mult,
+                )
 
-        def quantise(source, name):
-            codes = keep.tile([P, source.shape[1]], U32, name=f"{name}_codes", align_bytes=64)
-            scales = keep.tile([P, source.shape[1]], U8, name=f"{name}_scales", align_bytes=64)
-            nc.vector.quantize_mx(codes[:].bitcast(E4M3X4), scales[:], source.rearrange("p c t -> p (c t)"))
-            return codes, scales
+        def round_w2(b, at):
+            w2_bf16[b] = place(f"w2_bf16_{b}", [P, N, PACK], BF16, at)
+            nc.scalar.copy(side_by_side(w2_bf16[b][:]), by_slice(loaded["w2", b][:].rearrange("p (t n) -> p t n", t=PACK)))
 
-        def quantise_z(b, half):
-            z_codes[b, half], z_scales[b, half] = quantise(z_bf16[b, half][:], f"z{b}{half}")
+        def quantise(key, source, at):
+            name = "_".join(str(part) for part in key)
+            codes[key] = place("codes_" + name, [P, HALF], U32, at)
+            scales[key] = place("scales_" + name, [P, HALF], U8, SCALES_AT + len(scales) * HALF)
+            nc.vector.quantize_mx(codes[key][:].bitcast(E4M3X4), scales[key][:], source[:].rearrange("p c t -> p (c t)"))
 
         def second_product(half, n):
             columns = slice(n * P, (n + 1) * P)
-            y_bank = y_psum.tile([P, HALF], F32, name="y_bank")
+            y_bank = psum.tile([P, HALF], F32, name=f"y_bank{len(y_count) % Y_BANKS}")
             for b in range(ROW_BLOCKS):
                 nc.tensor.matmul_mx(
                     y_bank[:],
-                    lhsT=w2_codes[b][:, columns].bitcast(E4M3X4),
-                    lhsT_scale=w2_scales[b][:, columns],
-                    rhs=z_codes[b, half][:].bitcast(E4M3X4),
-                    rhs_scale=z_scales[b, half][:],
+                    lhsT=codes["w2", b][:, columns].bitcast(E4M3X4),
+                    lhsT_scale=scales["w2", b][:, columns],
+                    rhs=codes["z", b, half][:].bitcast(E4M3X4),
+                    rhs_scale=scales["z", b, half][:],
                     start=(b == 0),
                     stop=(b == ROW_BLOCKS - 1),
                 )
-            y_sb[half, n] = y_pool.tile([P, HALF], F32, name="y_sb")
+            y_sb[half, n] = place(f"y{half}{n}", [P, HALF], F32, Z_AT + len(y_count) * 2 * KIB)
+            y_count.append(n)
             nc.scalar.copy(y_sb[half, n][:], y_bank[:])
 
         def scatter(half, n):
@@ -241,41 +249,32 @@ def tile_list_lattice_flow_adjoint_kernel(
         last = ROW_BLOCKS - 1
         for b, t in slices:
             gather_phases(b, t)
-            if ("sT", b, t) == max(lent):
-                reorder_w1_scales()
-                gather_table_scales()
-            factor(b, t, entries(0) if b == last else slice(0, S))
+            if ("sT", b, t) == lent:
+                make_planes()
+            factor_in_ring(b, t, entries(0) if b == last else slice(0, S))
         reorder_w1()
         gather_table()
-        for t in range(PACK):
-            factor(last, t, entries(1))
-
-        units = [(b, half) for half in range(HALVES) for b in range(last)] + [(last, half) for half in range(HALVES)]
-        for b, half in units:
-            first_product(b, half)
-            times_h(b, half)
-
+        factor_in_ring(last, 0, entries(1))
+        late = place("late_sines", [P, PACK - 1, 2, HALF], F32, LATE_AT)
+        for t in range(1, PACK):
+            factor(last, t, entries(1), late[:, t - 1])
         for b in range(ROW_BLOCKS):
-            round_z(b, 0)
-            round_w2(b, nc.scalar.copy if b == 0 else nc.vector.tensor_copy)
-        for b in range(ROW_BLOCKS):
-            quantise_z(b, 0)
-            w2_codes[b], w2_scales[b] = quantise(w2_bf16[b][:], f"w2{b}")
+            round_w2(b, SINES_AT + (len(factor_count) + b) % SINE_SLOTS * 8 * KIB)
 
-        second_product(0, 0)
-        second_product(0, 1)
+        for half in range(HALVES):
+            for b in range(last):
+                make_z(b, half)
+        make_z(last, 0)
         for b in range(ROW_BLOCKS):
-            round_z(b, 1)
-        second_product(0, 2)
-        second_product(0, 3)
-        quantise_z(0, 1)
-        scatter(0, 0)
-        quantise_z(1, 1)
-        scatter(0, 1)
-        quantise_z(last, 1)
-        scatter(0, 2)
-        scatter(0, 3)
-
+            quantise(("z", b, 0), z_bf16[b, 0], LATE_AT + b * 2 * KIB)
+        for b in range(ROW_BLOCKS):
+            quantise(("w2", b), w2_bf16[b], LATE_AT + (ROW_BLOCKS + b) * 2 * KIB)
+        make_z(last, 1)
+        for b in range(ROW_BLOCKS):
+            quantise(("z", b, 1), z_bf16[b, 1], EXTRA_AT + S + H + b * 2 * KIB)
+        for n in range(OUT_TILES):
+            second_product(0, n)
+            scatter(0, n)
         for n in range(OUT_TILES):
             second_product(1, n)
             scatter(1, n)

@@ -165,7 +165,7 @@ def tile_list_lattice_flow_adjoint_kernel(
             nc.scalar.activation(minus_cos, x, ACT.Abs)
             nc.scalar.activation(sin, x, ACT.Sin)
             nc.scalar.activation(minus_cos, minus_cos, ACT.Sin, bias=-math.pi / 2)
-            if (b, t) == slices[0]:
+            if t != PACK - 1 and t != 1 or (b, t) == (0, 1):
                 nc.scalar.activation(sin, sin, ACT.Identity, scale=amp_column, bias=-1.0)
             else:
                 nc.gpsimd.tensor_scalar(sin, sin, amp_column, -1.0, ALU.mult, ALU.add)

@@ -32,6 +32,7 @@ SHIFTED = 32 * (QUADRANTS - 1) + SCALE_ROWS
 LINE = 4
 GROUP = HALF // PACK
 H_BANKS, Y_BANKS = 6, 2
+PAIR = 2
 KIB = 1024
 STREAM_SLOTS = 5
 SINE_SLOTS = 3
@@ -40,8 +41,9 @@ WINDOWS_AT = 0
 WORK_AT = WINDOWS_AT + OUT_TILES * 8 * KIB
 STREAM_AT = WORK_AT + ROW_BLOCKS * 16 * KIB
 SINES_AT = STREAM_AT + STREAM_SLOTS * 8 * KIB
-LATE_AT = SINES_AT + SINE_SLOTS * 8 * KIB
-Z_AT = LATE_AT + 12 * KIB
+LATE_AT = SINES_AT + 12 * KIB
+W2_AT = SINES_AT + SINE_SLOTS * 8 * KIB
+Z_AT = W2_AT + 12 * KIB
 V_CODES_AT = Z_AT + ROW_BLOCKS * HALVES * 4 * KIB
 W1_CODES_AT = V_CODES_AT + K_PASSES * 4 * KIB
 EXTRA_AT = W1_CODES_AT + K_PASSES * 6 * KIB
@@ -84,7 +86,7 @@ def tile_list_lattice_flow_adjoint_kernel(
             sources["w2", b] = (w2_blocks[b], F32)
         sources["wgo",] = (wgo, F32)
         to_load = list(sources)
-        lent = ("sT", 1, 0)
+        lent = ("sT", 1, 1)
         ring = [key for key in to_load if key != lent]
         loaded = {}
 
@@ -97,7 +99,7 @@ def tile_list_lattice_flow_adjoint_kernel(
 
         def load_scale_rows(tile, scales):
             for q in range(QUADRANTS):
-                nc.gpsimd.dma_start(
+                nc.sync.dma_start(
                     tile[32 * q : 32 * q + K_PASSES * SCALE_ROWS, :].bitcast(I32),
                     scales[:, SCALE_ROWS * q : SCALE_ROWS * (q + 1), :].bitcast(I32),
                 )
@@ -115,11 +117,11 @@ def tile_list_lattice_flow_adjoint_kernel(
         nc.sync.dma_start(idx2[:], offs2)
 
         windows = [place(f"window{n}", [P, T2], F32, WINDOWS_AT + n * 8 * KIB) for n in range(OUT_TILES)]
-        for window in windows:
-            nc.vector.memset(window[:], 0.0)
         for rows, scales in ((w1_rows, w1_scales), (tab_rows, tab_scales)):
             nc.vector.memset(rows[:].bitcast(I32), 0)
             load_scale_rows(rows, scales)
+        for window in windows:
+            nc.vector.memset(window[:], 0.0)
 
         v_codes = [place(f"v_codes{a}", [P, S], U32, V_CODES_AT + a * 4 * KIB) for a in range(K_PASSES)]
         w1_codes = [place(f"w1_codes{a}", [P, H], U32, W1_CODES_AT + a * 6 * KIB) for a in range(K_PASSES)]
@@ -162,10 +164,10 @@ def tile_list_lattice_flow_adjoint_kernel(
             x = work[b][:, t, columns]
             minus_cos, sin = sines[:, 0, :], sines[:, 1, :]
             amp_column = amp_sb[:, b, t : t + 1]
-            nc.scalar.activation(minus_cos, x, ACT.Abs)
             nc.scalar.activation(sin, x, ACT.Sin)
+            nc.scalar.activation(minus_cos, x, ACT.Abs)
             nc.scalar.activation(minus_cos, minus_cos, ACT.Sin, bias=-math.pi / 2)
-            if t != PACK - 1 and t != 1 or (b, t) == (0, 1):
+            if t == 1:
                 nc.scalar.activation(sin, sin, ACT.Identity, scale=amp_column, bias=-1.0)
             else:
                 nc.gpsimd.tensor_scalar(sin, sin, amp_column, -1.0, ALU.mult, ALU.add)
@@ -174,14 +176,15 @@ def tile_list_lattice_flow_adjoint_kernel(
         def factor_in_ring(b, t, columns):
             count = len(factor_count)
             factor_count.append(count)
-            at = SINES_AT + count % SINE_SLOTS * 8 * KIB
+            whole = min(count, (ROW_BLOCKS - 1) * PACK)
+            at = SINES_AT + (whole * 8 + (count - whole) * 4) % (SINE_SLOTS * 8) * KIB
             factor(b, t, columns, place(f"sines{count}", [P, 2, columns.stop - columns.start], F32, at))
 
         def by_slice(values):
-            return values.rearrange("p t (c i) -> p c t i", i=LINE)
+            return values.rearrange("p t (c i) -> p c t i", i=PAIR)
 
         def side_by_side(values):
-            return values.rearrange("p (c i) t -> p c t i", i=LINE)
+            return values.rearrange("p (c i) t -> p c t i", i=PAIR)
 
         def z_at(b, half):
             return Z_AT + (half * ROW_BLOCKS + b) * 4 * KIB
@@ -254,12 +257,10 @@ def tile_list_lattice_flow_adjoint_kernel(
             factor_in_ring(b, t, entries(0) if b == last else slice(0, S))
         reorder_w1()
         gather_table()
-        factor_in_ring(last, 0, entries(1))
-        late = place("late_sines", [P, PACK - 1, 2, HALF], F32, LATE_AT)
-        for t in range(1, PACK):
-            factor(last, t, entries(1), late[:, t - 1])
+        for t in range(PACK):
+            factor_in_ring(last, t, entries(1))
         for b in range(ROW_BLOCKS):
-            round_w2(b, SINES_AT + (len(factor_count) + b) % SINE_SLOTS * 8 * KIB)
+            round_w2(b, W2_AT + b * 4 * KIB)
 
         for half in range(HALVES):
             for b in range(last):

@@ -121,7 +121,7 @@ def tile_list_lattice_flow_adjoint_kernel(
             nc.vector.memset(rows[:].bitcast(I32), 0)
             load_scale_rows(rows, scales)
         for window in windows:
-            nc.vector.memset(window[:], 0.0)
+            nc.gpsimd.memset(window[:], 0.0)
 
         v_codes = [place(f"v_codes{a}", [P, S], U32, V_CODES_AT + a * 4 * KIB) for a in range(K_PASSES)]
         w1_codes = [place(f"w1_codes{a}", [P, H], U32, W1_CODES_AT + a * 6 * KIB) for a in range(K_PASSES)]

@@ -42,8 +42,8 @@ WORK_AT = WINDOWS_AT + OUT_TILES * 8 * KIB
 STREAM_AT = WORK_AT + ROW_BLOCKS * 16 * KIB
 SINES_AT = STREAM_AT + STREAM_SLOTS * 8 * KIB
 LATE_AT = SINES_AT + 12 * KIB
-W2_AT = SINES_AT + SINE_SLOTS * 8 * KIB
-Z_AT = W2_AT + 12 * KIB
+W2_AT = SINES_AT
+Z_AT = SINES_AT + SINE_SLOTS * 8 * KIB
 V_CODES_AT = Z_AT + ROW_BLOCKS * HALVES * 4 * KIB
 W1_CODES_AT = V_CODES_AT + K_PASSES * 4 * KIB
 EXTRA_AT = W1_CODES_AT + K_PASSES * 6 * KIB
@@ -99,7 +99,7 @@ def tile_list_lattice_flow_adjoint_kernel(
 
         def load_scale_rows(tile, scales):
             for q in range(QUADRANTS):
-                nc.sync.dma_start(
+                nc.gpsimd.dma_start(
                     tile[32 * q : 32 * q + K_PASSES * SCALE_ROWS, :].bitcast(I32),
                     scales[:, SCALE_ROWS * q : SCALE_ROWS * (q + 1), :].bitcast(I32),
                 )
@@ -117,11 +117,11 @@ def tile_list_lattice_flow_adjoint_kernel(
         nc.sync.dma_start(idx2[:], offs2)
 
         windows = [place(f"window{n}", [P, T2], F32, WINDOWS_AT + n * 8 * KIB) for n in range(OUT_TILES)]
+        for window in windows:
+            nc.vector.memset(window[:], 0.0)
         for rows, scales in ((w1_rows, w1_scales), (tab_rows, tab_scales)):
             nc.vector.memset(rows[:].bitcast(I32), 0)
             load_scale_rows(rows, scales)
-        for window in windows:
-            nc.gpsimd.memset(window[:], 0.0)
 
         v_codes = [place(f"v_codes{a}", [P, S], U32, V_CODES_AT + a * 4 * KIB) for a in range(K_PASSES)]
         w1_codes = [place(f"w1_codes{a}", [P, H], U32, W1_CODES_AT + a * 6 * KIB) for a in range(K_PASSES)]
@@ -167,7 +167,7 @@ def tile_list_lattice_flow_adjoint_kernel(
             nc.scalar.activation(sin, x, ACT.Sin)
             nc.scalar.activation(minus_cos, x, ACT.Abs)
             nc.scalar.activation(minus_cos, minus_cos, ACT.Sin, bias=-math.pi / 2)
-            if t == 1:
+            if t == 1 or (b, t) == (0, 3):
                 nc.scalar.activation(sin, sin, ACT.Identity, scale=amp_column, bias=-1.0)
             else:
                 nc.gpsimd.tensor_scalar(sin, sin, amp_column, -1.0, ALU.mult, ALU.add)
@@ -216,7 +216,8 @@ def tile_list_lattice_flow_adjoint_kernel(
 
         def round_w2(b, at):
             w2_bf16[b] = place(f"w2_bf16_{b}", [P, N, PACK], BF16, at)
-            nc.scalar.copy(side_by_side(w2_bf16[b][:]), by_slice(loaded["w2", b][:].rearrange("p (t n) -> p t n", t=PACK)))
+            rounded, rows = side_by_side(w2_bf16[b][:]), by_slice(loaded["w2", b][:].rearrange("p (t n) -> p t n", t=PACK))
+            nc.scalar.copy(rounded, rows)
 
         def quantise(key, source, at):
             name = "_".join(str(part) for part in key)

@@ -78,8 +78,7 @@ def tile_list_lattice_flow_adjoint_kernel(
         w2_blocks = w2.rearrange("(b p t) n -> b p (t n)", p=P, t=PACK)
         slices = [(b, t) for b in range(ROW_BLOCKS) for t in range(PACK)]
         sources = {("sT", b, t): (sT_slices[b, t], F32) for b, t in slices}
-        for a in range(K_PASSES):
-            sources["w1", a] = (w1_words[a].rearrange("p c i -> p (c i)").bitcast(I32), I32)
+        sources["w1",] = (w1_words.rearrange("a p c i -> p a (c i)").bitcast(I32), I32)
         for a in range(K_PASSES):
             sources["tab", a] = (tab_words[a].rearrange("p c i -> p (c i)").bitcast(I32), I32)
         for b in range(ROW_BLOCKS):
@@ -88,18 +87,19 @@ def tile_list_lattice_flow_adjoint_kernel(
         to_load = list(sources)
         lent = ("sT", 1, 1)
         ring = [key for key in to_load if key != lent]
+        ring.insert(ring.index(("w1",)), ("w1",))
         loaded = {}
 
         def load_next(count=1):
             for key in to_load[len(loaded) : len(loaded) + count]:
                 source, dtype = sources[key]
                 at = EXTRA_AT if key == lent else STREAM_AT + ring.index(key) % STREAM_SLOTS * 8 * KIB
-                loaded[key] = place("load_" + "_".join(str(part) for part in key), [P, source.shape[1]], dtype, at)
+                loaded[key] = place("load_" + "_".join(str(part) for part in key), [P, *source.shape[1:]], dtype, at)
                 nc.sync.dma_start(loaded[key][:], source)
 
         def load_scale_rows(tile, scales):
             for q in range(QUADRANTS):
-                nc.gpsimd.dma_start(
+                nc.sync.dma_start(
                     tile[32 * q : 32 * q + K_PASSES * SCALE_ROWS, :].bitcast(I32),
                     scales[:, SCALE_ROWS * q : SCALE_ROWS * (q + 1), :].bitcast(I32),
                 )
@@ -117,14 +117,14 @@ def tile_list_lattice_flow_adjoint_kernel(
         nc.sync.dma_start(idx2[:], offs2)
 
         windows = [place(f"window{n}", [P, T2], F32, WINDOWS_AT + n * 8 * KIB) for n in range(OUT_TILES)]
-        for window in windows:
-            nc.vector.memset(window[:], 0.0)
         for rows, scales in ((w1_rows, w1_scales), (tab_rows, tab_scales)):
             nc.vector.memset(rows[:].bitcast(I32), 0)
             load_scale_rows(rows, scales)
+        for window in windows:
+            nc.vector.memset(window[:], 0.0)
 
         v_codes = [place(f"v_codes{a}", [P, S], U32, V_CODES_AT + a * 4 * KIB) for a in range(K_PASSES)]
-        w1_codes = [place(f"w1_codes{a}", [P, H], U32, W1_CODES_AT + a * 6 * KIB) for a in range(K_PASSES)]
+        w1_codes = place("w1_codes", [P, K_PASSES, H], U32, W1_CODES_AT)
         v_planes = [place("v_plane0", [P, S], U8, EXTRA_AT), v_plane1]
         w1_planes = [place("w1_plane0", [P, H], U8, EXTRA_AT + S), w1_plane1]
         work = [place(f"work{b}", [P, PACK, S], F32, WORK_AT + b * 16 * KIB) for b in range(ROW_BLOCKS)]
@@ -132,17 +132,21 @@ def tile_list_lattice_flow_adjoint_kernel(
         h_count, y_count, factor_count = [], [], []
 
         def gather_phases(b, t):
-            nc.vector.tensor_copy(work[b][:, t, :], loaded["sT", b, t][:].indirect(idx[:]))
-            if ("sT", b, t) != lent:
+            if (b, t) == slices[0]:
+                for half in range(HALVES):
+                    phases = loaded["sT", b, t][:].indirect(idx[:, list_columns(half)])
+                    nc.vector.tensor_copy(work[b][:, t, entries(half)], phases)
+            else:
+                nc.vector.tensor_copy(work[b][:, t, :], loaded["sT", b, t][:].indirect(idx[:]))
+            if ("sT", b, t) not in (lent, ("sT", 1, 3)):
                 load_next()
 
         def reorder_w1():
-            for a in range(K_PASSES):
-                nc.vector.tensor_copy(
-                    w1_codes[a][:].rearrange("p (b t m i) -> p b m t i", t=PACK, b=ROW_BLOCKS, i=LINE),
-                    loaded["w1", a][:].bitcast(U32).rearrange("p (b m i t) -> p b m t i", t=PACK, b=ROW_BLOCKS, i=LINE),
-                )
-                load_next()
+            nc.vector.tensor_copy(
+                w1_codes[:].rearrange("p a (b t m i) -> p (a b) m t i", t=PACK, b=ROW_BLOCKS, i=LINE),
+                loaded["w1",][:].bitcast(U32).rearrange("p a (b m i t) -> p (a b) m t i", t=PACK, b=ROW_BLOCKS, i=LINE),
+            )
+            load_next(2)
 
         def make_planes():
             nc.vector.tensor_copy(
@@ -174,6 +178,12 @@ def tile_list_lattice_flow_adjoint_kernel(
             nc.gpsimd.tensor_tensor(x, sin, minus_cos, ALU.mult)
 
         def factor_in_ring(b, t, columns):
+            if (b, t) == slices[0]:
+                first = place("sines_first", [P, 2, S], F32, SINES_AT)
+                for half in range(HALVES):
+                    factor(b, t, entries(half), first[:, :, entries(half)])
+                factor_count.append(0)
+                return
             count = len(factor_count)
             factor_count.append(count)
             whole = min(count, (ROW_BLOCKS - 1) * PACK)
@@ -200,7 +210,7 @@ def tile_list_lattice_flow_adjoint_kernel(
                     for a in range(K_PASSES):
                         nc.tensor.matmul_mx(
                             h_bank[:, t, :],
-                            lhsT=w1_codes[a][:, rows].bitcast(E4M3X4),
+                            lhsT=w1_codes[:, a, rows].bitcast(E4M3X4),
                             lhsT_scale=w1_planes[a][:, rows],
                             rhs=v_codes[a][:, group].bitcast(E5M2X4),
                             rhs_scale=v_planes[a][:, group],

@@ -33,15 +33,16 @@ LINE = 4
 GROUP = HALF // PACK
 H_BANKS, Y_BANKS = 6, 2
 PAIR = 2
+AMP_RUN = LINE * (PACK - 1) + 1
 KIB = 1024
 STREAM_SLOTS = 5
-SINE_SLOTS = 3
+SINE_SLOTS = 6
 
 WINDOWS_AT = 0
 WORK_AT = WINDOWS_AT + OUT_TILES * 8 * KIB
 STREAM_AT = WORK_AT + ROW_BLOCKS * 16 * KIB
 SINES_AT = STREAM_AT + STREAM_SLOTS * 8 * KIB
-LATE_AT = SINES_AT + 12 * KIB
+LATE_AT = SINES_AT + 36 * KIB
 W2_AT = SINES_AT
 Z_AT = SINES_AT + SINE_SLOTS * 8 * KIB
 V_CODES_AT = Z_AT + ROW_BLOCKS * HALVES * 4 * KIB
@@ -49,6 +50,7 @@ W1_CODES_AT = V_CODES_AT + K_PASSES * 4 * KIB
 EXTRA_AT = W1_CODES_AT + K_PASSES * 6 * KIB
 SCALES_AT = EXTRA_AT + 9 * KIB
 ROWS_AT = SCALES_AT + 5 * KIB
+W1_RAW_AT = Z_AT
 
 
 def tile_list_lattice_flow_adjoint_kernel(
@@ -72,30 +74,43 @@ def tile_list_lattice_flow_adjoint_kernel(
         idx = keep.tile([P, S // PER_COLUMN], U16, name="idx")
         nc.sync.dma_start(idx[:], offs)
         idx2 = keep.tile([P, S // PER_COLUMN], U16, name="idx2")
-        amp_sb = keep.tile([P, ROW_BLOCKS, PACK], F32, name="amp_sb")
+        amp_sb = keep.tile([P, ROW_BLOCKS, PACK * LINE], F32, name="amp_sb")
 
-        sT_slices = sT.rearrange("(b p t) c -> b t p c", p=P, t=PACK)
-        w2_blocks = w2.rearrange("(b p t) n -> b p (t n)", p=P, t=PACK)
+        sT_slices = sT.rearrange("(b m t i) c -> b t m i c", b=ROW_BLOCKS, t=PACK, i=LINE)
+        w2_blocks = w2.rearrange("(b m t i) n -> b t m i n", b=ROW_BLOCKS, t=PACK, i=LINE)
         slices = [(b, t) for b in range(ROW_BLOCKS) for t in range(PACK)]
         sources = {("sT", b, t): (sT_slices[b, t], F32) for b, t in slices}
-        sources["w1",] = (w1_words.rearrange("a p c i -> p a (c i)").bitcast(I32), I32)
+        for a in range(K_PASSES):
+            sources["w1", a] = (w1_words[a].rearrange("p c i -> p (c i)").bitcast(I32), I32)
         for a in range(K_PASSES):
             sources["tab", a] = (tab_words[a].rearrange("p c i -> p (c i)").bitcast(I32), I32)
         for b in range(ROW_BLOCKS):
             sources["w2", b] = (w2_blocks[b], F32)
         sources["wgo",] = (wgo, F32)
         to_load = list(sources)
+        for a in range(K_PASSES):
+            to_load.remove(("w1", a))
+            to_load.insert(to_load.index(("sT", 1, 2)), ("w1", a))
+        for a in range(K_PASSES):
+            to_load.remove(("tab", a))
+            to_load.insert(to_load.index(("sT", 2, 2)), ("tab", a))
         lent = ("sT", 1, 1)
-        ring = [key for key in to_load if key != lent]
-        ring.insert(ring.index(("w1",)), ("w1",))
+        ring = [key for key in to_load if key != lent and key[0] != "w1"]
+        own = {lent: EXTRA_AT, ("w1", 0): W1_RAW_AT, ("w1", 1): W1_RAW_AT + 6 * KIB}
         loaded = {}
 
         def load_next(count=1):
             for key in to_load[len(loaded) : len(loaded) + count]:
                 source, dtype = sources[key]
-                at = EXTRA_AT if key == lent else STREAM_AT + ring.index(key) % STREAM_SLOTS * 8 * KIB
-                loaded[key] = place("load_" + "_".join(str(part) for part in key), [P, *source.shape[1:]], dtype, at)
-                nc.sync.dma_start(loaded[key][:], source)
+                at = own[key] if key in own else STREAM_AT + ring.index(key) % STREAM_SLOTS * 8 * KIB
+                name = "load_" + "_".join(str(part) for part in key)
+                if key[0] == "w2":
+                    loaded[key] = place(name, [P, PACK, N], dtype, at)
+                    for t in range(PACK):
+                        nc.sync.dma_start(loaded[key][:, t, :], source[t])
+                else:
+                    loaded[key] = place(name, [P, source.shape[-1]], dtype, at)
+                    nc.sync.dma_start(loaded[key][:], source)
 
         def load_scale_rows(tile, scales):
             for q in range(QUADRANTS):
@@ -112,8 +127,10 @@ def tile_list_lattice_flow_adjoint_kernel(
         v_plane1 = place("v_plane1", [P, S], U8, ROWS_AT + T + H)
         w1_plane1 = place("w1_plane1", [P, H], U8, ROWS_AT + T + H + S)
         load_next()
-        nc.sync.dma_start(amp_sb[:], amp.rearrange("(b p t) -> p b t", p=P, t=PACK))
-        load_next(STREAM_SLOTS)
+        amp_runs = amp.rearrange("(b m e) -> m b e", b=ROW_BLOCKS, e=PACK * LINE)
+        for i in range(LINE):
+            nc.sync.dma_start(amp_sb[i:P:LINE, :, 0:AMP_RUN], amp_runs[:, :, i : i + AMP_RUN])
+        load_next(STREAM_SLOTS + K_PASSES)
         nc.sync.dma_start(idx2[:], offs2)
 
         windows = [place(f"window{n}", [P, T2], F32, WINDOWS_AT + n * 8 * KIB) for n in range(OUT_TILES)]
@@ -127,31 +144,42 @@ def tile_list_lattice_flow_adjoint_kernel(
         w1_codes = place("w1_codes", [P, K_PASSES, H], U32, W1_CODES_AT)
         v_planes = [place("v_plane0", [P, S], U8, EXTRA_AT), v_plane1]
         w1_planes = [place("w1_plane0", [P, H], U8, EXTRA_AT + S), w1_plane1]
-        work = [place(f"work{b}", [P, PACK, S], F32, WORK_AT + b * 16 * KIB) for b in range(ROW_BLOCKS)]
+        last = ROW_BLOCKS - 1
+        work = [place(f"work{b}", [P, PACK, S], F32, WORK_AT + b * 16 * KIB) for b in range(last)]
+        def last_work_at(half):
+            return WORK_AT + (last * 16 + half * 8) * KIB
+
+        last_work = [place(f"last_work{half}", [P, PACK, HALF], F32, last_work_at(half)) for half in range(HALVES)]
+
+        def work_view(b, rows, columns):
+            if b < last:
+                return work[b][:, rows, columns]
+            half = columns.start // HALF
+            return last_work[half][:, rows, columns.start - half * HALF : columns.stop - half * HALF]
+
         z_bf16, codes, scales, w2_bf16, y_sb = {}, {}, {}, {}, {}
-        h_count, y_count, factor_count = [], [], []
+        h_count, y_count = [], []
 
         def gather_phases(b, t):
-            if (b, t) == slices[0]:
+            if (b, t) == slices[0] or b == last:
                 for half in range(HALVES):
                     phases = loaded["sT", b, t][:].indirect(idx[:, list_columns(half)])
-                    nc.vector.tensor_copy(work[b][:, t, entries(half)], phases)
+                    nc.vector.tensor_copy(work_view(b, t, entries(half)), phases)
             else:
                 nc.vector.tensor_copy(work[b][:, t, :], loaded["sT", b, t][:].indirect(idx[:]))
-            if ("sT", b, t) not in (lent, ("sT", 1, 3)):
+            if ("sT", b, t) != lent:
                 load_next()
 
-        def reorder_w1():
-            nc.vector.tensor_copy(
-                w1_codes[:].rearrange("p a (b t m i) -> p (a b) m t i", t=PACK, b=ROW_BLOCKS, i=LINE),
-                loaded["w1",][:].bitcast(U32).rearrange("p a (b m i t) -> p (a b) m t i", t=PACK, b=ROW_BLOCKS, i=LINE),
+        def reorder_w1(a):
+            nc.gpsimd.tensor_copy(
+                w1_codes[:, a, :].rearrange("p (b t m i) -> p b t m i", t=PACK, b=ROW_BLOCKS, i=LINE),
+                loaded["w1", a][:].bitcast(U32).rearrange("p (b m t i) -> p b t m i", t=PACK, b=ROW_BLOCKS, i=LINE),
             )
-            load_next(2)
 
         def make_planes():
             nc.vector.tensor_copy(
-                w1_planes[0][:].rearrange("p (b t m) -> p b t m", t=PACK, m=P),
-                w1_rows[:].rearrange("p (b m t) -> p b t m", t=PACK, m=P),
+                w1_planes[0][:].bitcast(I32).rearrange("p (b t m i) -> p b m t i", t=PACK, b=ROW_BLOCKS, i=LINE),
+                w1_rows[:].bitcast(I32).rearrange("p (b m i t) -> p b m t i", t=PACK, b=ROW_BLOCKS, i=LINE),
             )
             shift_second_pass(w1_planes[1], w1_planes[0])
             nc.vector.tensor_copy(v_planes[0][:], tab_rows[:].indirect(idx[:]))
@@ -164,31 +192,22 @@ def tile_list_lattice_flow_adjoint_kernel(
                     nc.vector.tensor_copy(v_codes[a][:, entries(half)], words.indirect(idx[:, list_columns(half)]))
             load_next(K_PASSES)
 
-        def factor(b, t, columns, sines):
-            x = work[b][:, t, columns]
-            minus_cos, sin = sines[:, 0, :], sines[:, 1, :]
-            amp_column = amp_sb[:, b, t : t + 1]
+        def factor(b, first, count, columns, at):
+            x = work_view(b, slice(first, first + count), columns)
+            shape = [P, 2, count, columns.stop - columns.start]
+            sines = place(f"sines{b}{first}{columns.start}", shape, F32, SINES_AT + at * KIB)
+            minus_cos, sin = sines[:, 0], sines[:, 1]
             nc.scalar.activation(sin, x, ACT.Sin)
             nc.scalar.activation(minus_cos, x, ACT.Abs)
             nc.scalar.activation(minus_cos, minus_cos, ACT.Sin, bias=-math.pi / 2)
-            if t == 1 or (b, t) == (0, 3):
-                nc.scalar.activation(sin, sin, ACT.Identity, scale=amp_column, bias=-1.0)
-            else:
-                nc.gpsimd.tensor_scalar(sin, sin, amp_column, -1.0, ALU.mult, ALU.add)
+            for t in range(first, first + count):
+                amp_column = amp_sb[:, b, LINE * t : LINE * t + 1]
+                one = sin[:, t - first]
+                if b == ROW_BLOCKS - 1 and t > 0:
+                    nc.scalar.activation(one, one, ACT.Identity, scale=amp_column, bias=-1.0)
+                else:
+                    nc.gpsimd.tensor_scalar(one, one, amp_column, -1.0, ALU.mult, ALU.add)
             nc.gpsimd.tensor_tensor(x, sin, minus_cos, ALU.mult)
-
-        def factor_in_ring(b, t, columns):
-            if (b, t) == slices[0]:
-                first = place("sines_first", [P, 2, S], F32, SINES_AT)
-                for half in range(HALVES):
-                    factor(b, t, entries(half), first[:, :, entries(half)])
-                factor_count.append(0)
-                return
-            count = len(factor_count)
-            factor_count.append(count)
-            whole = min(count, (ROW_BLOCKS - 1) * PACK)
-            at = SINES_AT + (whole * 8 + (count - whole) * 4) % (SINE_SLOTS * 8) * KIB
-            factor(b, t, columns, place(f"sines{count}", [P, 2, columns.stop - columns.start], F32, at))
 
         def by_slice(values):
             return values.rearrange("p t (c i) -> p c t i", i=PAIR)
@@ -219,20 +238,20 @@ def tile_list_lattice_flow_adjoint_kernel(
                         )
                 nc.vector.tensor_tensor(
                     side_by_side(z_bf16[b, half][:, start : start + GROUP, :]),
-                    by_slice(work[b][:, :, group]),
+                    by_slice(work_view(b, slice(0, PACK), group)),
                     by_slice(h_bank[:]),
                     ALU.mult,
                 )
 
         def round_w2(b, at):
             w2_bf16[b] = place(f"w2_bf16_{b}", [P, N, PACK], BF16, at)
-            rounded, rows = side_by_side(w2_bf16[b][:]), by_slice(loaded["w2", b][:].rearrange("p (t n) -> p t n", t=PACK))
+            rounded, rows = side_by_side(w2_bf16[b][:]), by_slice(loaded["w2", b][:])
             nc.scalar.copy(rounded, rows)
 
-        def quantise(key, source, at):
+        def quantise(key, source, at, scales_at):
             name = "_".join(str(part) for part in key)
             codes[key] = place("codes_" + name, [P, HALF], U32, at)
-            scales[key] = place("scales_" + name, [P, HALF], U8, SCALES_AT + len(scales) * HALF)
+            scales[key] = place("scales_" + name, [P, HALF], U8, scales_at + len(scales) * HALF)
             nc.vector.quantize_mx(codes[key][:].bitcast(E4M3X4), scales[key][:], source[:].rearrange("p c t -> p (c t)"))
 
         def second_product(half, n):
@@ -260,30 +279,40 @@ def tile_list_lattice_flow_adjoint_kernel(
                 ALU.mult,
             )
 
-        last = ROW_BLOCKS - 1
         for b, t in slices:
             gather_phases(b, t)
             if ("sT", b, t) == lent:
                 make_planes()
-            factor_in_ring(b, t, entries(0) if b == last else slice(0, S))
-        reorder_w1()
-        gather_table()
-        for t in range(PACK):
-            factor_in_ring(last, t, entries(1))
+            if (b, t) == (last, 1):
+                gather_table()
+            if (b, t) == (1, 0):
+                for a in range(K_PASSES):
+                    reorder_w1(a)
+            if (b, t) == (0, 0):
+                for half in range(HALVES):
+                    factor(b, t, 1, entries(half), 4 * half)
+            elif b == 0:
+                factor(b, t, 1, slice(0, S), 8 * t)
+            elif t % 2 == 1 and b < last:
+                factor(b, t - 1, 2, slice(0, S), 16 * ((2 * b + t // 2) % 3))
+            elif t % 2 == 1:
+                factor(b, t - 1, 2, entries(0), 16 + 4 * (t - 1))
+        for t in range(0, PACK, 2):
+            factor(last, t, 2, entries(1), 32 + 4 * t)
         for b in range(ROW_BLOCKS):
             round_w2(b, W2_AT + b * 4 * KIB)
 
-        for half in range(HALVES):
-            for b in range(last):
+        for b in range(last):
+            for half in range(HALVES):
                 make_z(b, half)
         make_z(last, 0)
         for b in range(ROW_BLOCKS):
-            quantise(("z", b, 0), z_bf16[b, 0], LATE_AT + b * 2 * KIB)
+            quantise(("z", b, 0), z_bf16[b, 0], LATE_AT + b * 2 * KIB, last_work_at(0))
         for b in range(ROW_BLOCKS):
-            quantise(("w2", b), w2_bf16[b], LATE_AT + (ROW_BLOCKS + b) * 2 * KIB)
+            quantise(("w2", b), w2_bf16[b], LATE_AT + (ROW_BLOCKS + b) * 2 * KIB, last_work_at(0))
         make_z(last, 1)
         for b in range(ROW_BLOCKS):
-            quantise(("z", b, 1), z_bf16[b, 1], EXTRA_AT + S + H + b * 2 * KIB)
+            quantise(("z", b, 1), z_bf16[b, 1], EXTRA_AT + S + H + b * 2 * KIB, last_work_at(1))
         for n in range(OUT_TILES):
             second_product(0, n)
             scatter(0, n)

@@ -43,14 +43,13 @@ WORK_AT = WINDOWS_AT + OUT_TILES * 8 * KIB
 STREAM_AT = WORK_AT + ROW_BLOCKS * 16 * KIB
 SINES_AT = STREAM_AT + STREAM_SLOTS * 8 * KIB
 LATE_AT = SINES_AT + 36 * KIB
-W2_AT = SINES_AT
+W2_AT = SINES_AT + 16 * KIB
 Z_AT = SINES_AT + SINE_SLOTS * 8 * KIB
 V_CODES_AT = Z_AT + ROW_BLOCKS * HALVES * 4 * KIB
 W1_CODES_AT = V_CODES_AT + K_PASSES * 4 * KIB
 EXTRA_AT = W1_CODES_AT + K_PASSES * 6 * KIB
 SCALES_AT = EXTRA_AT + 9 * KIB
 ROWS_AT = SCALES_AT + 5 * KIB
-W1_RAW_AT = Z_AT
 
 
 def tile_list_lattice_flow_adjoint_kernel(
@@ -88,21 +87,18 @@ def tile_list_lattice_flow_adjoint_kernel(
             sources["w2", b] = (w2_blocks[b], F32)
         sources["wgo",] = (wgo, F32)
         to_load = list(sources)
-        for a in range(K_PASSES):
-            to_load.remove(("w1", a))
-            to_load.insert(to_load.index(("sT", 1, 2)), ("w1", a))
-        for a in range(K_PASSES):
-            to_load.remove(("tab", a))
-            to_load.insert(to_load.index(("sT", 2, 2)), ("tab", a))
+        for name in ("w1", "tab"):
+            for a in range(K_PASSES):
+                to_load.remove((name, a))
+                to_load.insert(to_load.index(("sT", 2, 2)), (name, a))
         lent = ("sT", 1, 1)
-        ring = [key for key in to_load if key != lent and key[0] != "w1"]
-        own = {lent: EXTRA_AT, ("w1", 0): W1_RAW_AT, ("w1", 1): W1_RAW_AT + 6 * KIB}
+        ring = [key for key in to_load if key != lent]
         loaded = {}
 
         def load_next(count=1):
             for key in to_load[len(loaded) : len(loaded) + count]:
                 source, dtype = sources[key]
-                at = own[key] if key in own else STREAM_AT + ring.index(key) % STREAM_SLOTS * 8 * KIB
+                at = EXTRA_AT if key == lent else STREAM_AT + ring.index(key) % STREAM_SLOTS * 8 * KIB
                 name = "load_" + "_".join(str(part) for part in key)
                 if key[0] == "w2":
                     loaded[key] = place(name, [P, PACK, N], dtype, at)
@@ -130,7 +126,7 @@ def tile_list_lattice_flow_adjoint_kernel(
         amp_runs = amp.rearrange("(b m e) -> m b e", b=ROW_BLOCKS, e=PACK * LINE)
         for i in range(LINE):
             nc.sync.dma_start(amp_sb[i:P:LINE, :, 0:AMP_RUN], amp_runs[:, :, i : i + AMP_RUN])
-        load_next(STREAM_SLOTS + K_PASSES)
+        load_next(STREAM_SLOTS)
         nc.sync.dma_start(idx2[:], offs2)
 
         windows = [place(f"window{n}", [P, T2], F32, WINDOWS_AT + n * 8 * KIB) for n in range(OUT_TILES)]
@@ -170,11 +166,13 @@ def tile_list_lattice_flow_adjoint_kernel(
             if ("sT", b, t) != lent:
                 load_next()
 
-        def reorder_w1(a):
-            nc.gpsimd.tensor_copy(
-                w1_codes[:, a, :].rearrange("p (b t m i) -> p b t m i", t=PACK, b=ROW_BLOCKS, i=LINE),
-                loaded["w1", a][:].bitcast(U32).rearrange("p (b m t i) -> p b t m i", t=PACK, b=ROW_BLOCKS, i=LINE),
-            )
+        def reorder_w1():
+            for a in range(K_PASSES):
+                nc.vector.tensor_copy(
+                    w1_codes[:, a, :].rearrange("p (b t m i) -> p b m t i", t=PACK, b=ROW_BLOCKS, i=LINE),
+                    loaded["w1", a][:].bitcast(U32).rearrange("p (b m t i) -> p b m t i", t=PACK, b=ROW_BLOCKS, i=LINE),
+                )
+                load_next()
 
         def make_planes():
             nc.vector.tensor_copy(
@@ -203,7 +201,7 @@ def tile_list_lattice_flow_adjoint_kernel(
             for t in range(first, first + count):
                 amp_column = amp_sb[:, b, LINE * t : LINE * t + 1]
                 one = sin[:, t - first]
-                if b == ROW_BLOCKS - 1 and t > 0:
+                if t == 1:
                     nc.scalar.activation(one, one, ACT.Identity, scale=amp_column, bias=-1.0)
                 else:
                     nc.gpsimd.tensor_scalar(one, one, amp_column, -1.0, ALU.mult, ALU.add)
@@ -216,6 +214,8 @@ def tile_list_lattice_flow_adjoint_kernel(
             return values.rearrange("p (c i) t -> p c t i", i=PAIR)
 
         def z_at(b, half):
+            if b == 0:
+                return STREAM_AT + (ring.index(("sT",) + slices[-1]) % STREAM_SLOTS * 8 + half * 4) * KIB
             return Z_AT + (half * ROW_BLOCKS + b) * 4 * KIB
 
         def make_z(b, half):
@@ -284,10 +284,8 @@ def tile_list_lattice_flow_adjoint_kernel(
             if ("sT", b, t) == lent:
                 make_planes()
             if (b, t) == (last, 1):
+                reorder_w1()
                 gather_table()
-            if (b, t) == (1, 0):
-                for a in range(K_PASSES):
-                    reorder_w1(a)
             if (b, t) == (0, 0):
                 for half in range(HALVES):
                     factor(b, t, 1, entries(half), 4 * half)

@@ -201,17 +201,17 @@ def tile_list_lattice_flow_adjoint_kernel(
             for t in range(first, first + count):
                 amp_column = amp_sb[:, b, LINE * t : LINE * t + 1]
                 one = sin[:, t - first]
-                if t == 1:
+                if t == 1 or (b == last and t > 0):
                     nc.scalar.activation(one, one, ACT.Identity, scale=amp_column, bias=-1.0)
                 else:
                     nc.gpsimd.tensor_scalar(one, one, amp_column, -1.0, ALU.mult, ALU.add)
             nc.gpsimd.tensor_tensor(x, sin, minus_cos, ALU.mult)
 
-        def by_slice(values):
-            return values.rearrange("p t (c i) -> p c t i", i=PAIR)
+        def by_slice(values, run=PAIR):
+            return values.rearrange("p t (c i) -> p c t i", i=run)
 
-        def side_by_side(values):
-            return values.rearrange("p (c i) t -> p c t i", i=PAIR)
+        def side_by_side(values, run=PAIR):
+            return values.rearrange("p (c i) t -> p c t i", i=run)
 
         def z_at(b, half):
             if b == 0:
@@ -245,7 +245,7 @@ def tile_list_lattice_flow_adjoint_kernel(
 
         def round_w2(b, at):
             w2_bf16[b] = place(f"w2_bf16_{b}", [P, N, PACK], BF16, at)
-            rounded, rows = side_by_side(w2_bf16[b][:]), by_slice(loaded["w2", b][:])
+            rounded, rows = side_by_side(w2_bf16[b][:], LINE), by_slice(loaded["w2", b][:], LINE)
             nc.scalar.copy(rounded, rows)
 
         def quantise(key, source, at, scales_at):

@@ -87,18 +87,20 @@ def tile_list_lattice_flow_adjoint_kernel(
             sources["w2", b] = (w2_blocks[b], F32)
         sources["wgo",] = (wgo, F32)
         to_load = list(sources)
-        for name in ("w1", "tab"):
-            for a in range(K_PASSES):
-                to_load.remove((name, a))
-                to_load.insert(to_load.index(("sT", 2, 2)), (name, a))
+        for key in (("w1", 0), ("tab", 0), ("tab", 1)):
+            to_load.remove(key)
+            to_load.insert(to_load.index(("sT", 2, 2)), key)
+        to_load.remove(("w1", 1))
+        to_load.insert(to_load.index(("sT", 1, 2)), ("w1", 1))
         lent = ("sT", 1, 1)
-        ring = [key for key in to_load if key != lent]
+        own = {lent: EXTRA_AT, ("w1", 1): Z_AT}
+        ring = [key for key in to_load if key not in own]
         loaded = {}
 
         def load_next(count=1):
             for key in to_load[len(loaded) : len(loaded) + count]:
                 source, dtype = sources[key]
-                at = EXTRA_AT if key == lent else STREAM_AT + ring.index(key) % STREAM_SLOTS * 8 * KIB
+                at = own[key] if key in own else STREAM_AT + ring.index(key) % STREAM_SLOTS * 8 * KIB
                 name = "load_" + "_".join(str(part) for part in key)
                 if key[0] == "w2":
                     loaded[key] = place(name, [P, PACK, N], dtype, at)
@@ -126,7 +128,7 @@ def tile_list_lattice_flow_adjoint_kernel(
         amp_runs = amp.rearrange("(b m e) -> m b e", b=ROW_BLOCKS, e=PACK * LINE)
         for i in range(LINE):
             nc.sync.dma_start(amp_sb[i:P:LINE, :, 0:AMP_RUN], amp_runs[:, :, i : i + AMP_RUN])
-        load_next(STREAM_SLOTS)
+        load_next(STREAM_SLOTS + 1)
         nc.sync.dma_start(idx2[:], offs2)
 
         windows = [place(f"window{n}", [P, T2], F32, WINDOWS_AT + n * 8 * KIB) for n in range(OUT_TILES)]
@@ -134,7 +136,7 @@ def tile_list_lattice_flow_adjoint_kernel(
             nc.vector.memset(rows[:].bitcast(I32), 0)
             load_scale_rows(rows, scales)
         for window in windows:
-            nc.vector.memset(window[:], 0.0)
+            nc.vector.memset(window[:].bitcast(I32), 0)
 
         v_codes = [place(f"v_codes{a}", [P, S], U32, V_CODES_AT + a * 4 * KIB) for a in range(K_PASSES)]
         w1_codes = place("w1_codes", [P, K_PASSES, H], U32, W1_CODES_AT)
@@ -166,13 +168,11 @@ def tile_list_lattice_flow_adjoint_kernel(
             if ("sT", b, t) != lent:
                 load_next()
 
-        def reorder_w1():
-            for a in range(K_PASSES):
-                nc.vector.tensor_copy(
-                    w1_codes[:, a, :].rearrange("p (b t m i) -> p b m t i", t=PACK, b=ROW_BLOCKS, i=LINE),
-                    loaded["w1", a][:].bitcast(U32).rearrange("p (b m t i) -> p b m t i", t=PACK, b=ROW_BLOCKS, i=LINE),
-                )
-                load_next()
+        def reorder_w1(a, copy, walk):
+            copy(
+                w1_codes[:, a, :].rearrange("p (b t m i) -> " + walk, t=PACK, b=ROW_BLOCKS, i=LINE),
+                loaded["w1", a][:].bitcast(U32).rearrange("p (b m t i) -> " + walk, t=PACK, b=ROW_BLOCKS, i=LINE),
+            )
 
         def make_planes():
             nc.vector.tensor_copy(
@@ -195,8 +195,9 @@ def tile_list_lattice_flow_adjoint_kernel(
             shape = [P, 2, count, columns.stop - columns.start]
             sines = place(f"sines{b}{first}{columns.start}", shape, F32, SINES_AT + at * KIB)
             minus_cos, sin = sines[:, 0], sines[:, 1]
-            nc.scalar.activation(sin, x, ACT.Sin)
-            nc.scalar.activation(minus_cos, x, ACT.Abs)
+            steps = [(minus_cos, ACT.Abs), (sin, ACT.Sin)]
+            for result, function in reversed(steps) if (b, first, columns.start) == (0, 0, 0) else steps:
+                nc.scalar.activation(result, x, function)
             nc.scalar.activation(minus_cos, minus_cos, ACT.Sin, bias=-math.pi / 2)
             for t in range(first, first + count):
                 amp_column = amp_sb[:, b, LINE * t : LINE * t + 1]
@@ -284,8 +285,11 @@ def tile_list_lattice_flow_adjoint_kernel(
             if ("sT", b, t) == lent:
                 make_planes()
             if (b, t) == (last, 1):
-                reorder_w1()
+                reorder_w1(0, nc.vector.tensor_copy, "p b m t i")
+                load_next()
                 gather_table()
+            if (b, t) == (1, 0):
+                reorder_w1(1, nc.gpsimd.tensor_copy, "p b t m i")
             if (b, t) == (0, 0):
                 for half in range(HALVES):
                     factor(b, t, 1, entries(half), 4 * half)

@@ -31,25 +31,20 @@ SCALE_ROWS = 4
 SHIFTED = 32 * (QUADRANTS - 1) + SCALE_ROWS
 LINE = 4
 GROUP = HALF // PACK
-H_BANKS, Y_BANKS = 6, 2
 PAIR = 2
 AMP_RUN = LINE * (PACK - 1) + 1
 KIB = 1024
 STREAM_SLOTS = 5
-SINE_SLOTS = 6
 
 WINDOWS_AT = 0
-WORK_AT = WINDOWS_AT + OUT_TILES * 8 * KIB
+W1_RAW_AT = WINDOWS_AT + (OUT_TILES - 1) * 8 * KIB
+WORK_AT = W1_RAW_AT + 12 * KIB
 STREAM_AT = WORK_AT + ROW_BLOCKS * 16 * KIB
 SINES_AT = STREAM_AT + STREAM_SLOTS * 8 * KIB
-LATE_AT = SINES_AT + 36 * KIB
-W2_AT = SINES_AT + 16 * KIB
-Z_AT = SINES_AT + SINE_SLOTS * 8 * KIB
-V_CODES_AT = Z_AT + ROW_BLOCKS * HALVES * 4 * KIB
+LATE_AT = SINES_AT + 6 * 8 * KIB
+V_CODES_AT = LATE_AT + 20 * KIB
 W1_CODES_AT = V_CODES_AT + K_PASSES * 4 * KIB
-EXTRA_AT = W1_CODES_AT + K_PASSES * 6 * KIB
-SCALES_AT = EXTRA_AT + 9 * KIB
-ROWS_AT = SCALES_AT + 5 * KIB
+ROWS_AT = W1_CODES_AT + K_PASSES * 6 * KIB
 
 
 def tile_list_lattice_flow_adjoint_kernel(
@@ -70,48 +65,48 @@ def tile_list_lattice_flow_adjoint_kernel(
         def list_columns(half):
             return slice(half * HALF // PER_COLUMN, (half + 1) * HALF // PER_COLUMN)
 
+        def slot_at(slot):
+            return STREAM_AT + slot * 8 * KIB
+
         idx = keep.tile([P, S // PER_COLUMN], U16, name="idx")
-        nc.sync.dma_start(idx[:], offs)
         idx2 = keep.tile([P, S // PER_COLUMN], U16, name="idx2")
         amp_sb = keep.tile([P, ROW_BLOCKS, PACK * LINE], F32, name="amp_sb")
+        last = ROW_BLOCKS - 1
 
         sT_slices = sT.rearrange("(b m t i) c -> b t m i c", b=ROW_BLOCKS, t=PACK, i=LINE)
         w2_blocks = w2.rearrange("(b m t i) n -> b t m i n", b=ROW_BLOCKS, t=PACK, i=LINE)
         slices = [(b, t) for b in range(ROW_BLOCKS) for t in range(PACK)]
-        sources = {("sT", b, t): (sT_slices[b, t], F32) for b, t in slices}
+        lent = ("sT", 0, 3)
+        ring = [("sT",) + s for s in slices if ("sT",) + s != lent]
         for a in range(K_PASSES):
-            sources["w1", a] = (w1_words[a].rearrange("p c i -> p (c i)").bitcast(I32), I32)
-        for a in range(K_PASSES):
-            sources["tab", a] = (tab_words[a].rearrange("p c i -> p (c i)").bitcast(I32), I32)
-        for b in range(ROW_BLOCKS):
-            sources["w2", b] = (w2_blocks[b], F32)
-        sources["wgo",] = (wgo, F32)
-        to_load = list(sources)
-        for key in (("w1", 0), ("tab", 0), ("tab", 1)):
-            to_load.remove(key)
-            to_load.insert(to_load.index(("sT", 2, 2)), key)
-        to_load.remove(("w1", 1))
-        to_load.insert(to_load.index(("sT", 1, 2)), ("w1", 1))
-        lent = ("sT", 1, 1)
-        own = {lent: EXTRA_AT, ("w1", 1): Z_AT}
-        ring = [key for key in to_load if key not in own]
+            ring.insert(ring.index(("sT", last, 1)), ("tab", a))
+        ring.extend([("w2", b) for b in range(ROW_BLOCKS)] + [("wgo",)])
         loaded = {}
 
-        def load_next(count=1):
-            for key in to_load[len(loaded) : len(loaded) + count]:
-                source, dtype = sources[key]
-                at = own[key] if key in own else STREAM_AT + ring.index(key) % STREAM_SLOTS * 8 * KIB
-                name = "load_" + "_".join(str(part) for part in key)
-                if key[0] == "w2":
-                    loaded[key] = place(name, [P, PACK, N], dtype, at)
-                    for t in range(PACK):
-                        nc.sync.dma_start(loaded[key][:, t, :], source[t])
-                else:
-                    loaded[key] = place(name, [P, source.shape[-1]], dtype, at)
-                    nc.sync.dma_start(loaded[key][:], source)
+        def load(key):
+            name = "load_" + "_".join(str(part) for part in key)
+            at = W1_RAW_AT if key == lent else slot_at(ring.index(key) % STREAM_SLOTS)
+            if key[0] == "w2":
+                loaded[key] = place(name, [P, PACK, N], F32, at)
+                for t in range(PACK):
+                    nc.sync.dma_start(loaded[key][:, t, :], w2_blocks[key[1], t])
+            elif key[0] == "tab":
+                loaded[key] = place(name, [P, T], I32, at)
+                nc.sync.dma_start(loaded[key][:], tab_words[key[1]].rearrange("p c i -> p (c i)").bitcast(I32))
+            elif key[0] == "wgo":
+                loaded[key] = place(name, [P, S], F32, at)
+                nc.sync.dma_start(loaded[key][:], wgo)
+            else:
+                loaded[key] = place(name, [P, T], F32, at)
+                nc.sync.dma_start(loaded[key][:], sT_slices[key[1], key[2]])
 
-        def load_scale_rows(tile, scales):
-            for q in range(QUADRANTS):
+        def load_into_slot_of(key):
+            following = ring.index(key) + STREAM_SLOTS
+            if following < len(ring):
+                load(ring[following])
+
+        def load_scale_rows(tile, scales, quadrants):
+            for q in quadrants:
                 nc.sync.dma_start(
                     tile[32 * q : 32 * q + K_PASSES * SCALE_ROWS, :].bitcast(I32),
                     scales[:, SCALE_ROWS * q : SCALE_ROWS * (q + 1), :].bitcast(I32),
@@ -122,91 +117,111 @@ def tile_list_lattice_flow_adjoint_kernel(
 
         tab_rows = place("tab_rows", [P, T], U8, ROWS_AT)
         w1_rows = place("w1_rows", [P, H], U8, ROWS_AT + T)
-        v_plane1 = place("v_plane1", [P, S], U8, ROWS_AT + T + H)
-        w1_plane1 = place("w1_plane1", [P, H], U8, ROWS_AT + T + H + S)
-        load_next()
+        v_planes = [place(f"v_plane{a}", [P, S], U8, ROWS_AT + T + H + a * S) for a in range(K_PASSES)]
+        w1_planes = [place(f"w1_plane{a}", [P, H], U8, ROWS_AT + T + H + 2 * S + a * H) for a in range(K_PASSES)]
+        windows = {n: place(f"window{n}", [P, T2], F32, WINDOWS_AT + n * 8 * KIB) for n in range(OUT_TILES - 1)}
+        for rows in (tab_rows, w1_rows):
+            nc.vector.memset(rows[:].bitcast(I32), 0)
+        for n in range(OUT_TILES - 1):
+            nc.vector.memset(windows[n][:].bitcast(I32), 0)
+
+        nc.sync.dma_start(idx[:], offs)
+        load(("sT", 0, 0))
         amp_runs = amp.rearrange("(b m e) -> m b e", b=ROW_BLOCKS, e=PACK * LINE)
         for i in range(LINE):
             nc.sync.dma_start(amp_sb[i:P:LINE, :, 0:AMP_RUN], amp_runs[:, :, i : i + AMP_RUN])
-        load_next(STREAM_SLOTS + 1)
+        load(("sT", 0, 1))
+        load(("sT", 0, 2))
+        load_scale_rows(tab_rows, tab_scales, range(0, 2))
+        load(("sT", 0, 3))
+        load_scale_rows(tab_rows, tab_scales, range(2, 4))
+        load(("sT", 1, 0))
+        load_scale_rows(w1_rows, w1_scales, range(0, 2))
+        load(("sT", 1, 1))
+        load_scale_rows(w1_rows, w1_scales, range(2, 4))
         nc.sync.dma_start(idx2[:], offs2)
 
-        windows = [place(f"window{n}", [P, T2], F32, WINDOWS_AT + n * 8 * KIB) for n in range(OUT_TILES)]
-        for rows, scales in ((w1_rows, w1_scales), (tab_rows, tab_scales)):
-            nc.vector.memset(rows[:].bitcast(I32), 0)
-            load_scale_rows(rows, scales)
-        for window in windows:
-            nc.vector.memset(window[:].bitcast(I32), 0)
-
         v_codes = [place(f"v_codes{a}", [P, S], U32, V_CODES_AT + a * 4 * KIB) for a in range(K_PASSES)]
-        w1_codes = place("w1_codes", [P, K_PASSES, H], U32, W1_CODES_AT)
-        v_planes = [place("v_plane0", [P, S], U8, EXTRA_AT), v_plane1]
-        w1_planes = [place("w1_plane0", [P, H], U8, EXTRA_AT + S), w1_plane1]
-        last = ROW_BLOCKS - 1
-        work = [place(f"work{b}", [P, PACK, S], F32, WORK_AT + b * 16 * KIB) for b in range(last)]
-        def last_work_at(half):
-            return WORK_AT + (last * 16 + half * 8) * KIB
+        w1_codes = [place(f"w1_codes{a}", [P, H], U32, W1_CODES_AT + a * 6 * KIB) for a in range(K_PASSES)]
 
-        last_work = [place(f"last_work{half}", [P, PACK, HALF], F32, last_work_at(half)) for half in range(HALVES)]
+        def work_at(b, half):
+            return WORK_AT + (b * 16 + half * 8) * KIB
+
+        work = {0: place("work0", [P, PACK, S], F32, work_at(0, 0))}
+        for b in range(1, ROW_BLOCKS):
+            for half in range(HALVES):
+                work[b, half] = place(f"work{b}{half}", [P, PACK, HALF], F32, work_at(b, half))
 
         def work_view(b, rows, columns):
-            if b < last:
-                return work[b][:, rows, columns]
+            if b == 0:
+                return work[0][:, rows, columns]
             half = columns.start // HALF
-            return last_work[half][:, rows, columns.start - half * HALF : columns.stop - half * HALF]
+            return work[b, half][:, rows, columns.start - half * HALF : columns.stop - half * HALF]
 
-        z_bf16, codes, scales, w2_bf16, y_sb = {}, {}, {}, {}, {}
-        h_count, y_count = [], []
+        w1_raw, z_bf16, codes, scales, y_banks, y_sb, late = {}, {}, {}, {}, {}, {}, {}
 
         def gather_phases(b, t):
-            if (b, t) == slices[0] or b == last:
-                for half in range(HALVES):
-                    phases = loaded["sT", b, t][:].indirect(idx[:, list_columns(half)])
-                    nc.vector.tensor_copy(work_view(b, t, entries(half)), phases)
+            window = loaded["sT", b, t]
+            if b == 0 and t > 0:
+                nc.vector.tensor_copy(work[0][:, t, :], window[:].indirect(idx[:]))
             else:
-                nc.vector.tensor_copy(work[b][:, t, :], loaded["sT", b, t][:].indirect(idx[:]))
-            if ("sT", b, t) != lent:
-                load_next()
+                for half in range(HALVES):
+                    nc.vector.tensor_copy(
+                        work_view(b, t, entries(half)), window[:].indirect(idx[:, list_columns(half)])
+                    )
 
-        def reorder_w1(a, copy, walk):
-            copy(
-                w1_codes[:, a, :].rearrange("p (b t m i) -> " + walk, t=PACK, b=ROW_BLOCKS, i=LINE),
-                loaded["w1", a][:].bitcast(U32).rearrange("p (b m t i) -> " + walk, t=PACK, b=ROW_BLOCKS, i=LINE),
-            )
+        def load_w1():
+            for a in range(K_PASSES):
+                w1_raw[a] = place(f"w1_raw{a}", [P, H], I32, W1_RAW_AT + a * 6 * KIB)
+                nc.sync.dma_start(w1_raw[a][:], w1_words[a].rearrange("p c i -> p (c i)").bitcast(I32))
 
-        def make_planes():
-            nc.vector.tensor_copy(
-                w1_planes[0][:].bitcast(I32).rearrange("p (b t m i) -> p b m t i", t=PACK, b=ROW_BLOCKS, i=LINE),
-                w1_rows[:].bitcast(I32).rearrange("p (b m i t) -> p b m t i", t=PACK, b=ROW_BLOCKS, i=LINE),
+        def reorder_w1():
+            nc.gpsimd.tensor_copy(
+                w1_planes[0][:].bitcast(I32).rearrange("p (b t m) -> p b t m", t=PACK, b=ROW_BLOCKS),
+                w1_rows[:].bitcast(I32).rearrange("p (b m t) -> p b t m", t=PACK, b=ROW_BLOCKS),
             )
             shift_second_pass(w1_planes[1], w1_planes[0])
+            for a in range(K_PASSES):
+                nc.gpsimd.tensor_copy(
+                    w1_codes[a][:].rearrange("p (b t m i) -> p b t m i", t=PACK, b=ROW_BLOCKS, i=LINE),
+                    w1_raw[a][:].bitcast(U32).rearrange("p (b m t i) -> p b t m i", t=PACK, b=ROW_BLOCKS, i=LINE),
+                )
+
+        def gather_table_scales():
             nc.vector.tensor_copy(v_planes[0][:], tab_rows[:].indirect(idx[:]))
             shift_second_pass(v_planes[1], v_planes[0])
 
         def gather_table():
-            for half in range(HALVES):
-                for a in range(K_PASSES):
-                    words = loaded["tab", a][:].bitcast(U32)
-                    nc.vector.tensor_copy(v_codes[a][:, entries(half)], words.indirect(idx[:, list_columns(half)]))
-            load_next(K_PASSES)
+            for a in range(K_PASSES):
+                nc.vector.tensor_copy(v_codes[a][:], loaded["tab", a][:].bitcast(U32).indirect(idx[:]))
+                load_into_slot_of(("tab", a))
 
-        def factor(b, first, count, columns, at):
+        def factor(b, first, count, columns, at, on_scalar, result=None):
             x = work_view(b, slice(first, first + count), columns)
             shape = [P, 2, count, columns.stop - columns.start]
             sines = place(f"sines{b}{first}{columns.start}", shape, F32, SINES_AT + at * KIB)
             minus_cos, sin = sines[:, 0], sines[:, 1]
             steps = [(minus_cos, ACT.Abs), (sin, ACT.Sin)]
-            for result, function in reversed(steps) if (b, first, columns.start) == (0, 0, 0) else steps:
-                nc.scalar.activation(result, x, function)
+            for target, function in reversed(steps) if (b, first, columns.start) == (0, 0, 0) else steps:
+                nc.scalar.activation(target, x, function)
             nc.scalar.activation(minus_cos, minus_cos, ACT.Sin, bias=-math.pi / 2)
+            if result is None:
+                result = x
             for t in range(first, first + count):
                 amp_column = amp_sb[:, b, LINE * t : LINE * t + 1]
                 one = sin[:, t - first]
-                if t == 1 or (b == last and t > 0):
+                if t in on_scalar:
                     nc.scalar.activation(one, one, ACT.Identity, scale=amp_column, bias=-1.0)
-                else:
-                    nc.gpsimd.tensor_scalar(one, one, amp_column, -1.0, ALU.mult, ALU.add)
-            nc.gpsimd.tensor_tensor(x, sin, minus_cos, ALU.mult)
+            for t in range(first, first + count):
+                amp_column = amp_sb[:, b, LINE * t : LINE * t + 1]
+                if t not in on_scalar:
+                    nc.gpsimd.tensor_scalar(result[:, t - first], sin[:, t - first], amp_column, -1.0, ALU.mult, ALU.add)
+            for t in range(first, first + count):
+                if count == 1 or len(on_scalar) not in (0, count):
+                    source = sin if t in on_scalar else result
+                    nc.gpsimd.tensor_tensor(result[:, t - first], source[:, t - first], minus_cos[:, t - first], ALU.mult)
+            if count > 1 and len(on_scalar) in (0, count):
+                nc.gpsimd.tensor_tensor(result, sin if on_scalar else result, minus_cos, ALU.mult)
 
         def by_slice(values, run=PAIR):
             return values.rearrange("p t (c i) -> p c t i", i=run)
@@ -214,65 +229,66 @@ def tile_list_lattice_flow_adjoint_kernel(
         def side_by_side(values, run=PAIR):
             return values.rearrange("p (c i) t -> p c t i", i=run)
 
-        def z_at(b, half):
-            if b == 0:
-                return STREAM_AT + (ring.index(("sT",) + slices[-1]) % STREAM_SLOTS * 8 + half * 4) * KIB
-            return Z_AT + (half * ROW_BLOCKS + b) * 4 * KIB
-
-        def make_z(b, half):
-            z_bf16[b, half] = place(f"z{b}{half}", [P, HALF, PACK], BF16, z_at(b, half))
-            for start in range(0, HALF, GROUP):
+        def make_z(b, half, at, banks):
+            z_bf16[b, half] = place(f"z{b}{half}", [P, HALF, PACK], BF16, at)
+            for start, bank in zip(range(0, HALF, GROUP), banks):
                 group = slice(half * HALF + start, half * HALF + start + GROUP)
-                h_bank = psum.tile([P, PACK, GROUP], F32, name=f"h_bank{len(h_count) % H_BANKS}")
-                h_count.append(start)
+                h_bank = psum.tile([P, PACK, GROUP], F32, name=f"bank{bank}")
                 for t in range(PACK):
                     rows = slice(b * PASS + t * P, b * PASS + (t + 1) * P)
                     for a in range(K_PASSES):
                         nc.tensor.matmul_mx(
                             h_bank[:, t, :],
-                            lhsT=w1_codes[:, a, rows].bitcast(E4M3X4),
+                            lhsT=w1_codes[a][:, rows].bitcast(E4M3X4),
                             lhsT_scale=w1_planes[a][:, rows],
                             rhs=v_codes[a][:, group].bitcast(E5M2X4),
                             rhs_scale=v_planes[a][:, group],
                             start=(a == 0),
                             stop=(a == K_PASSES - 1),
                         )
+                if (b, half) in late:
+                    factors = late[b, half][:, :, start : start + GROUP]
+                else:
+                    factors = work_view(b, slice(0, PACK), group)
                 nc.vector.tensor_tensor(
                     side_by_side(z_bf16[b, half][:, start : start + GROUP, :]),
-                    by_slice(work_view(b, slice(0, PACK), group)),
+                    by_slice(factors),
                     by_slice(h_bank[:]),
                     ALU.mult,
                 )
 
-        def round_w2(b, at):
-            w2_bf16[b] = place(f"w2_bf16_{b}", [P, N, PACK], BF16, at)
-            rounded, rows = side_by_side(w2_bf16[b][:], LINE), by_slice(loaded["w2", b][:], LINE)
-            nc.scalar.copy(rounded, rows)
-
         def quantise(key, source, at, scales_at):
             name = "_".join(str(part) for part in key)
             codes[key] = place("codes_" + name, [P, HALF], U32, at)
-            scales[key] = place("scales_" + name, [P, HALF], U8, scales_at + len(scales) * HALF)
-            nc.vector.quantize_mx(codes[key][:].bitcast(E4M3X4), scales[key][:], source[:].rearrange("p c t -> p (c t)"))
+            scales[key] = place("scales_" + name, [P, HALF], U8, scales_at)
+            nc.vector.quantize_mx(codes[key][:].bitcast(E4M3X4), scales[key][:], source.rearrange("p c t -> p (c t)"))
 
-        def second_product(half, n):
-            columns = slice(n * P, (n + 1) * P)
-            y_bank = psum.tile([P, HALF], F32, name=f"y_bank{len(y_count) % Y_BANKS}")
+        def second_product(half, banks):
+            for n, bank in enumerate(banks):
+                y_banks[half, n] = psum.tile([P, HALF], F32, name=f"bank{bank}")
             for b in range(ROW_BLOCKS):
-                nc.tensor.matmul_mx(
-                    y_bank[:],
-                    lhsT=codes["w2", b][:, columns].bitcast(E4M3X4),
-                    lhsT_scale=scales["w2", b][:, columns],
-                    rhs=codes["z", b, half][:].bitcast(E4M3X4),
-                    rhs_scale=scales["z", b, half][:],
-                    start=(b == 0),
-                    stop=(b == ROW_BLOCKS - 1),
-                )
-            y_sb[half, n] = place(f"y{half}{n}", [P, HALF], F32, Z_AT + len(y_count) * 2 * KIB)
-            y_count.append(n)
-            nc.scalar.copy(y_sb[half, n][:], y_bank[:])
+                for n in range(OUT_TILES):
+                    columns = slice(n * P, (n + 1) * P)
+                    nc.tensor.matmul_mx(
+                        y_banks[half, n][:],
+                        lhsT=codes["w2", b][:, columns].bitcast(E4M3X4),
+                        lhsT_scale=scales["w2", b][:, columns],
+                        rhs=codes["z", b, half][:].bitcast(E4M3X4),
+                        rhs_scale=scales["z", b, half][:],
+                        start=(b == 0),
+                        stop=(b == last),
+                    )
 
-        def scatter(half, n):
+        def weigh(half, n, at):
+            y_sb[half, n] = place(f"y{half}{n}", [P, HALF], F32, at)
+            nc.vector.tensor_tensor(y_sb[half, n][:], y_banks[half, n][:], loaded["wgo",][:, entries(half)], ALU.mult)
+
+        def scatter_weighed(half, n):
+            nc.vector.tensor_copy(windows[n][:].indirect(idx2[:, list_columns(half)]), y_sb[half, n][:])
+
+        def copy_and_scatter(half, n, at):
+            y_sb[half, n] = place(f"y{half}{n}", [P, HALF], F32, at)
+            nc.scalar.copy(y_sb[half, n][:], y_banks[half, n][:])
             nc.vector.tensor_tensor(
                 windows[n][:].indirect(idx2[:, list_columns(half)]),
                 y_sb[half, n][:],
@@ -281,44 +297,64 @@ def tile_list_lattice_flow_adjoint_kernel(
             )
 
         for b, t in slices:
+            if (b, t) == (last, 1):
+                reorder_w1()
+                gather_table()
             gather_phases(b, t)
             if ("sT", b, t) == lent:
-                make_planes()
-            if (b, t) == (last, 1):
-                reorder_w1(0, nc.vector.tensor_copy, "p b m t i")
-                load_next()
-                gather_table()
-            if (b, t) == (1, 0):
-                reorder_w1(1, nc.gpsimd.tensor_copy, "p b t m i")
+                load_w1()
+                gather_table_scales()
+            else:
+                load_into_slot_of(("sT", b, t))
             if (b, t) == (0, 0):
                 for half in range(HALVES):
-                    factor(b, t, 1, entries(half), 4 * half)
+                    factor(b, t, 1, entries(half), 4 * half, ())
             elif b == 0:
-                factor(b, t, 1, slice(0, S), 8 * t)
-            elif t % 2 == 1 and b < last:
-                factor(b, t - 1, 2, slice(0, S), 16 * ((2 * b + t // 2) % 3))
+                factor(b, t, 1, slice(0, S), 8 * t, (3,))
+            elif b == last and t >= 2:
+                factor(b, t, 1, entries(0), 24 + 4 * (t - 2), (2, 3))
             elif t % 2 == 1:
-                factor(b, t - 1, 2, entries(0), 16 + 4 * (t - 1))
-        for t in range(0, PACK, 2):
-            factor(last, t, 2, entries(1), 32 + 4 * t)
-        for b in range(ROW_BLOCKS):
-            round_w2(b, W2_AT + b * 4 * KIB)
+                factor(b, t - 1, 2, entries(0), 8 * (2 * (b - 1) + t // 2), ())
+        windows[OUT_TILES - 1] = place("window3", [P, T2], F32, W1_RAW_AT)
+        nc.gpsimd.memset(windows[OUT_TILES - 1][:].bitcast(I32), 0)
 
-        for b in range(last):
-            for half in range(HALVES):
-                make_z(b, half)
-        make_z(last, 0)
+        w2_bf16 = place("w2_bf16", [P, ROW_BLOCKS, N, PACK], BF16, LATE_AT + 4 * KIB)
         for b in range(ROW_BLOCKS):
-            quantise(("z", b, 0), z_bf16[b, 0], LATE_AT + b * 2 * KIB, last_work_at(0))
+            if b == 1:
+                nc.gpsimd.tensor_scalar(
+                    w2_bf16[:, b], loaded["w2", b][:].rearrange("p t c -> p c t"), 1.0, 0.0, ALU.mult, ALU.add
+                )
+            else:
+                nc.scalar.copy(side_by_side(w2_bf16[:, b], LINE), by_slice(loaded["w2", b][:], LINE))
+
+        make_z(0, 0, slot_at(ring.index(("sT", last, PACK - 1)) % STREAM_SLOTS), range(0, 4))
+        make_z(1, 0, LATE_AT, range(4, 8))
+        make_z(2, 0, LATE_AT + 16 * KIB, range(0, 4))
         for b in range(ROW_BLOCKS):
-            quantise(("w2", b), w2_bf16[b], LATE_AT + (ROW_BLOCKS + b) * 2 * KIB, last_work_at(0))
-        make_z(last, 1)
+            quantise(("z", b, 0), z_bf16[b, 0][:], work_at(1, 0) + b * 2 * KIB, work_at(last, 0) + b * KIB)
+            w2_codes_at = work_at(1, 0) + 6 * KIB if b == 0 else work_at(last, 0) + (2 + 2 * b) * KIB
+            quantise(("w2", b), w2_bf16[:, b], w2_codes_at, work_at(last, 0) + b * KIB + HALF)
+        second_product(0, range(0, 4))
+        make_z(0, 1, LATE_AT + 8 * KIB, range(4, 8))
+
+        for b in range(1, ROW_BLOCKS):
+            late[b, 1] = place(f"late{b}", [P, PACK, HALF], F32, LATE_AT + (b - 1) * 12 * KIB)
+            for first in range(0, PACK, 2):
+                at = 32 + 4 * first if b == 1 else 4 * first
+                on_scalar = () if first == 0 else (first, first + 1)
+                factor(b, first, 2, entries(1), at, on_scalar, late[b, 1][:, first : first + 2])
+
+        for n in range(OUT_TILES - 1):
+            weigh(0, n, SINES_AT + (24 + 2 * n) * KIB)
+            if n != 1:
+                scatter_weighed(0, n // 2)
+        scatter_weighed(0, 2)
+        make_z(1, 1, SINES_AT + 16 * KIB, range(4, 8))
+        make_z(2, 1, SINES_AT + 20 * KIB, (0, 1, 2, 4))
         for b in range(ROW_BLOCKS):
-            quantise(("z", b, 1), z_bf16[b, 1], EXTRA_AT + S + H + b * 2 * KIB, last_work_at(1))
+            quantise(("z", b, 1), z_bf16[b, 1][:], work_at(1, 1) + b * 2 * KIB, LATE_AT + 12 * KIB + b * HALF)
+        second_product(1, (5, 6, 7, 0))
+        copy_and_scatter(0, OUT_TILES - 1, LATE_AT + 8 * KIB)
         for n in range(OUT_TILES):
-            second_product(0, n)
-            scatter(0, n)
-        for n in range(OUT_TILES):
-            second_product(1, n)
-            scatter(1, n)
+            copy_and_scatter(1, n, LATE_AT + n * 2 * KIB)
             nc.sync.dma_start(out[n * P : (n + 1) * P, :], windows[n][:])

@@ -37,11 +37,11 @@ KIB = 1024
 STREAM_SLOTS = 5
 
 WINDOWS_AT = 0
-W1_RAW_AT = WINDOWS_AT + (OUT_TILES - 1) * 8 * KIB
+W1_RAW_AT = WINDOWS_AT + OUT_TILES * 8 * KIB
 WORK_AT = W1_RAW_AT + 12 * KIB
 STREAM_AT = WORK_AT + ROW_BLOCKS * 16 * KIB
 SINES_AT = STREAM_AT + STREAM_SLOTS * 8 * KIB
-LATE_AT = SINES_AT + 6 * 8 * KIB
+LATE_AT = SINES_AT + 4 * 8 * KIB
 V_CODES_AT = LATE_AT + 20 * KIB
 W1_CODES_AT = V_CODES_AT + K_PASSES * 4 * KIB
 ROWS_AT = W1_CODES_AT + K_PASSES * 6 * KIB
@@ -76,16 +76,16 @@ def tile_list_lattice_flow_adjoint_kernel(
         sT_slices = sT.rearrange("(b m t i) c -> b t m i c", b=ROW_BLOCKS, t=PACK, i=LINE)
         w2_blocks = w2.rearrange("(b m t i) n -> b t m i n", b=ROW_BLOCKS, t=PACK, i=LINE)
         slices = [(b, t) for b in range(ROW_BLOCKS) for t in range(PACK)]
-        lent = ("sT", 0, 3)
-        ring = [("sT",) + s for s in slices if ("sT",) + s != lent]
+        ring = [("sT",) + s for s in slices]
         for a in range(K_PASSES):
             ring.insert(ring.index(("sT", last, 1)), ("tab", a))
-        ring.extend([("w2", b) for b in range(ROW_BLOCKS)] + [("wgo",)])
+        ring.insert(ring.index(("sT", last, 1)), ("w2", 0))
+        ring.extend([("w2", b) for b in range(1, ROW_BLOCKS)] + [("wgo",)])
         loaded = {}
 
         def load(key):
             name = "load_" + "_".join(str(part) for part in key)
-            at = W1_RAW_AT if key == lent else slot_at(ring.index(key) % STREAM_SLOTS)
+            at = slot_at(ring.index(key) % STREAM_SLOTS)
             if key[0] == "w2":
                 loaded[key] = place(name, [P, PACK, N], F32, at)
                 for t in range(PACK):
@@ -94,7 +94,7 @@ def tile_list_lattice_flow_adjoint_kernel(
                 loaded[key] = place(name, [P, T], I32, at)
                 nc.sync.dma_start(loaded[key][:], tab_words[key[1]].rearrange("p c i -> p (c i)").bitcast(I32))
             elif key[0] == "wgo":
-                loaded[key] = place(name, [P, S], F32, at)
+                loaded[key] = place(name, [P, S], F32, at + 4 * KIB)
                 nc.sync.dma_start(loaded[key][:], wgo)
             else:
                 loaded[key] = place(name, [P, T], F32, at)
@@ -119,10 +119,18 @@ def tile_list_lattice_flow_adjoint_kernel(
         w1_rows = place("w1_rows", [P, H], U8, ROWS_AT + T)
         v_planes = [place(f"v_plane{a}", [P, S], U8, ROWS_AT + T + H + a * S) for a in range(K_PASSES)]
         w1_planes = [place(f"w1_plane{a}", [P, H], U8, ROWS_AT + T + H + 2 * S + a * H) for a in range(K_PASSES)]
-        windows = {n: place(f"window{n}", [P, T2], F32, WINDOWS_AT + n * 8 * KIB) for n in range(OUT_TILES - 1)}
+        windows = {n: place(f"window{n}", [P, T2], F32, WINDOWS_AT + n * 8 * KIB) for n in range(OUT_TILES)}
         for rows in (tab_rows, w1_rows):
             nc.vector.memset(rows[:].bitcast(I32), 0)
-        for n in range(OUT_TILES - 1):
+        w1_codes = [place(f"w1_codes{a}", [P, H], U32, W1_CODES_AT + a * 6 * KIB) for a in range(K_PASSES)]
+        for a in range(K_PASSES):
+            w1_raw = place(f"w1_raw{a}", [P, H], I32, W1_RAW_AT + a * 6 * KIB)
+            nc.sync.dma_start(w1_raw[:], w1_words[a].rearrange("p c i -> p (c i)").bitcast(I32))
+            nc.vector.tensor_copy(
+                w1_codes[a][:].rearrange("p (b t m i) -> p t b m i", t=PACK, b=ROW_BLOCKS, i=LINE),
+                w1_raw[:].bitcast(U32).rearrange("p (b m t i) -> p t b m i", t=PACK, b=ROW_BLOCKS, i=LINE),
+            )
+        for n in range(OUT_TILES):
             nc.vector.memset(windows[n][:].bitcast(I32), 0)
 
         nc.sync.dma_start(idx[:], offs)
@@ -137,12 +145,10 @@ def tile_list_lattice_flow_adjoint_kernel(
         load_scale_rows(tab_rows, tab_scales, range(2, 4))
         load(("sT", 1, 0))
         load_scale_rows(w1_rows, w1_scales, range(0, 2))
-        load(("sT", 1, 1))
         load_scale_rows(w1_rows, w1_scales, range(2, 4))
         nc.sync.dma_start(idx2[:], offs2)
 
         v_codes = [place(f"v_codes{a}", [P, S], U32, V_CODES_AT + a * 4 * KIB) for a in range(K_PASSES)]
-        w1_codes = [place(f"w1_codes{a}", [P, H], U32, W1_CODES_AT + a * 6 * KIB) for a in range(K_PASSES)]
 
         def work_at(b, half):
             return WORK_AT + (b * 16 + half * 8) * KIB
@@ -158,7 +164,7 @@ def tile_list_lattice_flow_adjoint_kernel(
             half = columns.start // HALF
             return work[b, half][:, rows, columns.start - half * HALF : columns.stop - half * HALF]
 
-        w1_raw, z_bf16, codes, scales, y_banks, y_sb, late = {}, {}, {}, {}, {}, {}, {}
+        z_bf16, codes, scales, y_banks, y_sb, late = {}, {}, {}, {}, {}, {}
 
         def gather_phases(b, t):
             window = loaded["sT", b, t]
@@ -170,24 +176,12 @@ def tile_list_lattice_flow_adjoint_kernel(
                         work_view(b, t, entries(half)), window[:].indirect(idx[:, list_columns(half)])
                     )
 
-        def load_w1():
-            for a in range(K_PASSES):
-                w1_raw[a] = place(f"w1_raw{a}", [P, H], I32, W1_RAW_AT + a * 6 * KIB)
-                nc.sync.dma_start(w1_raw[a][:], w1_words[a].rearrange("p c i -> p (c i)").bitcast(I32))
-
-        def reorder_w1():
-            nc.gpsimd.tensor_copy(
-                w1_planes[0][:].bitcast(I32).rearrange("p (b t m) -> p b t m", t=PACK, b=ROW_BLOCKS),
-                w1_rows[:].bitcast(I32).rearrange("p (b m t) -> p b t m", t=PACK, b=ROW_BLOCKS),
+        def make_planes():
+            nc.vector.tensor_copy(
+                w1_planes[0][:].bitcast(I32).rearrange("p (b t m i) -> p b m t i", t=PACK, b=ROW_BLOCKS, i=LINE),
+                w1_rows[:].bitcast(I32).rearrange("p (b m i t) -> p b m t i", t=PACK, b=ROW_BLOCKS, i=LINE),
             )
             shift_second_pass(w1_planes[1], w1_planes[0])
-            for a in range(K_PASSES):
-                nc.gpsimd.tensor_copy(
-                    w1_codes[a][:].rearrange("p (b t m i) -> p b t m i", t=PACK, b=ROW_BLOCKS, i=LINE),
-                    w1_raw[a][:].bitcast(U32).rearrange("p (b m t i) -> p b t m i", t=PACK, b=ROW_BLOCKS, i=LINE),
-                )
-
-        def gather_table_scales():
             nc.vector.tensor_copy(v_planes[0][:], tab_rows[:].indirect(idx[:]))
             shift_second_pass(v_planes[1], v_planes[0])
 
@@ -199,7 +193,7 @@ def tile_list_lattice_flow_adjoint_kernel(
         def factor(b, first, count, columns, at, on_scalar, result=None):
             x = work_view(b, slice(first, first + count), columns)
             shape = [P, 2, count, columns.stop - columns.start]
-            sines = place(f"sines{b}{first}{columns.start}", shape, F32, SINES_AT + at * KIB)
+            sines = place(f"sines{b}{first}{columns.start}", shape, F32, at)
             minus_cos, sin = sines[:, 0], sines[:, 1]
             steps = [(minus_cos, ACT.Abs), (sin, ACT.Sin)]
             for target, function in reversed(steps) if (b, first, columns.start) == (0, 0, 0) else steps:
@@ -296,39 +290,35 @@ def tile_list_lattice_flow_adjoint_kernel(
                 ALU.mult,
             )
 
+        w2_bf16 = place("w2_bf16", [P, ROW_BLOCKS, N, PACK], BF16, LATE_AT + 4 * KIB)
+
+        def round_w2(b):
+            nc.scalar.copy(side_by_side(w2_bf16[:, b], LINE), by_slice(loaded["w2", b][:], LINE))
+
         for b, t in slices:
             if (b, t) == (last, 1):
-                reorder_w1()
                 gather_table()
+                round_w2(0)
+                load_into_slot_of(("w2", 0))
             gather_phases(b, t)
-            if ("sT", b, t) == lent:
-                load_w1()
-                gather_table_scales()
-            else:
-                load_into_slot_of(("sT", b, t))
+            load_into_slot_of(("sT", b, t))
+            if (b, t) == (1, 0):
+                make_planes()
             if (b, t) == (0, 0):
                 for half in range(HALVES):
-                    factor(b, t, 1, entries(half), 4 * half, ())
+                    factor(b, t, 1, entries(half), SINES_AT + 4 * half * KIB, ())
             elif b == 0:
-                factor(b, t, 1, slice(0, S), 8 * t, (3,))
-            elif b == last and t >= 2:
-                factor(b, t, 1, entries(0), 24 + 4 * (t - 2), (2, 3))
+                factor(b, t, 1, slice(0, S), SINES_AT + 8 * t * KIB, ())
+            elif b == last:
+                factor(b, t, 1, entries(0), SINES_AT + (16 + 4 * t) * KIB, (3,))
             elif t % 2 == 1:
-                factor(b, t - 1, 2, entries(0), 8 * (2 * (b - 1) + t // 2), ())
-        windows[OUT_TILES - 1] = place("window3", [P, T2], F32, W1_RAW_AT)
-        nc.gpsimd.memset(windows[OUT_TILES - 1][:].bitcast(I32), 0)
+                factor(b, t - 1, 2, entries(0), SINES_AT + 4 * (t - 1) * KIB, ())
+        for b in range(1, ROW_BLOCKS):
+            round_w2(b)
 
-        w2_bf16 = place("w2_bf16", [P, ROW_BLOCKS, N, PACK], BF16, LATE_AT + 4 * KIB)
-        for b in range(ROW_BLOCKS):
-            if b == 1:
-                nc.gpsimd.tensor_scalar(
-                    w2_bf16[:, b], loaded["w2", b][:].rearrange("p t c -> p c t"), 1.0, 0.0, ALU.mult, ALU.add
-                )
-            else:
-                nc.scalar.copy(side_by_side(w2_bf16[:, b], LINE), by_slice(loaded["w2", b][:], LINE))
-
-        make_z(0, 0, slot_at(ring.index(("sT", last, PACK - 1)) % STREAM_SLOTS), range(0, 4))
-        make_z(1, 0, LATE_AT, range(4, 8))
+        last_slot_at = slot_at(ring.index(("sT", last, PACK - 1)) % STREAM_SLOTS)
+        make_z(0, 0, last_slot_at, range(0, 4))
+        make_z(1, 0, last_slot_at + 4 * KIB, range(4, 8))
         make_z(2, 0, LATE_AT + 16 * KIB, range(0, 4))
         for b in range(ROW_BLOCKS):
             quantise(("z", b, 0), z_bf16[b, 0][:], work_at(1, 0) + b * 2 * KIB, work_at(last, 0) + b * KIB)
@@ -340,7 +330,7 @@ def tile_list_lattice_flow_adjoint_kernel(
         for b in range(1, ROW_BLOCKS):
             late[b, 1] = place(f"late{b}", [P, PACK, HALF], F32, LATE_AT + (b - 1) * 12 * KIB)
             for first in range(0, PACK, 2):
-                at = 32 + 4 * first if b == 1 else 4 * first
+                at = slot_at(first // 2) + 2 * KIB
                 on_scalar = () if first == 0 else (first, first + 1)
                 factor(b, first, 2, entries(1), at, on_scalar, late[b, 1][:, first : first + 2])
 

@@ -37,12 +37,13 @@ KIB = 1024
 STREAM_SLOTS = 5
 
 WINDOWS_AT = 0
-W1_RAW_AT = WINDOWS_AT + OUT_TILES * 8 * KIB
-WORK_AT = W1_RAW_AT + 12 * KIB
+LENT_AT = WINDOWS_AT + OUT_TILES * 8 * KIB
+WORK_AT = LENT_AT + 8 * KIB
 STREAM_AT = WORK_AT + ROW_BLOCKS * 16 * KIB
 SINES_AT = STREAM_AT + STREAM_SLOTS * 8 * KIB
-LATE_AT = SINES_AT + 4 * 8 * KIB
-V_CODES_AT = LATE_AT + 20 * KIB
+LATE_AT = SINES_AT + 6 * 8 * KIB
+Z_AT = LATE_AT + 18 * KIB
+V_CODES_AT = Z_AT + 10 * KIB
 W1_CODES_AT = V_CODES_AT + K_PASSES * 4 * KIB
 ROWS_AT = W1_CODES_AT + K_PASSES * 6 * KIB
 
@@ -76,26 +77,30 @@ def tile_list_lattice_flow_adjoint_kernel(
         sT_slices = sT.rearrange("(b m t i) c -> b t m i c", b=ROW_BLOCKS, t=PACK, i=LINE)
         w2_blocks = w2.rearrange("(b m t i) n -> b t m i n", b=ROW_BLOCKS, t=PACK, i=LINE)
         slices = [(b, t) for b in range(ROW_BLOCKS) for t in range(PACK)]
-        ring = [("sT",) + s for s in slices]
-        for a in range(K_PASSES):
-            ring.insert(ring.index(("sT", last, 1)), ("tab", a))
-        ring.insert(ring.index(("sT", last, 1)), ("w2", 0))
-        ring.extend([("w2", b) for b in range(1, ROW_BLOCKS)] + [("wgo",)])
+        lent = ("sT", 1, 1)
+        ring = [("sT",) + s for s in slices if ("sT",) + s != lent]
+        for key in (("w1", 0), ("tab", 0), ("tab", 1)):
+            ring.insert(ring.index(("sT", last, 2)), key)
+        ring.extend([("w2", b) for b in range(ROW_BLOCKS)] + [("wgo",)])
         loaded = {}
 
         def load(key):
             name = "load_" + "_".join(str(part) for part in key)
-            at = slot_at(ring.index(key) % STREAM_SLOTS)
-            if key[0] == "w2":
+            own = {lent: LENT_AT, ("w1", 1): Z_AT}
+            at = own[key] if key in own else slot_at(ring.index(key) % STREAM_SLOTS)
+            if key[0] == "w1":
+                loaded[key] = place(name, [P, H], I32, at)
+                nc.sync.dma_start(loaded[key][:], w1_words[key[1]].rearrange("p c i -> p (c i)").bitcast(I32))
+            elif key[0] == "wgo":
+                loaded[key] = place(name, [P, S], F32, at)
+                nc.sync.dma_start(loaded[key][:], wgo)
+            elif key[0] == "w2":
                 loaded[key] = place(name, [P, PACK, N], F32, at)
                 for t in range(PACK):
                     nc.sync.dma_start(loaded[key][:, t, :], w2_blocks[key[1], t])
             elif key[0] == "tab":
                 loaded[key] = place(name, [P, T], I32, at)
                 nc.sync.dma_start(loaded[key][:], tab_words[key[1]].rearrange("p c i -> p (c i)").bitcast(I32))
-            elif key[0] == "wgo":
-                loaded[key] = place(name, [P, S], F32, at + 4 * KIB)
-                nc.sync.dma_start(loaded[key][:], wgo)
             else:
                 loaded[key] = place(name, [P, T], F32, at)
                 nc.sync.dma_start(loaded[key][:], sT_slices[key[1], key[2]])
@@ -117,19 +122,11 @@ def tile_list_lattice_flow_adjoint_kernel(
 
         tab_rows = place("tab_rows", [P, T], U8, ROWS_AT)
         w1_rows = place("w1_rows", [P, H], U8, ROWS_AT + T)
-        v_planes = [place(f"v_plane{a}", [P, S], U8, ROWS_AT + T + H + a * S) for a in range(K_PASSES)]
-        w1_planes = [place(f"w1_plane{a}", [P, H], U8, ROWS_AT + T + H + 2 * S + a * H) for a in range(K_PASSES)]
+        v_planes = {1: place("v_plane1", [P, S], U8, ROWS_AT + T + H)}
+        w1_planes = {1: place("w1_plane1", [P, H], U8, ROWS_AT + T + H + S)}
         windows = {n: place(f"window{n}", [P, T2], F32, WINDOWS_AT + n * 8 * KIB) for n in range(OUT_TILES)}
-        for rows in (tab_rows, w1_rows):
+        for rows in (w1_rows, tab_rows):
             nc.vector.memset(rows[:].bitcast(I32), 0)
-        w1_codes = [place(f"w1_codes{a}", [P, H], U32, W1_CODES_AT + a * 6 * KIB) for a in range(K_PASSES)]
-        for a in range(K_PASSES):
-            w1_raw = place(f"w1_raw{a}", [P, H], I32, W1_RAW_AT + a * 6 * KIB)
-            nc.sync.dma_start(w1_raw[:], w1_words[a].rearrange("p c i -> p (c i)").bitcast(I32))
-            nc.vector.tensor_copy(
-                w1_codes[a][:].rearrange("p (b t m i) -> p t b m i", t=PACK, b=ROW_BLOCKS, i=LINE),
-                w1_raw[:].bitcast(U32).rearrange("p (b m t i) -> p t b m i", t=PACK, b=ROW_BLOCKS, i=LINE),
-            )
         for n in range(OUT_TILES):
             nc.vector.memset(windows[n][:].bitcast(I32), 0)
 
@@ -138,45 +135,50 @@ def tile_list_lattice_flow_adjoint_kernel(
         amp_runs = amp.rearrange("(b m e) -> m b e", b=ROW_BLOCKS, e=PACK * LINE)
         for i in range(LINE):
             nc.sync.dma_start(amp_sb[i:P:LINE, :, 0:AMP_RUN], amp_runs[:, :, i : i + AMP_RUN])
-        load(("sT", 0, 1))
-        load(("sT", 0, 2))
-        load_scale_rows(tab_rows, tab_scales, range(0, 2))
-        load(("sT", 0, 3))
-        load_scale_rows(tab_rows, tab_scales, range(2, 4))
-        load(("sT", 1, 0))
-        load_scale_rows(w1_rows, w1_scales, range(0, 2))
-        load_scale_rows(w1_rows, w1_scales, range(2, 4))
+        for key in [("sT",) + s for s in slices[1:6]] + [("w1", 1)]:
+            load(key)
         nc.sync.dma_start(idx2[:], offs2)
+        load_scale_rows(w1_rows, w1_scales, range(QUADRANTS))
+        load_scale_rows(tab_rows, tab_scales, range(QUADRANTS))
 
         v_codes = [place(f"v_codes{a}", [P, S], U32, V_CODES_AT + a * 4 * KIB) for a in range(K_PASSES)]
 
         def work_at(b, half):
             return WORK_AT + (b * 16 + half * 8) * KIB
 
-        work = {0: place("work0", [P, PACK, S], F32, work_at(0, 0))}
-        for b in range(1, ROW_BLOCKS):
-            for half in range(HALVES):
-                work[b, half] = place(f"work{b}{half}", [P, PACK, HALF], F32, work_at(b, half))
+        work = {b: place(f"work{b}", [P, PACK, S], F32, work_at(b, 0)) for b in range(last)}
+        for half in range(HALVES):
+            work[last, half] = place(f"work{last}{half}", [P, PACK, HALF], F32, work_at(last, half))
 
         def work_view(b, rows, columns):
-            if b == 0:
-                return work[0][:, rows, columns]
+            if b < last:
+                return work[b][:, rows, columns]
             half = columns.start // HALF
             return work[b, half][:, rows, columns.start - half * HALF : columns.stop - half * HALF]
 
-        z_bf16, codes, scales, y_banks, y_sb, late = {}, {}, {}, {}, {}, {}
+        z_bf16, codes, scales, y_banks, y_sb = {}, {}, {}, {}, {}
 
         def gather_phases(b, t):
             window = loaded["sT", b, t]
-            if b == 0 and t > 0:
-                nc.vector.tensor_copy(work[0][:, t, :], window[:].indirect(idx[:]))
+            if b < last and (b, t) != (0, 0):
+                nc.vector.tensor_copy(work[b][:, t, :], window[:].indirect(idx[:]))
             else:
                 for half in range(HALVES):
                     nc.vector.tensor_copy(
                         work_view(b, t, entries(half)), window[:].indirect(idx[:, list_columns(half)])
                     )
 
+        w1_codes = place("w1_codes", [P, K_PASSES, H], U32, W1_CODES_AT)
+
+        def reorder_w1(a, copy, walk):
+            copy(
+                w1_codes[:, a, :].rearrange("p (b t m i) -> " + walk, t=PACK, b=ROW_BLOCKS, i=LINE),
+                loaded["w1", a][:].bitcast(U32).rearrange("p (b m t i) -> " + walk, t=PACK, b=ROW_BLOCKS, i=LINE),
+            )
+
         def make_planes():
+            v_planes[0] = place("v_plane0", [P, S], U8, LENT_AT)
+            w1_planes[0] = place("w1_plane0", [P, H], U8, LENT_AT + S)
             nc.vector.tensor_copy(
                 w1_planes[0][:].bitcast(I32).rearrange("p (b t m i) -> p b m t i", t=PACK, b=ROW_BLOCKS, i=LINE),
                 w1_rows[:].bitcast(I32).rearrange("p (b m i t) -> p b m t i", t=PACK, b=ROW_BLOCKS, i=LINE),
@@ -190,32 +192,35 @@ def tile_list_lattice_flow_adjoint_kernel(
                 nc.vector.tensor_copy(v_codes[a][:], loaded["tab", a][:].bitcast(U32).indirect(idx[:]))
                 load_into_slot_of(("tab", a))
 
-        def factor(b, first, count, columns, at, on_scalar, result=None):
-            x = work_view(b, slice(first, first + count), columns)
-            shape = [P, 2, count, columns.stop - columns.start]
-            sines = place(f"sines{b}{first}{columns.start}", shape, F32, at)
-            minus_cos, sin = sines[:, 0], sines[:, 1]
+        def sines(name, x, at):
+            both = place(name, [P, 2] + list(x.shape[1:]), F32, at)
+            minus_cos, sin = both[:, 0], both[:, 1]
             steps = [(minus_cos, ACT.Abs), (sin, ACT.Sin)]
-            for target, function in reversed(steps) if (b, first, columns.start) == (0, 0, 0) else steps:
+            for target, function in reversed(steps) if name == "sines000" else steps:
                 nc.scalar.activation(target, x, function)
             nc.scalar.activation(minus_cos, minus_cos, ACT.Sin, bias=-math.pi / 2)
-            if result is None:
-                result = x
+            return minus_cos, sin
+
+        def amp_column(b, t):
+            return amp_sb[:, b, LINE * t : LINE * t + 1]
+
+        def factor(b, first, count, columns, at):
+            x = work_view(b, slice(first, first + count), columns)
+            minus_cos, sin = sines(f"sines{b}{first}{columns.start}", x, at)
             for t in range(first, first + count):
-                amp_column = amp_sb[:, b, LINE * t : LINE * t + 1]
                 one = sin[:, t - first]
-                if t in on_scalar:
-                    nc.scalar.activation(one, one, ACT.Identity, scale=amp_column, bias=-1.0)
-            for t in range(first, first + count):
-                amp_column = amp_sb[:, b, LINE * t : LINE * t + 1]
-                if t not in on_scalar:
-                    nc.gpsimd.tensor_scalar(result[:, t - first], sin[:, t - first], amp_column, -1.0, ALU.mult, ALU.add)
-            for t in range(first, first + count):
-                if count == 1 or len(on_scalar) not in (0, count):
-                    source = sin if t in on_scalar else result
-                    nc.gpsimd.tensor_tensor(result[:, t - first], source[:, t - first], minus_cos[:, t - first], ALU.mult)
-            if count > 1 and len(on_scalar) in (0, count):
-                nc.gpsimd.tensor_tensor(result, sin if on_scalar else result, minus_cos, ALU.mult)
+                if t == 1 or (b == last and t > 0):
+                    nc.scalar.activation(one, one, ACT.Identity, scale=amp_column(b, t), bias=-1.0)
+                else:
+                    nc.gpsimd.tensor_scalar(one, one, amp_column(b, t), -1.0, ALU.mult, ALU.add)
+            nc.gpsimd.tensor_tensor(x, sin, minus_cos, ALU.mult)
+
+        def late_factor(columns, at):
+            x = work_view(last, slice(0, PACK), columns)
+            minus_cos, sin = sines(f"late{columns.start}", x, at)
+            for t in range(PACK):
+                nc.scalar.activation(sin[:, t], sin[:, t], ACT.Identity, scale=amp_column(last, t), bias=-1.0)
+            return minus_cos, sin
 
         def by_slice(values, run=PAIR):
             return values.rearrange("p t (c i) -> p c t i", i=run)
@@ -223,39 +228,40 @@ def tile_list_lattice_flow_adjoint_kernel(
         def side_by_side(values, run=PAIR):
             return values.rearrange("p (c i) t -> p c t i", i=run)
 
-        def make_z(b, half, at, banks):
-            z_bf16[b, half] = place(f"z{b}{half}", [P, HALF, PACK], BF16, at)
-            for start, bank in zip(range(0, HALF, GROUP), banks):
-                group = slice(half * HALF + start, half * HALF + start + GROUP)
+        def make_z(b, first, z, banks, factors=None):
+            for g, bank in enumerate(banks):
+                group = slice(first + g * GROUP, first + (g + 1) * GROUP)
                 h_bank = psum.tile([P, PACK, GROUP], F32, name=f"bank{bank}")
                 for t in range(PACK):
-                    rows = slice(b * PASS + t * P, b * PASS + (t + 1) * P)
                     for a in range(K_PASSES):
                         nc.tensor.matmul_mx(
                             h_bank[:, t, :],
-                            lhsT=w1_codes[a][:, rows].bitcast(E4M3X4),
-                            lhsT_scale=w1_planes[a][:, rows],
+                            lhsT=w1_codes[:, a, b * PASS + t * P : b * PASS + (t + 1) * P].bitcast(E4M3X4),
+                            lhsT_scale=w1_planes[a][:, b * PASS + t * P : b * PASS + (t + 1) * P],
                             rhs=v_codes[a][:, group].bitcast(E5M2X4),
                             rhs_scale=v_planes[a][:, group],
                             start=(a == 0),
                             stop=(a == K_PASSES - 1),
                         )
-                if (b, half) in late:
-                    factors = late[b, half][:, :, start : start + GROUP]
+                if factors is None:
+                    factor_group = work_view(b, slice(0, PACK), group)
                 else:
-                    factors = work_view(b, slice(0, PACK), group)
+                    factor_group = factors[:, :, g * GROUP : (g + 1) * GROUP]
                 nc.vector.tensor_tensor(
-                    side_by_side(z_bf16[b, half][:, start : start + GROUP, :]),
-                    by_slice(factors),
+                    side_by_side(z[:, g * GROUP : (g + 1) * GROUP, :]),
+                    by_slice(factor_group),
                     by_slice(h_bank[:]),
                     ALU.mult,
                 )
 
-        def quantise(key, source, at, scales_at):
-            name = "_".join(str(part) for part in key)
-            codes[key] = place("codes_" + name, [P, HALF], U32, at)
-            scales[key] = place("scales_" + name, [P, HALF], U8, scales_at)
-            nc.vector.quantize_mx(codes[key][:].bitcast(E4M3X4), scales[key][:], source.rearrange("p c t -> p (c t)"))
+        def quantise(key, source, at, scales_at, columns=slice(0, HALF)):
+            if key not in codes:
+                name = "_".join(str(part) for part in key)
+                codes[key] = place("codes_" + name, [P, HALF], U32, at)
+                scales[key] = place("scales_" + name, [P, HALF], U8, scales_at)
+            nc.vector.quantize_mx(
+                codes[key][:, columns].bitcast(E4M3X4), scales[key][:, columns], source.rearrange("p c t -> p (c t)")
+            )
 
         def second_product(half, banks):
             for n, bank in enumerate(banks):
@@ -273,13 +279,6 @@ def tile_list_lattice_flow_adjoint_kernel(
                         stop=(b == last),
                     )
 
-        def weigh(half, n, at):
-            y_sb[half, n] = place(f"y{half}{n}", [P, HALF], F32, at)
-            nc.vector.tensor_tensor(y_sb[half, n][:], y_banks[half, n][:], loaded["wgo",][:, entries(half)], ALU.mult)
-
-        def scatter_weighed(half, n):
-            nc.vector.tensor_copy(windows[n][:].indirect(idx2[:, list_columns(half)]), y_sb[half, n][:])
-
         def copy_and_scatter(half, n, at):
             y_sb[half, n] = place(f"y{half}{n}", [P, HALF], F32, at)
             nc.scalar.copy(y_sb[half, n][:], y_banks[half, n][:])
@@ -290,61 +289,67 @@ def tile_list_lattice_flow_adjoint_kernel(
                 ALU.mult,
             )
 
-        w2_bf16 = place("w2_bf16", [P, ROW_BLOCKS, N, PACK], BF16, LATE_AT + 4 * KIB)
+        w2_bf16 = place("w2_bf16", [P, ROW_BLOCKS, N, PACK], BF16, LATE_AT)
 
         def round_w2(b):
             nc.scalar.copy(side_by_side(w2_bf16[:, b], LINE), by_slice(loaded["w2", b][:], LINE))
 
         for b, t in slices:
-            if (b, t) == (last, 1):
-                gather_table()
-                round_w2(0)
-                load_into_slot_of(("w2", 0))
             gather_phases(b, t)
-            load_into_slot_of(("sT", b, t))
-            if (b, t) == (1, 0):
+            if ("sT", b, t) == lent:
                 make_planes()
+            else:
+                load_into_slot_of(("sT", b, t))
+            if (b, t) == (last, 1):
+                reorder_w1(0, nc.vector.tensor_copy, "p b m t i")
+                load_into_slot_of(("w1", 0))
+                gather_table()
+            if (b, t) == (1, 0):
+                reorder_w1(1, nc.gpsimd.tensor_copy, "p b t m i")
             if (b, t) == (0, 0):
                 for half in range(HALVES):
-                    factor(b, t, 1, entries(half), SINES_AT + 4 * half * KIB, ())
+                    factor(b, t, 1, entries(half), SINES_AT + 4 * half * KIB)
             elif b == 0:
-                factor(b, t, 1, slice(0, S), SINES_AT + 8 * t * KIB, ())
-            elif b == last:
-                factor(b, t, 1, entries(0), SINES_AT + (16 + 4 * t) * KIB, (3,))
+                factor(b, t, 1, slice(0, S), SINES_AT + 8 * t * KIB)
+            elif t % 2 == 1 and b < last:
+                factor(b, t - 1, 2, slice(0, S), SINES_AT + 16 * ((2 * b + t // 2) % 3) * KIB)
             elif t % 2 == 1:
-                factor(b, t - 1, 2, entries(0), SINES_AT + 4 * (t - 1) * KIB, ())
-        for b in range(1, ROW_BLOCKS):
+                factor(b, t - 1, 2, entries(0), SINES_AT + (16 + 4 * (t - 1)) * KIB)
+        for b in range(ROW_BLOCKS):
             round_w2(b)
 
         last_slot_at = slot_at(ring.index(("sT", last, PACK - 1)) % STREAM_SLOTS)
-        make_z(0, 0, last_slot_at, range(0, 4))
-        make_z(1, 0, last_slot_at + 4 * KIB, range(4, 8))
-        make_z(2, 0, LATE_AT + 16 * KIB, range(0, 4))
+        for half in range(HALVES):
+            z_bf16[0, half] = place(f"z0{half}", [P, HALF, PACK], BF16, last_slot_at + half * 4 * KIB)
+            make_z(0, half * HALF, z_bf16[0, half], range(4 * half, 4 * half + 4))
+        z_bf16[1, 0] = place("z10", [P, HALF, PACK], BF16, Z_AT)
+        make_z(1, 0, z_bf16[1, 0], range(0, 4))
+        z_third = place("z_third", [P, HALF // 2, PACK], BF16, Z_AT + 4 * KIB)
+        make_z(1, HALF, z_third, (4, 5))
+        z_bf16[last, 0] = place("z20", [P, HALF, PACK], BF16, Z_AT + 6 * KIB)
+        make_z(last, 0, z_bf16[last, 0], (6, 7, 0, 1))
         for b in range(ROW_BLOCKS):
-            quantise(("z", b, 0), z_bf16[b, 0][:], work_at(1, 0) + b * 2 * KIB, work_at(last, 0) + b * KIB)
-            w2_codes_at = work_at(1, 0) + 6 * KIB if b == 0 else work_at(last, 0) + (2 + 2 * b) * KIB
-            quantise(("w2", b), w2_bf16[:, b], w2_codes_at, work_at(last, 0) + b * KIB + HALF)
-        second_product(0, range(0, 4))
-        make_z(0, 1, LATE_AT + 8 * KIB, range(4, 8))
-
-        for b in range(1, ROW_BLOCKS):
-            late[b, 1] = place(f"late{b}", [P, PACK, HALF], F32, LATE_AT + (b - 1) * 12 * KIB)
-            for first in range(0, PACK, 2):
-                at = slot_at(first // 2) + 2 * KIB
-                on_scalar = () if first == 0 else (first, first + 1)
-                factor(b, first, 2, entries(1), at, on_scalar, late[b, 1][:, first : first + 2])
-
+            quantise(("z", b, 0), z_bf16[b, 0][:], work_at(0, 0) + b * 4 * KIB, work_at(last, 0) + b * KIB)
+            quantise(("w2", b), w2_bf16[:, b], work_at(0, 0) + (b * 4 + 2) * KIB, work_at(last, 0) + b * KIB + HALF)
+        second_product(0, range(4, 8))
+        z_fourth = place("z_fourth", [P, HALF // 2, PACK], BF16, LATE_AT)
+        make_z(1, HALF + HALF // 2, z_fourth, (2, 3))
+        quantise(("z", 0, 1), z_bf16[0, 1][:], work_at(0, 0) + 12 * KIB, work_at(last, 0) + 3 * KIB)
         for n in range(OUT_TILES - 1):
-            weigh(0, n, SINES_AT + (24 + 2 * n) * KIB)
-            if n != 1:
-                scatter_weighed(0, n // 2)
-        scatter_weighed(0, 2)
-        make_z(1, 1, SINES_AT + 16 * KIB, range(4, 8))
-        make_z(2, 1, SINES_AT + 20 * KIB, (0, 1, 2, 4))
-        for b in range(ROW_BLOCKS):
-            quantise(("z", b, 1), z_bf16[b, 1][:], work_at(1, 1) + b * 2 * KIB, LATE_AT + 12 * KIB + b * HALF)
-        second_product(1, (5, 6, 7, 0))
-        copy_and_scatter(0, OUT_TILES - 1, LATE_AT + 8 * KIB)
+            copy_and_scatter(0, n, slot_at(ring.index(("w2", 0)) % STREAM_SLOTS) + n * 2 * KIB)
+
+        z_bf16[last, 1] = place("z21", [P, HALF, PACK], BF16, Z_AT)
+        for part in range(2):
+            first = HALF + part * HALF // 2
+            minus_cos, sin = late_factor(slice(first, first + HALF // 2), LATE_AT + (2 + 8 * part) * KIB)
+            nc.vector.tensor_tensor(sin, sin, minus_cos, ALU.mult)
+            z_part = z_bf16[last, 1][:, part * HALF // 2 : (part + 1) * HALF // 2, :]
+            make_z(last, first, z_part, (2 * part, 2 * part + 1), sin)
+        for source, columns in ((z_fourth, slice(HALF // 2, HALF)), (z_third, slice(0, HALF // 2))):
+            quantise(("z", 1, 1), source[:], work_at(0, 0) + 14 * KIB, LATE_AT + 10 * KIB, columns)
+        quantise(("z", last, 1), z_bf16[last, 1][:], work_at(last, 0) + 4 * KIB, LATE_AT + 11 * KIB)
+        second_product(1, (4, 5, 6, 0))
+        copy_and_scatter(0, OUT_TILES - 1, LATE_AT)
         for n in range(OUT_TILES):
-            copy_and_scatter(1, n, LATE_AT + n * 2 * KIB)
+            copy_and_scatter(1, n, slot_at(ring.index(("w2", 1)) % STREAM_SLOTS) + n * 2 * KIB)
             nc.sync.dma_start(out[n * P : (n + 1) * P, :], windows[n][:])

@@ -31,6 +31,7 @@ SCALE_ROWS = 4
 SHIFTED = 32 * (QUADRANTS - 1) + SCALE_ROWS
 LINE = 4
 GROUP = HALF // PACK
+SIDE = N // 2
 PAIR = 2
 AMP_RUN = LINE * (PACK - 1) + 1
 KIB = 1024
@@ -42,8 +43,8 @@ WORK_AT = LENT_AT + 8 * KIB
 STREAM_AT = WORK_AT + ROW_BLOCKS * 16 * KIB
 SINES_AT = STREAM_AT + STREAM_SLOTS * 8 * KIB
 LATE_AT = SINES_AT + 6 * 8 * KIB
-Z_AT = LATE_AT + 18 * KIB
-V_CODES_AT = Z_AT + 10 * KIB
+Z_AT = LATE_AT + 12 * KIB
+V_CODES_AT = Z_AT + 16 * KIB
 W1_CODES_AT = V_CODES_AT + K_PASSES * 4 * KIB
 ROWS_AT = W1_CODES_AT + K_PASSES * 6 * KIB
 
@@ -79,36 +80,37 @@ def tile_list_lattice_flow_adjoint_kernel(
         slices = [(b, t) for b in range(ROW_BLOCKS) for t in range(PACK)]
         lent = ("sT", 1, 1)
         ring = [("sT",) + s for s in slices if ("sT",) + s != lent]
-        for key in (("w1", 0), ("tab", 0), ("tab", 1)):
-            ring.insert(ring.index(("sT", last, 2)), key)
-        ring.extend([("w2", b) for b in range(ROW_BLOCKS)] + [("wgo",)])
+        for a in range(K_PASSES):
+            ring.insert(ring.index(("sT", last, 2)), ("tab", a))
         loaded = {}
+
+        w1_blocks = w1_words.rearrange("a p (b c) i -> b p a (c i)", b=ROW_BLOCKS)
+
+        def slot_of(key):
+            return LENT_AT if key == lent else slot_at(ring.index(key) % STREAM_SLOTS)
 
         def load(key):
             name = "load_" + "_".join(str(part) for part in key)
-            own = {lent: LENT_AT, ("w1", 1): Z_AT}
-            at = own[key] if key in own else slot_at(ring.index(key) % STREAM_SLOTS)
-            if key[0] == "w1":
-                loaded[key] = place(name, [P, H], I32, at)
-                nc.sync.dma_start(loaded[key][:], w1_words[key[1]].rearrange("p c i -> p (c i)").bitcast(I32))
-            elif key[0] == "wgo":
-                loaded[key] = place(name, [P, S], F32, at)
-                nc.sync.dma_start(loaded[key][:], wgo)
-            elif key[0] == "w2":
-                loaded[key] = place(name, [P, PACK, N], F32, at)
-                for t in range(PACK):
-                    nc.sync.dma_start(loaded[key][:, t, :], w2_blocks[key[1], t])
-            elif key[0] == "tab":
-                loaded[key] = place(name, [P, T], I32, at)
+            if key[0] == "tab":
+                loaded[key] = place(name, [P, T], I32, slot_of(key))
                 nc.sync.dma_start(loaded[key][:], tab_words[key[1]].rearrange("p c i -> p (c i)").bitcast(I32))
             else:
-                loaded[key] = place(name, [P, T], F32, at)
+                loaded[key] = place(name, [P, T], F32, slot_of(key))
                 nc.sync.dma_start(loaded[key][:], sT_slices[key[1], key[2]])
 
         def load_into_slot_of(key):
             following = ring.index(key) + STREAM_SLOTS
             if following < len(ring):
                 load(ring[following])
+
+        def load_w1(b, at):
+            loaded["w1", b] = place(f"load_w1_{b}", [P, K_PASSES, PASS], I32, at)
+            nc.sync.dma_start(loaded["w1", b][:], w1_blocks[b].bitcast(I32))
+
+        def load_w2(side, b, at):
+            loaded["w2", side, b] = place(f"load_w2_{side}{b}", [P, PACK, SIDE], F32, at)
+            for t in range(PACK):
+                nc.sync.dma_start(loaded["w2", side, b][:, t, :], w2_blocks[b, t, :, :, side * SIDE : (side + 1) * SIDE])
 
         def load_scale_rows(tile, scales, quadrants):
             for q in quadrants:
@@ -135,8 +137,10 @@ def tile_list_lattice_flow_adjoint_kernel(
         amp_runs = amp.rearrange("(b m e) -> m b e", b=ROW_BLOCKS, e=PACK * LINE)
         for i in range(LINE):
             nc.sync.dma_start(amp_sb[i:P:LINE, :, 0:AMP_RUN], amp_runs[:, :, i : i + AMP_RUN])
-        for key in [("sT",) + s for s in slices[1:6]] + [("w1", 1)]:
-            load(key)
+        for s in slices[1:6]:
+            load(("sT",) + s)
+        for block in range(last):
+            load_w1(block, Z_AT + block * 4 * KIB)
         nc.sync.dma_start(idx2[:], offs2)
         load_scale_rows(w1_rows, w1_scales, range(QUADRANTS))
         load_scale_rows(tab_rows, tab_scales, range(QUADRANTS))
@@ -168,12 +172,13 @@ def tile_list_lattice_flow_adjoint_kernel(
                         work_view(b, t, entries(half)), window[:].indirect(idx[:, list_columns(half)])
                     )
 
-        w1_codes = place("w1_codes", [P, K_PASSES, H], U32, W1_CODES_AT)
+        w1_codes = {}
 
-        def reorder_w1(a, copy, walk):
-            copy(
-                w1_codes[:, a, :].rearrange("p (b t m i) -> " + walk, t=PACK, b=ROW_BLOCKS, i=LINE),
-                loaded["w1", a][:].bitcast(U32).rearrange("p (b m t i) -> " + walk, t=PACK, b=ROW_BLOCKS, i=LINE),
+        def reorder_w1(b):
+            w1_codes[b] = place(f"w1_codes{b}", [P, K_PASSES, PASS], U32, W1_CODES_AT + b * 4 * KIB)
+            nc.gpsimd.tensor_copy(
+                w1_codes[b][:].rearrange("p a (t m i) -> p a t m i", t=PACK, i=LINE),
+                loaded["w1", b][:].bitcast(U32).rearrange("p a (m t i) -> p a t m i", t=PACK, i=LINE),
             )
 
         def make_planes():
@@ -190,7 +195,6 @@ def tile_list_lattice_flow_adjoint_kernel(
         def gather_table():
             for a in range(K_PASSES):
                 nc.vector.tensor_copy(v_codes[a][:], loaded["tab", a][:].bitcast(U32).indirect(idx[:]))
-                load_into_slot_of(("tab", a))
 
         def sines(name, x, at):
             both = place(name, [P, 2] + list(x.shape[1:]), F32, at)
@@ -204,23 +208,16 @@ def tile_list_lattice_flow_adjoint_kernel(
         def amp_column(b, t):
             return amp_sb[:, b, LINE * t : LINE * t + 1]
 
-        def factor(b, first, count, columns, at):
+        def factor(b, first, count, columns, at, result=None):
             x = work_view(b, slice(first, first + count), columns)
             minus_cos, sin = sines(f"sines{b}{first}{columns.start}", x, at)
             for t in range(first, first + count):
                 one = sin[:, t - first]
-                if t == 1 or (b == last and t > 0):
+                if t == 1 or (b == last and t > 0) or result is not None:
                     nc.scalar.activation(one, one, ACT.Identity, scale=amp_column(b, t), bias=-1.0)
                 else:
                     nc.gpsimd.tensor_scalar(one, one, amp_column(b, t), -1.0, ALU.mult, ALU.add)
-            nc.gpsimd.tensor_tensor(x, sin, minus_cos, ALU.mult)
-
-        def late_factor(columns, at):
-            x = work_view(last, slice(0, PACK), columns)
-            minus_cos, sin = sines(f"late{columns.start}", x, at)
-            for t in range(PACK):
-                nc.scalar.activation(sin[:, t], sin[:, t], ACT.Identity, scale=amp_column(last, t), bias=-1.0)
-            return minus_cos, sin
+            nc.gpsimd.tensor_tensor(x if result is None else result, sin, minus_cos, ALU.mult)
 
         def by_slice(values, run=PAIR):
             return values.rearrange("p t (c i) -> p c t i", i=run)
@@ -228,72 +225,69 @@ def tile_list_lattice_flow_adjoint_kernel(
         def side_by_side(values, run=PAIR):
             return values.rearrange("p (c i) t -> p c t i", i=run)
 
-        def make_z(b, first, z, banks, factors=None):
-            for g, bank in enumerate(banks):
-                group = slice(first + g * GROUP, first + (g + 1) * GROUP)
-                h_bank = psum.tile([P, PACK, GROUP], F32, name=f"bank{bank}")
+        def make_z(b, half, at):
+            z_bf16[b, half] = place(f"z{b}{half}", [P, HALF, PACK], BF16, at)
+            for g in range(PACK):
+                group = slice(half * HALF + g * GROUP, half * HALF + (g + 1) * GROUP)
+                h_bank = psum.tile([P, PACK, GROUP], F32, name=f"bank{half * PACK + g}")
                 for t in range(PACK):
                     for a in range(K_PASSES):
                         nc.tensor.matmul_mx(
                             h_bank[:, t, :],
-                            lhsT=w1_codes[:, a, b * PASS + t * P : b * PASS + (t + 1) * P].bitcast(E4M3X4),
+                            lhsT=w1_codes[b][:, a, t * P : (t + 1) * P].bitcast(E4M3X4),
                             lhsT_scale=w1_planes[a][:, b * PASS + t * P : b * PASS + (t + 1) * P],
                             rhs=v_codes[a][:, group].bitcast(E5M2X4),
                             rhs_scale=v_planes[a][:, group],
                             start=(a == 0),
                             stop=(a == K_PASSES - 1),
                         )
-                if factors is None:
-                    factor_group = work_view(b, slice(0, PACK), group)
+                if (b, half) == (last, 1):
+                    factors = last_factors[:, :, g * GROUP : (g + 1) * GROUP]
                 else:
-                    factor_group = factors[:, :, g * GROUP : (g + 1) * GROUP]
+                    factors = work_view(b, slice(0, PACK), group)
                 nc.vector.tensor_tensor(
-                    side_by_side(z[:, g * GROUP : (g + 1) * GROUP, :]),
-                    by_slice(factor_group),
+                    side_by_side(z_bf16[b, half][:, g * GROUP : (g + 1) * GROUP, :]),
+                    by_slice(factors),
                     by_slice(h_bank[:]),
                     ALU.mult,
                 )
 
-        def quantise(key, source, at, scales_at, columns=slice(0, HALF)):
-            if key not in codes:
-                name = "_".join(str(part) for part in key)
-                codes[key] = place("codes_" + name, [P, HALF], U32, at)
-                scales[key] = place("scales_" + name, [P, HALF], U8, scales_at)
-            nc.vector.quantize_mx(
-                codes[key][:, columns].bitcast(E4M3X4), scales[key][:, columns], source.rearrange("p c t -> p (c t)")
-            )
+        def round_w2(side, b):
+            w2_bf16[side, b] = place(f"w2_bf16_{side}{b}", [P, SIDE, PACK], BF16, LATE_AT + (side * 6 + b * 2) * KIB)
+            nc.scalar.copy(side_by_side(w2_bf16[side, b][:], LINE), by_slice(loaded["w2", side, b][:], LINE))
 
-        def second_product(half, banks):
-            for n, bank in enumerate(banks):
-                y_banks[half, n] = psum.tile([P, HALF], F32, name=f"bank{bank}")
+        def quantise(key, source, at, scales_at):
+            name = "_".join(str(part) for part in key)
+            codes[key] = place("codes_" + name, [P, source.shape[1]], U32, at)
+            scales[key] = place("scales_" + name, [P, source.shape[1]], U8, scales_at)
+            nc.vector.quantize_mx(codes[key][:].bitcast(E4M3X4), scales[key][:], source[:].rearrange("p c t -> p (c t)"))
+
+        def second_product(half, side, first_bank):
+            for n in range(2):
+                y_banks[half, 2 * side + n] = psum.tile([P, HALF], F32, name=f"bank{first_bank + n}")
             for b in range(ROW_BLOCKS):
-                for n in range(OUT_TILES):
+                for n in range(2):
                     columns = slice(n * P, (n + 1) * P)
                     nc.tensor.matmul_mx(
-                        y_banks[half, n][:],
-                        lhsT=codes["w2", b][:, columns].bitcast(E4M3X4),
-                        lhsT_scale=scales["w2", b][:, columns],
+                        y_banks[half, 2 * side + n][:],
+                        lhsT=codes["w2", side, b][:, columns].bitcast(E4M3X4),
+                        lhsT_scale=scales["w2", side, b][:, columns],
                         rhs=codes["z", b, half][:].bitcast(E4M3X4),
                         rhs_scale=scales["z", b, half][:],
                         start=(b == 0),
                         stop=(b == last),
                     )
 
-        def copy_and_scatter(half, n, at):
+        def copy_out(half, n, at):
             y_sb[half, n] = place(f"y{half}{n}", [P, HALF], F32, at)
             nc.scalar.copy(y_sb[half, n][:], y_banks[half, n][:])
+
+        def scatter(half, n):
             nc.vector.tensor_tensor(
-                windows[n][:].indirect(idx2[:, list_columns(half)]),
-                y_sb[half, n][:],
-                loaded["wgo",][:, entries(half)],
-                ALU.mult,
+                windows[n][:].indirect(idx2[:, list_columns(half)]), y_sb[half, n][:], wgo_sb[:, entries(half)], ALU.mult
             )
 
-        w2_bf16 = place("w2_bf16", [P, ROW_BLOCKS, N, PACK], BF16, LATE_AT)
-
-        def round_w2(b):
-            nc.scalar.copy(side_by_side(w2_bf16[:, b], LINE), by_slice(loaded["w2", b][:], LINE))
-
+        w2_bf16 = {}
         for b, t in slices:
             gather_phases(b, t)
             if ("sT", b, t) == lent:
@@ -301,11 +295,20 @@ def tile_list_lattice_flow_adjoint_kernel(
             else:
                 load_into_slot_of(("sT", b, t))
             if (b, t) == (last, 1):
-                reorder_w1(0, nc.vector.tensor_copy, "p b m t i")
-                load_into_slot_of(("w1", 0))
+                load_w1(last, slot_of(("sT", b, t)))
                 gather_table()
-            if (b, t) == (1, 0):
-                reorder_w1(1, nc.gpsimd.tensor_copy, "p b t m i")
+                for block in range(last):
+                    load_w2(0, block, slot_of(("tab", 0)) + block * 4 * KIB)
+                load_w2(0, last, slot_of(("tab", 1)))
+                wgo_sb = place("wgo_sb", [P, S], F32, slot_of(("tab", 1)) + 4 * KIB)
+                nc.sync.dma_start(wgo_sb[:], wgo)
+            if (b, t) == (last, 2):
+                for block in range(last):
+                    load_w2(1, block, slot_of(("sT", b, t)) + block * 4 * KIB)
+            if (b, t) == (0, PACK - 1):
+                reorder_w1(0)
+            if (b, t) == (1, 1):
+                reorder_w1(1)
             if (b, t) == (0, 0):
                 for half in range(HALVES):
                     factor(b, t, 1, entries(half), SINES_AT + 4 * half * KIB)
@@ -315,41 +318,42 @@ def tile_list_lattice_flow_adjoint_kernel(
                 factor(b, t - 1, 2, slice(0, S), SINES_AT + 16 * ((2 * b + t // 2) % 3) * KIB)
             elif t % 2 == 1:
                 factor(b, t - 1, 2, entries(0), SINES_AT + (16 + 4 * (t - 1)) * KIB)
+        reorder_w1(last)
+        last_factors = place("last_factors", [P, PACK, HALF], F32, slot_of(("sT", last, 1)))
+        for t in range(0, PACK, 2):
+            factor(last, t, 2, entries(1), SINES_AT + (32 + 4 * t) * KIB, last_factors[:, t : t + 2])
         for b in range(ROW_BLOCKS):
-            round_w2(b)
+            round_w2(0, b)
+        load_w2(1, last, SINES_AT + 12 * KIB)
 
-        last_slot_at = slot_at(ring.index(("sT", last, PACK - 1)) % STREAM_SLOTS)
         for half in range(HALVES):
-            z_bf16[0, half] = place(f"z0{half}", [P, HALF, PACK], BF16, last_slot_at + half * 4 * KIB)
-            make_z(0, half * HALF, z_bf16[0, half], range(4 * half, 4 * half + 4))
-        z_bf16[1, 0] = place("z10", [P, HALF, PACK], BF16, Z_AT)
-        make_z(1, 0, z_bf16[1, 0], range(0, 4))
-        z_third = place("z_third", [P, HALF // 2, PACK], BF16, Z_AT + 4 * KIB)
-        make_z(1, HALF, z_third, (4, 5))
-        z_bf16[last, 0] = place("z20", [P, HALF, PACK], BF16, Z_AT + 6 * KIB)
-        make_z(last, 0, z_bf16[last, 0], (6, 7, 0, 1))
+            make_z(0, half, slot_of(("sT", last, PACK - 1)) + half * 4 * KIB)
+        for half in range(HALVES):
+            make_z(1, half, Z_AT + half * 4 * KIB)
+        make_z(last, 0, Z_AT + 8 * KIB)
         for b in range(ROW_BLOCKS):
-            quantise(("z", b, 0), z_bf16[b, 0][:], work_at(0, 0) + b * 4 * KIB, work_at(last, 0) + b * KIB)
-            quantise(("w2", b), w2_bf16[:, b], work_at(0, 0) + (b * 4 + 2) * KIB, work_at(last, 0) + b * KIB + HALF)
-        second_product(0, range(4, 8))
-        z_fourth = place("z_fourth", [P, HALF // 2, PACK], BF16, LATE_AT)
-        make_z(1, HALF + HALF // 2, z_fourth, (2, 3))
-        quantise(("z", 0, 1), z_bf16[0, 1][:], work_at(0, 0) + 12 * KIB, work_at(last, 0) + 3 * KIB)
-        for n in range(OUT_TILES - 1):
-            copy_and_scatter(0, n, slot_at(ring.index(("w2", 0)) % STREAM_SLOTS) + n * 2 * KIB)
-
-        z_bf16[last, 1] = place("z21", [P, HALF, PACK], BF16, Z_AT)
-        for part in range(2):
-            first = HALF + part * HALF // 2
-            minus_cos, sin = late_factor(slice(first, first + HALF // 2), LATE_AT + (2 + 8 * part) * KIB)
-            nc.vector.tensor_tensor(sin, sin, minus_cos, ALU.mult)
-            z_part = z_bf16[last, 1][:, part * HALF // 2 : (part + 1) * HALF // 2, :]
-            make_z(last, first, z_part, (2 * part, 2 * part + 1), sin)
-        for source, columns in ((z_fourth, slice(HALF // 2, HALF)), (z_third, slice(0, HALF // 2))):
-            quantise(("z", 1, 1), source[:], work_at(0, 0) + 14 * KIB, LATE_AT + 10 * KIB, columns)
-        quantise(("z", last, 1), z_bf16[last, 1][:], work_at(last, 0) + 4 * KIB, LATE_AT + 11 * KIB)
-        second_product(1, (4, 5, 6, 0))
-        copy_and_scatter(0, OUT_TILES - 1, LATE_AT)
-        for n in range(OUT_TILES):
-            copy_and_scatter(1, n, slot_at(ring.index(("w2", 1)) % STREAM_SLOTS) + n * 2 * KIB)
-            nc.sync.dma_start(out[n * P : (n + 1) * P, :], windows[n][:])
+            quantise(("z", b, 0), z_bf16[b, 0], work_at(0, 0) + b * 2 * KIB, work_at(last, 0) + b * KIB)
+        make_z(last, 1, Z_AT)
+        for b in range(ROW_BLOCKS):
+            quantise(("w2", 0, b), w2_bf16[0, b], work_at(0, 0) + (6 + b) * KIB, slot_of(("sT", last, 1)) + b * KIB)
+        second_product(0, 0, 0)
+        for n in range(2):
+            copy_out(0, n, slot_of(("tab", 0)) + n * 2 * KIB)
+        for b in range(ROW_BLOCKS):
+            quantise(("z", b, 1), z_bf16[b, 1], work_at(1, 0) + b * 2 * KIB, LATE_AT + 4 * KIB + b * HALF)
+        second_product(1, 0, 2)
+        for b in range(ROW_BLOCKS):
+            round_w2(1, b)
+            quantise(("w2", 1, b), w2_bf16[1, b], work_at(1, 0) + (6 + b) * KIB, slot_of(("sT", last, 1)) + (4 + b) * KIB)
+        for n in range(2):
+            copy_out(1, n, LATE_AT + (6 + 2 * n) * KIB)
+        for half in range(HALVES):
+            second_product(half, 1, 4 + 2 * half)
+            for n in range(2, OUT_TILES):
+                copy_out(half, n, SINES_AT + (2 * half + n) * 2 * KIB)
+        for side in range(2):
+            for half in range(HALVES):
+                for n in range(2 * side, 2 * side + 2):
+                    scatter(half, n)
+                    if half == HALVES - 1:
+                        nc.sync.dma_start(out[n * P : (n + 1) * P, :], windows[n][:])

@@ -36,6 +36,7 @@ PAIR = 2
 AMP_RUN = LINE * (PACK - 1) + 1
 KIB = 1024
 STREAM_SLOTS = 5
+SLOT_ORDER = [0, 1, 3, 4, 2]
 
 WINDOWS_AT = 0
 LENT_AT = WINDOWS_AT + OUT_TILES * 8 * KIB
@@ -68,7 +69,7 @@ def tile_list_lattice_flow_adjoint_kernel(
             return slice(half * HALF // PER_COLUMN, (half + 1) * HALF // PER_COLUMN)
 
         def slot_at(slot):
-            return STREAM_AT + slot * 8 * KIB
+            return STREAM_AT + SLOT_ORDER.index(slot) * 8 * KIB
 
         idx = keep.tile([P, S // PER_COLUMN], U16, name="idx")
         idx2 = keep.tile([P, S // PER_COLUMN], U16, name="idx2")
@@ -82,6 +83,7 @@ def tile_list_lattice_flow_adjoint_kernel(
         ring = [("sT",) + s for s in slices if ("sT",) + s != lent]
         for a in range(K_PASSES):
             ring.insert(ring.index(("sT", last, 2)), ("tab", a))
+        ring.insert(ring.index(("sT", last, PACK - 1)), ("w1", 1))
         loaded = {}
 
         w1_blocks = w1_words.rearrange("a p (b c) i -> b p a (c i)", b=ROW_BLOCKS)
@@ -91,7 +93,9 @@ def tile_list_lattice_flow_adjoint_kernel(
 
         def load(key):
             name = "load_" + "_".join(str(part) for part in key)
-            if key[0] == "tab":
+            if key[0] == "w1":
+                load_w1(key[1], slot_of(key) + 2 * KIB)
+            elif key[0] == "tab":
                 loaded[key] = place(name, [P, T], I32, slot_of(key))
                 nc.sync.dma_start(loaded[key][:], tab_words[key[1]].rearrange("p c i -> p (c i)").bitcast(I32))
             else:
@@ -139,8 +143,7 @@ def tile_list_lattice_flow_adjoint_kernel(
             nc.sync.dma_start(amp_sb[i:P:LINE, :, 0:AMP_RUN], amp_runs[:, :, i : i + AMP_RUN])
         for s in slices[1:6]:
             load(("sT",) + s)
-        for block in range(last):
-            load_w1(block, Z_AT + block * 4 * KIB)
+        load_w1(0, Z_AT)
         nc.sync.dma_start(idx2[:], offs2)
         load_scale_rows(w1_rows, w1_scales, range(QUADRANTS))
         load_scale_rows(tab_rows, tab_scales, range(QUADRANTS))
@@ -213,7 +216,7 @@ def tile_list_lattice_flow_adjoint_kernel(
             minus_cos, sin = sines(f"sines{b}{first}{columns.start}", x, at)
             for t in range(first, first + count):
                 one = sin[:, t - first]
-                if t == 1 or (b == last and t > 0) or result is not None:
+                if t == 1 or (b == last and (t > 0 or columns.start > 0)):
                     nc.scalar.activation(one, one, ACT.Identity, scale=amp_column(b, t), bias=-1.0)
                 else:
                     nc.gpsimd.tensor_scalar(one, one, amp_column(b, t), -1.0, ALU.mult, ALU.add)
@@ -225,9 +228,10 @@ def tile_list_lattice_flow_adjoint_kernel(
         def side_by_side(values, run=PAIR):
             return values.rearrange("p (c i) t -> p c t i", i=run)
 
-        def make_z(b, half, at):
-            z_bf16[b, half] = place(f"z{b}{half}", [P, HALF, PACK], BF16, at)
-            for g in range(PACK):
+        def make_z(b, half, at, groups=range(PACK)):
+            key = (b, half, groups.start)
+            z_bf16[key] = place(f"z{b}{half}{groups.start}", [P, len(groups) * GROUP, PACK], BF16, at)
+            for g in groups:
                 group = slice(half * HALF + g * GROUP, half * HALF + (g + 1) * GROUP)
                 h_bank = psum.tile([P, PACK, GROUP], F32, name=f"bank{half * PACK + g}")
                 for t in range(PACK):
@@ -241,12 +245,12 @@ def tile_list_lattice_flow_adjoint_kernel(
                             start=(a == 0),
                             stop=(a == K_PASSES - 1),
                         )
-                if (b, half) == (last, 1):
-                    factors = last_factors[:, :, g * GROUP : (g + 1) * GROUP]
+                if b == last:
+                    factors = own_factors[half][:, :, g * GROUP : (g + 1) * GROUP]
                 else:
                     factors = work_view(b, slice(0, PACK), group)
                 nc.vector.tensor_tensor(
-                    side_by_side(z_bf16[b, half][:, g * GROUP : (g + 1) * GROUP, :]),
+                    side_by_side(z_bf16[key][:, (g - groups.start) * GROUP : (g - groups.start + 1) * GROUP, :]),
                     by_slice(factors),
                     by_slice(h_bank[:]),
                     ALU.mult,
@@ -256,11 +260,18 @@ def tile_list_lattice_flow_adjoint_kernel(
             w2_bf16[side, b] = place(f"w2_bf16_{side}{b}", [P, SIDE, PACK], BF16, LATE_AT + (side * 6 + b * 2) * KIB)
             nc.scalar.copy(side_by_side(w2_bf16[side, b][:], LINE), by_slice(loaded["w2", side, b][:], LINE))
 
-        def quantise(key, source, at, scales_at):
+        def quantise(key, sources, at, scales_at):
             name = "_".join(str(part) for part in key)
-            codes[key] = place("codes_" + name, [P, source.shape[1]], U32, at)
-            scales[key] = place("scales_" + name, [P, source.shape[1]], U8, scales_at)
-            nc.vector.quantize_mx(codes[key][:].bitcast(E4M3X4), scales[key][:], source[:].rearrange("p c t -> p (c t)"))
+            width = sum(source.shape[1] for source in sources)
+            codes[key] = place("codes_" + name, [P, width], U32, at)
+            scales[key] = place("scales_" + name, [P, width], U8, scales_at)
+            for number, source in enumerate(sources):
+                columns = slice(number * source.shape[1], (number + 1) * source.shape[1])
+                nc.vector.quantize_mx(
+                    codes[key][:, columns].bitcast(E4M3X4),
+                    scales[key][:, columns],
+                    source[:].rearrange("p c t -> p (c t)"),
+                )
 
         def second_product(half, side, first_bank):
             for n in range(2):
@@ -287,28 +298,27 @@ def tile_list_lattice_flow_adjoint_kernel(
                 windows[n][:].indirect(idx2[:, list_columns(half)]), y_sb[half, n][:], wgo_sb[:, entries(half)], ALU.mult
             )
 
-        w2_bf16 = {}
+        w2_bf16, own_factors = {}, {}
         for b, t in slices:
             gather_phases(b, t)
             if ("sT", b, t) == lent:
                 make_planes()
             else:
                 load_into_slot_of(("sT", b, t))
+            if (b, t) == (last, 0):
+                reorder_w1(1)
             if (b, t) == (last, 1):
-                load_w1(last, slot_of(("sT", b, t)))
                 gather_table()
+                load_w1(last, slot_of(("tab", 0)) + 4 * KIB)
+                reorder_w1(last)
                 for block in range(last):
-                    load_w2(0, block, slot_of(("tab", 0)) + block * 4 * KIB)
-                load_w2(0, last, slot_of(("tab", 1)))
-                wgo_sb = place("wgo_sb", [P, S], F32, slot_of(("tab", 1)) + 4 * KIB)
-                nc.sync.dma_start(wgo_sb[:], wgo)
+                    load_w2(0, block, slot_of(("tab", 1)) + block * 4 * KIB)
             if (b, t) == (last, 2):
+                load_w2(0, last, slot_of(("sT", b, t)))
                 for block in range(last):
-                    load_w2(1, block, slot_of(("sT", b, t)) + block * 4 * KIB)
+                    load_w2(1, block, SINES_AT + (4 + 4 * block) * KIB)
             if (b, t) == (0, PACK - 1):
                 reorder_w1(0)
-            if (b, t) == (1, 1):
-                reorder_w1(1)
             if (b, t) == (0, 0):
                 for half in range(HALVES):
                     factor(b, t, 1, entries(half), SINES_AT + 4 * half * KIB)
@@ -317,34 +327,38 @@ def tile_list_lattice_flow_adjoint_kernel(
             elif t % 2 == 1 and b < last:
                 factor(b, t - 1, 2, slice(0, S), SINES_AT + 16 * ((2 * b + t // 2) % 3) * KIB)
             elif t % 2 == 1:
-                factor(b, t - 1, 2, entries(0), SINES_AT + (16 + 4 * (t - 1)) * KIB)
-        reorder_w1(last)
-        last_factors = place("last_factors", [P, PACK, HALF], F32, slot_of(("sT", last, 1)))
+                if t == 1:
+                    own_factors[0] = place("own_factors0", [P, PACK, HALF], F32, slot_of(("tab", 0)) + 4 * KIB)
+                factor(b, t - 1, 2, entries(0), SINES_AT + (16 + 4 * (t - 1)) * KIB, own_factors[0][:, t - 1 : t + 1])
+        own_factors[1] = place("own_factors1", [P, PACK, HALF], F32, SINES_AT + 24 * KIB)
         for t in range(0, PACK, 2):
-            factor(last, t, 2, entries(1), SINES_AT + (32 + 4 * t) * KIB, last_factors[:, t : t + 2])
+            factor(last, t, 2, entries(1), SINES_AT + (32 + 4 * t) * KIB, own_factors[1][:, t : t + 2])
         for b in range(ROW_BLOCKS):
             round_w2(0, b)
         load_w2(1, last, SINES_AT + 12 * KIB)
+        wgo_sb = place("wgo_sb", [P, S], F32, SINES_AT + 16 * KIB)
+        nc.sync.dma_start(wgo_sb[:], wgo)
 
-        for half in range(HALVES):
-            make_z(0, half, slot_of(("sT", last, PACK - 1)) + half * 4 * KIB)
-        for half in range(HALVES):
-            make_z(1, half, Z_AT + half * 4 * KIB)
+        make_z(0, 0, slot_of(("sT", last, 2)) + 4 * KIB, range(0, 2))
+        make_z(0, 0, slot_of(("sT", last, PACK - 1)), range(2, PACK))
+        make_z(0, 1, slot_of(("sT", last, PACK - 1)) + 2 * KIB)
+        make_z(1, 0, slot_of(("sT", last, PACK - 1)) + 6 * KIB)
+        make_z(1, 1, Z_AT + 4 * KIB)
         make_z(last, 0, Z_AT + 8 * KIB)
         for b in range(ROW_BLOCKS):
-            quantise(("z", b, 0), z_bf16[b, 0], work_at(0, 0) + b * 2 * KIB, work_at(last, 0) + b * KIB)
-        make_z(last, 1, Z_AT)
+            quantise(("z", b, 0), [z_bf16[key] for key in z_bf16 if key[:2] == (b, 0)], work_at(0, 0) + b * 2 * KIB, slot_of(("w1", 1)) + b * KIB)
+        make_z(last, 1, slot_of(("sT", last, PACK - 1)) + 6 * KIB)
         for b in range(ROW_BLOCKS):
-            quantise(("w2", 0, b), w2_bf16[0, b], work_at(0, 0) + (6 + b) * KIB, slot_of(("sT", last, 1)) + b * KIB)
+            quantise(("w2", 0, b), [w2_bf16[0, b]], work_at(0, 0) + (6 + b) * KIB, SINES_AT + (24 + b) * KIB)
         second_product(0, 0, 0)
         for n in range(2):
-            copy_out(0, n, slot_of(("tab", 0)) + n * 2 * KIB)
+            copy_out(0, n, slot_of(("tab", 1)) + (4 + 2 * n) * KIB)
         for b in range(ROW_BLOCKS):
-            quantise(("z", b, 1), z_bf16[b, 1], work_at(1, 0) + b * 2 * KIB, LATE_AT + 4 * KIB + b * HALF)
+            quantise(("z", b, 1), [z_bf16[b, 1, 0]], work_at(1, 0) + b * 2 * KIB, LATE_AT + 4 * KIB + b * HALF)
         second_product(1, 0, 2)
         for b in range(ROW_BLOCKS):
             round_w2(1, b)
-            quantise(("w2", 1, b), w2_bf16[1, b], work_at(1, 0) + (6 + b) * KIB, slot_of(("sT", last, 1)) + (4 + b) * KIB)
+            quantise(("w2", 1, b), [w2_bf16[1, b]], work_at(1, 0) + (6 + b) * KIB, SINES_AT + (28 + b) * KIB)
         for n in range(2):
             copy_out(1, n, LATE_AT + (6 + 2 * n) * KIB)
         for half in range(HALVES):

@@ -130,10 +130,10 @@ def tile_list_lattice_flow_adjoint_kernel(
         w1_rows = place("w1_rows", [P, H], U8, ROWS_AT + T)
         v_planes = {1: place("v_plane1", [P, S], U8, ROWS_AT + T + H)}
         w1_planes = {1: place("w1_plane1", [P, H], U8, ROWS_AT + T + H + S)}
-        windows = {n: place(f"window{n}", [P, T2], F32, WINDOWS_AT + n * 8 * KIB) for n in range(OUT_TILES)}
+        windows = {n: place(f"window{n}", [P, T2], F32, WINDOWS_AT + n * 8 * KIB) for n in range(OUT_TILES - 1)}
         for rows in (w1_rows, tab_rows):
             nc.vector.memset(rows[:].bitcast(I32), 0)
-        for n in range(OUT_TILES):
+        for n in range(OUT_TILES - 1):
             nc.vector.memset(windows[n][:].bitcast(I32), 0)
 
         nc.sync.dma_start(idx[:], offs)
@@ -331,8 +331,11 @@ def tile_list_lattice_flow_adjoint_kernel(
                     own_factors[0] = place("own_factors0", [P, PACK, HALF], F32, slot_of(("tab", 0)) + 4 * KIB)
                 factor(b, t - 1, 2, entries(0), SINES_AT + (16 + 4 * (t - 1)) * KIB, own_factors[0][:, t - 1 : t + 1])
         own_factors[1] = place("own_factors1", [P, PACK, HALF], F32, SINES_AT + 24 * KIB)
-        for t in range(0, PACK, 2):
-            factor(last, t, 2, entries(1), SINES_AT + (32 + 4 * t) * KIB, own_factors[1][:, t : t + 2])
+        last_window_at = WINDOWS_AT + (OUT_TILES - 1) * 8 * KIB
+        factor(last, 0, 2, entries(1), SINES_AT + 32 * KIB, own_factors[1][:, 0:2])
+        factor(last, 2, 2, entries(1), last_window_at, own_factors[1][:, 2:4])
+        windows[OUT_TILES - 1] = place("last_window", [P, T2], F32, last_window_at)
+        nc.gpsimd.memset(windows[OUT_TILES - 1][:].bitcast(I32), 0)
         for b in range(ROW_BLOCKS):
             round_w2(0, b)
         load_w2(1, last, SINES_AT + 12 * KIB)

import math
from contextlib import ExitStack

import concourse.mybir as mybir

K, T, S, H, N, T2 = 1024, 2048, 1024, 1536, 512, 2048
FLOPS = 2 * K * H * S + 2 * H * N * S

F32 = mybir.dt.float32
BF16 = mybir.dt.bfloat16
I32 = mybir.dt.int32
U32 = mybir.dt.uint32
U16 = mybir.dt.uint16
U8 = mybir.dt.uint8
E4M3X4 = mybir.dt.float8_e4m3fn_x4
E5M2X4 = mybir.dt.float8_e5m2_x4
ACT = mybir.ActivationFunctionType
ALU = mybir.AluOpType

P = 128
PACK = 4
PASS = P * PACK
K_PASSES = K // PASS
ROW_BLOCKS = H // PASS
HALF = 512
HALVES = S // HALF
OUT_TILES = N // P
PER_COLUMN = 16
QUADRANTS = 4
SCALE_ROWS = 4
SHIFTED = 32 * (QUADRANTS - 1) + SCALE_ROWS
LINE = 4
GROUP = HALF // PACK
SIDE = N // 2
PAIR = 2
AMP_RUN = LINE * (PACK - 1) + 1
KIB = 1024
STREAM_SLOTS = 5
SLOT_ORDER = [0, 1, 3, 4, 2]

WINDOWS_AT = 0
LENT_AT = WINDOWS_AT + OUT_TILES * 8 * KIB
WORK_AT = LENT_AT + 8 * KIB
STREAM_AT = WORK_AT + ROW_BLOCKS * 16 * KIB
SINES_AT = STREAM_AT + STREAM_SLOTS * 8 * KIB
LATE_AT = SINES_AT + 6 * 8 * KIB
Z_AT = LATE_AT + 12 * KIB
V_CODES_AT = Z_AT + 16 * KIB
W1_CODES_AT = V_CODES_AT + K_PASSES * 4 * KIB
ROWS_AT = W1_CODES_AT + K_PASSES * 6 * KIB


def tile_list_lattice_flow_adjoint_kernel(
    tc, tab_words, tab_scales, offs, offs2, sT, w1_words, w1_scales, amp, w2, wgo, out
):
    nc = tc.nc
    with ExitStack() as ctx:
        keep = ctx.enter_context(tc.tile_pool(name="keep", bufs=1))
        sbuf = ctx.enter_context(tc.tile_pool(name="sbuf", bufs=1))
        psum = ctx.enter_context(tc.psum_pool(name="psum", bufs=1))

        def place(name, shape, dtype, at):
            return sbuf.tile(shape, dtype, name=name, offset=at, align_bytes=64)

        def entries(half):
            return slice(half * HALF, (half + 1) * HALF)

        def list_columns(half):
            return slice(half * HALF // PER_COLUMN, (half + 1) * HALF // PER_COLUMN)

        def slot_at(slot):
            return STREAM_AT + SLOT_ORDER.index(slot) * 8 * KIB

        idx = keep.tile([P, S // PER_COLUMN], U16, name="idx")
        idx2 = keep.tile([P, S // PER_COLUMN], U16, name="idx2")
        amp_sb = keep.tile([P, ROW_BLOCKS, PACK * LINE], F32, name="amp_sb")
        last = ROW_BLOCKS - 1

        sT_slices = sT.rearrange("(b m t i) c -> b t m i c", b=ROW_BLOCKS, t=PACK, i=LINE)
        w2_blocks = w2.rearrange("(b m t i) n -> b t m i n", b=ROW_BLOCKS, t=PACK, i=LINE)
        slices = [(b, t) for b in range(ROW_BLOCKS) for t in range(PACK)]
        lent = ("sT", 1, 1)
        ring = [("sT",) + s for s in slices if ("sT",) + s != lent]
        for a in range(K_PASSES):
            ring.insert(ring.index(("sT", last, 2)), ("tab", a))
        ring.insert(ring.index(("sT", last, PACK - 1)), ("w1", 1))
        loaded = {}

        w1_blocks = w1_words.rearrange("a p (b c) i -> b p a (c i)", b=ROW_BLOCKS)

        def slot_of(key):
            return LENT_AT if key == lent else slot_at(ring.index(key) % STREAM_SLOTS)

        def load(key):
            name = "load_" + "_".join(str(part) for part in key)
            if key[0] == "w1":
                load_w1(key[1], slot_of(key) + 2 * KIB)
            elif key[0] == "tab":
                loaded[key] = place(name, [P, T], I32, slot_of(key))
                nc.sync.dma_start(loaded[key][:], tab_words[key[1]].rearrange("p c i -> p (c i)").bitcast(I32))
            else:
                loaded[key] = place(name, [P, T], F32, slot_of(key))
                nc.sync.dma_start(loaded[key][:], sT_slices[key[1], key[2]])

        def load_into_slot_of(key):
            following = ring.index(key) + STREAM_SLOTS
            if following < len(ring):
                load(ring[following])

        def load_w1(b, at):
            loaded["w1", b] = place(f"load_w1_{b}", [P, K_PASSES, PASS], I32, at)
            nc.sync.dma_start(loaded["w1", b][:], w1_blocks[b].bitcast(I32))

        def load_w2(side, b, at):
            loaded["w2", side, b] = place(f"load_w2_{side}{b}", [P, PACK, SIDE], F32, at)
            for t in range(PACK):
                nc.sync.dma_start(loaded["w2", side, b][:, t, :], w2_blocks[b, t, :, :, side * SIDE : (side + 1) * SIDE])

        def load_scale_rows(tile, scales, quadrants):
            for q in quadrants:
                nc.sync.dma_start(
                    tile[32 * q : 32 * q + K_PASSES * SCALE_ROWS, :].bitcast(I32),
                    scales[:, SCALE_ROWS * q : SCALE_ROWS * (q + 1), :].bitcast(I32),
                )

        def shift_second_pass(plane, both):
            nc.sync.dma_start(plane[0:SHIFTED, :].bitcast(I32), both[SCALE_ROWS : SCALE_ROWS + SHIFTED, :].bitcast(I32))

        tab_rows = place("tab_rows", [P, T], U8, ROWS_AT)
        w1_rows = place("w1_rows", [P, H], U8, ROWS_AT + T)
        v_planes = {1: place("v_plane1", [P, S], U8, ROWS_AT + T + H)}
        w1_planes = {1: place("w1_plane1", [P, H], U8, ROWS_AT + T + H + S)}
        windows = {n: place(f"window{n}", [P, T2], F32, WINDOWS_AT + n * 8 * KIB) for n in range(OUT_TILES - 1)}
        for rows in (w1_rows, tab_rows):
            nc.vector.memset(rows[:].bitcast(I32), 0)
        for n in range(OUT_TILES - 1):
            nc.vector.memset(windows[n][:].bitcast(I32), 0)

        nc.sync.dma_start(idx[:], offs)
        load(("sT", 0, 0))
        amp_runs = amp.rearrange("(b m e) -> m b e", b=ROW_BLOCKS, e=PACK * LINE)
        for i in range(LINE):
            nc.sync.dma_start(amp_sb[i:P:LINE, :, 0:AMP_RUN], amp_runs[:, :, i : i + AMP_RUN])
        for s in slices[1:6]:
            load(("sT",) + s)
        load_w1(0, Z_AT)
        nc.sync.dma_start(idx2[:], offs2)
        load_scale_rows(w1_rows, w1_scales, range(QUADRANTS))
        load_scale_rows(tab_rows, tab_scales, range(QUADRANTS))

        v_codes = [place(f"v_codes{a}", [P, S], U32, V_CODES_AT + a * 4 * KIB) for a in range(K_PASSES)]

        def work_at(b, half):
            return WORK_AT + (b * 16 + half * 8) * KIB

        work = {b: place(f"work{b}", [P, PACK, S], F32, work_at(b, 0)) for b in range(last)}
        for half in range(HALVES):
            work[last, half] = place(f"work{last}{half}", [P, PACK, HALF], F32, work_at(last, half))

        def work_view(b, rows, columns):
            if b < last:
                return work[b][:, rows, columns]
            half = columns.start // HALF
            return work[b, half][:, rows, columns.start - half * HALF : columns.stop - half * HALF]

        z_bf16, codes, scales, y_banks, y_sb = {}, {}, {}, {}, {}

        def gather_phases(b, t):
            window = loaded["sT", b, t]
            if b < last and (b, t) != (0, 0):
                nc.vector.tensor_copy(work[b][:, t, :], window[:].indirect(idx[:]))
            else:
                for half in range(HALVES):
                    nc.vector.tensor_copy(
                        work_view(b, t, entries(half)), window[:].indirect(idx[:, list_columns(half)])
                    )

        w1_codes = {}

        def reorder_w1(b):
            w1_codes[b] = place(f"w1_codes{b}", [P, K_PASSES, PASS], U32, W1_CODES_AT + b * 4 * KIB)
            nc.gpsimd.tensor_copy(
                w1_codes[b][:].rearrange("p a (t m i) -> p a t m i", t=PACK, i=LINE),
                loaded["w1", b][:].bitcast(U32).rearrange("p a (m t i) -> p a t m i", t=PACK, i=LINE),
            )

        def make_planes():
            v_planes[0] = place("v_plane0", [P, S], U8, LENT_AT)
            w1_planes[0] = place("w1_plane0", [P, H], U8, LENT_AT + S)
            nc.vector.tensor_copy(
                w1_planes[0][:].bitcast(I32).rearrange("p (b t m i) -> p b m t i", t=PACK, b=ROW_BLOCKS, i=LINE),
                w1_rows[:].bitcast(I32).rearrange("p (b m i t) -> p b m t i", t=PACK, b=ROW_BLOCKS, i=LINE),
            )
            shift_second_pass(w1_planes[1], w1_planes[0])
            nc.vector.tensor_copy(v_planes[0][:], tab_rows[:].indirect(idx[:]))
            shift_second_pass(v_planes[1], v_planes[0])

        def gather_table():
            for a in range(K_PASSES):
                nc.vector.tensor_copy(v_codes[a][:], loaded["tab", a][:].bitcast(U32).indirect(idx[:]))

        def sines(name, x, at):
            both = place(name, [P, 2] + list(x.shape[1:]), F32, at)
            minus_cos, sin = both[:, 0], both[:, 1]
            steps = [(minus_cos, ACT.Abs), (sin, ACT.Sin)]
            for target, function in reversed(steps) if name == "sines000" else steps:
                nc.scalar.activation(target, x, function)
            nc.scalar.activation(minus_cos, minus_cos, ACT.Sin, bias=-math.pi / 2)
            return minus_cos, sin

        def amp_column(b, t):
            return amp_sb[:, b, LINE * t : LINE * t + 1]

        def factor(b, first, count, columns, at, result=None):
            x = work_view(b, slice(first, first + count), columns)
            minus_cos, sin = sines(f"sines{b}{first}{columns.start}", x, at)
            for t in range(first, first + count):
                one = sin[:, t - first]
                if t == 1 or (b == last and (t > 0 or columns.start > 0)):
                    nc.scalar.activation(one, one, ACT.Identity, scale=amp_column(b, t), bias=-1.0)
                else:
                    nc.gpsimd.tensor_scalar(one, one, amp_column(b, t), -1.0, ALU.mult, ALU.add)
            nc.gpsimd.tensor_tensor(x if result is None else result, sin, minus_cos, ALU.mult)

        def by_slice(values, run=PAIR):
            return values.rearrange("p t (c i) -> p c t i", i=run)

        def side_by_side(values, run=PAIR):
            return values.rearrange("p (c i) t -> p c t i", i=run)

        def make_z(b, half, at, groups=range(PACK)):
            key = (b, half, groups.start)
            z_bf16[key] = place(f"z{b}{half}{groups.start}", [P, len(groups) * GROUP, PACK], BF16, at)
            for g in groups:
                group = slice(half * HALF + g * GROUP, half * HALF + (g + 1) * GROUP)
                h_bank = psum.tile([P, PACK, GROUP], F32, name=f"bank{half * PACK + g}")
                for t in range(PACK):
                    for a in range(K_PASSES):
                        nc.tensor.matmul_mx(
                            h_bank[:, t, :],
                            lhsT=w1_codes[b][:, a, t * P : (t + 1) * P].bitcast(E4M3X4),
                            lhsT_scale=w1_planes[a][:, b * PASS + t * P : b * PASS + (t + 1) * P],
                            rhs=v_codes[a][:, group].bitcast(E5M2X4),
                            rhs_scale=v_planes[a][:, group],
                            start=(a == 0),
                            stop=(a == K_PASSES - 1),
                        )
                if b == last:
                    factors = own_factors[half][:, :, g * GROUP : (g + 1) * GROUP]
                else:
                    factors = work_view(b, slice(0, PACK), group)
                nc.vector.tensor_tensor(
                    side_by_side(z_bf16[key][:, (g - groups.start) * GROUP : (g - groups.start + 1) * GROUP, :]),
                    by_slice(factors),
                    by_slice(h_bank[:]),
                    ALU.mult,
                )

        def round_w2(side, b):
            w2_bf16[side, b] = place(f"w2_bf16_{side}{b}", [P, SIDE, PACK], BF16, LATE_AT + (side * 6 + b * 2) * KIB)
            nc.scalar.copy(side_by_side(w2_bf16[side, b][:], LINE), by_slice(loaded["w2", side, b][:], LINE))

        def quantise(key, sources, at, scales_at):
            name = "_".join(str(part) for part in key)
            width = sum(source.shape[1] for source in sources)
            codes[key] = place("codes_" + name, [P, width], U32, at)
            scales[key] = place("scales_" + name, [P, width], U8, scales_at)
            for number, source in enumerate(sources):
                columns = slice(number * source.shape[1], (number + 1) * source.shape[1])
                nc.vector.quantize_mx(
                    codes[key][:, columns].bitcast(E4M3X4),
                    scales[key][:, columns],
                    source[:].rearrange("p c t -> p (c t)"),
                )

        def second_product(half, side, first_bank):
            for n in range(2):
                y_banks[half, 2 * side + n] = psum.tile([P, HALF], F32, name=f"bank{first_bank + n}")
            for b in range(ROW_BLOCKS):
                for n in range(2):
                    columns = slice(n * P, (n + 1) * P)
                    nc.tensor.matmul_mx(
                        y_banks[half, 2 * side + n][:],
                        lhsT=codes["w2", side, b][:, columns].bitcast(E4M3X4),
                        lhsT_scale=scales["w2", side, b][:, columns],
                        rhs=codes["z", b, half][:].bitcast(E4M3X4),
                        rhs_scale=scales["z", b, half][:],
                        start=(b == 0),
                        stop=(b == last),
                    )

        def copy_out(half, n, at):
            y_sb[half, n] = place(f"y{half}{n}", [P, HALF], F32, at)
            nc.scalar.copy(y_sb[half, n][:], y_banks[half, n][:])

        def scatter(half, n):
            nc.vector.tensor_tensor(
                windows[n][:].indirect(idx2[:, list_columns(half)]), y_sb[half, n][:], wgo_sb[:, entries(half)], ALU.mult
            )

        w2_bf16, own_factors = {}, {}
        for b, t in slices:
            gather_phases(b, t)
            if ("sT", b, t) == lent:
                make_planes()
            else:
                load_into_slot_of(("sT", b, t))
            if (b, t) == (last, 0):
                reorder_w1(1)
            if (b, t) == (last, 1):
                gather_table()
                load_w1(last, slot_of(("tab", 0)) + 4 * KIB)
                reorder_w1(last)
                for block in range(last):
                    load_w2(0, block, slot_of(("tab", 1)) + block * 4 * KIB)
            if (b, t) == (last, 2):
                load_w2(0, last, slot_of(("sT", b, t)))
                for block in range(last):
                    load_w2(1, block, SINES_AT + (4 + 4 * block) * KIB)
            if (b, t) == (0, PACK - 1):
                reorder_w1(0)
            if (b, t) == (0, 0):
                for half in range(HALVES):
                    factor(b, t, 1, entries(half), SINES_AT + 4 * half * KIB)
            elif b == 0:
                factor(b, t, 1, slice(0, S), SINES_AT + 8 * t * KIB)
            elif t % 2 == 1 and b < last:
                factor(b, t - 1, 2, slice(0, S), SINES_AT + 16 * ((2 * b + t // 2) % 3) * KIB)
            elif t % 2 == 1:
                if t == 1:
                    own_factors[0] = place("own_factors0", [P, PACK, HALF], F32, slot_of(("tab", 0)) + 4 * KIB)
                factor(b, t - 1, 2, entries(0), SINES_AT + (16 + 4 * (t - 1)) * KIB, own_factors[0][:, t - 1 : t + 1])
        own_factors[1] = place("own_factors1", [P, PACK, HALF], F32, SINES_AT + 24 * KIB)
        last_window_at = WINDOWS_AT + (OUT_TILES - 1) * 8 * KIB
        factor(last, 0, 2, entries(1), SINES_AT + 32 * KIB, own_factors[1][:, 0:2])
        factor(last, 2, 2, entries(1), last_window_at, own_factors[1][:, 2:4])
        windows[OUT_TILES - 1] = place("last_window", [P, T2], F32, last_window_at)
        nc.gpsimd.memset(windows[OUT_TILES - 1][:].bitcast(I32), 0)
        for b in range(ROW_BLOCKS):
            round_w2(0, b)
        load_w2(1, last, SINES_AT + 12 * KIB)
        wgo_sb = place("wgo_sb", [P, S], F32, SINES_AT + 16 * KIB)
        nc.sync.dma_start(wgo_sb[:], wgo)

        make_z(0, 0, slot_of(("sT", last, 2)) + 4 * KIB, range(0, 2))
        make_z(0, 0, slot_of(("sT", last, PACK - 1)), range(2, PACK))
        make_z(0, 1, slot_of(("sT", last, PACK - 1)) + 2 * KIB)
        make_z(1, 0, slot_of(("sT", last, PACK - 1)) + 6 * KIB)
        make_z(1, 1, Z_AT + 4 * KIB)
        make_z(last, 0, Z_AT + 8 * KIB)
        for b in range(ROW_BLOCKS):
            quantise(("z", b, 0), [z_bf16[key] for key in z_bf16 if key[:2] == (b, 0)], work_at(0, 0) + b * 2 * KIB, slot_of(("w1", 1)) + b * KIB)
        make_z(last, 1, slot_of(("sT", last, PACK - 1)) + 6 * KIB)
        for b in range(ROW_BLOCKS):
            quantise(("w2", 0, b), [w2_bf16[0, b]], work_at(0, 0) + (6 + b) * KIB, SINES_AT + (24 + b) * KIB)
        second_product(0, 0, 0)
        for n in range(2):
            copy_out(0, n, slot_of(("tab", 1)) + (4 + 2 * n) * KIB)
        for b in range(ROW_BLOCKS):
            quantise(("z", b, 1), [z_bf16[b, 1, 0]], work_at(1, 0) + b * 2 * KIB, LATE_AT + 4 * KIB + b * HALF)
        second_product(1, 0, 2)
        for b in range(ROW_BLOCKS):
            round_w2(1, b)
            quantise(("w2", 1, b), [w2_bf16[1, b]], work_at(1, 0) + (6 + b) * KIB, SINES_AT + (28 + b) * KIB)
        for n in range(2):
            copy_out(1, n, LATE_AT + (6 + 2 * n) * KIB)
        for half in range(HALVES):
            second_product(half, 1, 4 + 2 * half)
            for n in range(2, OUT_TILES):
                copy_out(half, n, SINES_AT + (2 * half + n) * 2 * KIB)
        for side in range(2):
            for half in range(HALVES):
                for n in range(2 * side, 2 * side + 2):
                    scatter(half, n)
                    if half == HALVES - 1:
                        nc.sync.dma_start(out[n * P : (n + 1) * P, :], windows[n][:])
